import numpy as np, ml_dtypes
CORES = [242,247,114,119]
N = 4
BF = ml_dtypes.bfloat16
def gentries(a):
    return np.ascontiguousarray(a.reshape(8, 16, -1).transpose(0, 2, 1)).reshape(8, -1)
def gtable(e):
    e = np.asarray(e); return np.ascontiguousarray(e.reshape(8, -1, 16).transpose(0, 2, 1)).reshape(128, -1).astype(np.int32)
def f(rng, *shape):
    return (rng.standard_normal(shape, dtype=np.float32) * np.exp2(rng.integers(-2, 3, shape[:-1] + (1,)))).astype(BF)
def wide(rng, *shape):
    v = f(rng, *shape).astype(np.float32); k = shape[:-2] + (1, shape[-1])
    return (v * np.exp2(rng.integers(-6, 7, k)) * (rng.random(k) > 0.0625)).astype(BF)
V, W, G, P, Q, RO = 1024, 2048, 256, 256, 128, 4
M = V + (N - 1) * G + 1
def nodes(an, of):
    A = np.full((N, 8, M), M - 1, np.int64); A[..., :V] = an
    O = np.zeros((N, 8, M), np.int64); O[..., :M - 1] = of
    return A, O
def dates(A, O):
    s, p = O, A
    for i in range(3):
        s = s + np.take_along_axis(s, p, 2); p = np.take_along_axis(p, p, 2)
    return s & (W - 1)
def parts(rng):
    u = rng.random((N, 8, V))
    an = np.where(u < 0.25, M - 1, np.where(u < 0.4, rng.integers(V, M - 1, (N, 8, V)), rng.integers(0, V, (N, 8, V))))
    return an, rng.integers(0, W, (N, 8, M - 1)), rng.integers(0, 256, (N, 8, 16, W)), rng.integers(0, V, (N, 8, (N - 1) * G))
def statures(rng):
    sc = np.exp2(rng.integers(-2, 3, (1, 8, 16, 1)).astype(np.float64)); sh = rng.choice(np.array([-0.8, -0.5, -0.2, 0.1]), (N, 8, 1, 1))
    x = rng.standard_normal((N, 8, 16, V)) + 0.7 * rng.standard_normal((N, 8, 1, V)) + sh
    s = rng.standard_normal((N, 8, 16, W)) + 0.7 * rng.standard_normal((N, 8, 1, W))
    return np.floor(8 * x) * 0.125 * sc, np.floor(8 * s) * 0.125 * sc
def pack(x, an, of, s, wk, snd):
    b = lambda v: np.ascontiguousarray(v).reshape(N, 128, -1).astype(np.float32).astype(BF)
    return {"x": b(x), "an0": np.stack([gtable(e) for e in an]), "of0": np.stack([gtable(e) for e in of]), "s0": b(s), "wk": b(wk), "snd": np.stack([gtable(e) for e in snd])}
def setup_inputs(rng):
    an, of, wk, snd = parts(rng); x, s = statures(rng)
    return pack(x, an, of, s, wk, snd)
def setup_inputs_room(rng):
    an, of, wk, snd = parts(rng); day = np.arange(W)
    an[..., 0] = M - 1; an[..., V - 1] = M - 1; of[..., 0] = 0; of[..., V - 1] = W - 2
    D = dates(*nodes(an, of))[..., :V]
    s = rng.integers(36, 61, (N, 8, 16, W)) * 0.25
    s[..., day % 4 == 3] = rng.integers(4, 29, (N, 8, 16, W // 4)) * 0.25
    o = s[1::2]; o[..., day % 4 == 1] = rng.integers(-32, -3, (o.shape[0], 8, 16, W // 4)) * 0.25
    k = rng.permutation(16)
    wk[:, :, k[0]] = 4 * rng.integers(0, 64, (N, 8, W)) + (day + 1) % 4
    wk[1::2, :, k[1]] = 4 * rng.integers(0, 64, (o.shape[0], 8, W)) + (day + 3) % 4
    x = 16 + rng.integers(0, 33, (N, 8, 16, V)) * 0.25
    for q in range(N):
        for g in range(8):
            n = int(rng.choice(np.array([0, 1, 2, P - 1, P, P + 1, P + Q]))); nf = int(rng.choice(np.array([0, 1, Q - 1, Q, Q + 1, P])))
            if q == 0: n = (P, P + 1, P - 1, 1, 0, P, P, P)[g]; nf = (Q, Q + 1, Q - 1, 1, 0, 0, P, Q + 1)[g]
            e = np.flatnonzero(D[q, g] % 2 == 0); e = e[(e > 0) & (e < V - 1)]
            w = np.concatenate([np.array([0, V - 1]), rng.permutation(e)])[:n]
            x[q, g][:, w] = rng.integers(29, 36, (16, len(w))) * 0.25
            i = w[len(w) - min(nf, len(w)):]
            x[q, g][:, i] = rng.integers(0, 4, (16, len(i))) * 0.25
    return pack(x, an, of, s, wk, snd)
def setup_inputs_ties(rng):
    an, of, wk, snd = parts(rng)
    of = rng.choice(np.array([0, 1, W - 1, W // 2, 14]), (N, 8, M - 1)); wk[:, ::2] = rng.choice(np.array([0, 1, 2, 255]), (N, 4, 16, W))
    x = np.floor(4 * rng.random((N, 8, 16, V)) * (0.3 + 0.7 * rng.random((N, 8, 1, V))))
    s = np.floor(4 * rng.random((N, 8, 16, W)) * (0.3 + 0.7 * rng.random((N, 8, 1, W)))) + 2 * (rng.random((N, 8, 1, W)) < 0.4)
    x[..., 0] = -1; x[..., V - 1] = -1
    x = np.where((x == 0) & (rng.random(x.shape) < 0.5), -0.0, x); s = np.where((s == 0) & (rng.random(s.shape) < 0.5), -0.0, s)
    return pack(x, an, of, s, wk, snd)
def setup_inputs_chains(rng):
    an, of, wk, snd = parts(rng); x, s = statures(rng); v = np.arange(V); d = int(rng.integers(0, W))
    for q in range(N):
        for g in range(8):
            k = (g + q) % 8
            if k == 0: an[q, g] = (v + 1) % V
            if k == 1: an[q, g] = v
            if k == 2: an[q, g] = rng.integers(V, M - 1, V)
            if k == 3: an[q, g] = M - 1
            if k == 4: an[q, g] = rng.choice(np.array([0, 5, V - 1]), V)
            if k == 5: an[q, g] = np.where(v == 0, M - 1, v - 1)
            if k > 5:
                an[q, g] = M - 1; of[q, g, :V] = d
                w = 1 + rng.permutation(255)[:16]; wk[q, g, :, d] = w; c = (d + 7 * w) & (W - 1)
                i = np.sort(rng.permutation(16)[:2])
                s[q, g] = 16 + 0.25 * rng.integers(0, 32, (16, W))
                s[q, g][:, c[i[0]]] = 0.25 * rng.integers(0, 16, 16)
                m = np.arange(P) if k == 6 else np.arange(int(rng.integers(0, 16)), V, 16)
                y = 28 + 0.25 * rng.integers(0, 16, (16, V))
                y[:, m] = 8 + 0.25 * rng.integers(0, 16, (16, len(m)))
                if k == 6: y[:, rng.permutation(P)[:56]] = -8 + 0.25 * rng.integers(0, 16, (16, 56))
                if k == 7: s[q, g][:, c[i[1]]] = -16 + 0.25 * rng.integers(0, 16, 16)
                x[q, g] = y
    snd[:, ::2] = rng.choice(np.array([0, 3, V // 2, V - 1]), (N, 4, (N - 1) * G))
    return pack(x, an, of, s, wk, snd)
def setup_inputs_calm(rng):
    an, of, wk, snd = parts(rng); x, s = statures(rng); q = int(rng.integers(0, N)); g = int(rng.integers(0, 8))
    x[:, g] += 64
    x[(q + 2) % N] += 64; x[q] = np.minimum(x[q], 20) - 64
    o = s[(q + 1) % N]; o[..., 1::2] -= 128
    w = rng.permutation(256)[:16]; wk[:, g, :, 0] = w; day = (7 * w) & (W - 1)
    for r in range(N):
        if r != q: s[r, g][:, day] = -2.0 ** 20
    x[q, :, :, 0] = -2.0 ** 20
    return pack(x, an, of, s, wk, snd)
def setup_inputs_spread(rng):
    an, of, wk, snd = parts(rng)
    of = np.minimum(np.exp2(13 * rng.random((N, 8, M - 1))).astype(np.int64) - 1, W - 1)
    x = np.abs(wide(rng, N, 8, 16, V).astype(np.float32)); s = np.abs(wide(rng, N, 8, 16, W).astype(np.float32))
    k = rng.permutation(8); sc = np.ones((1, 8, 1, 1), np.float32); sc[:, k[0]] = 2.0 ** -40; sc[:, k[1]] = 512
    x = np.minimum(x * sc, np.float32(2.0 ** 20)); s = np.minimum(s * sc, np.float32(2.0 ** 20))
    x[:, k[1], :, V - 1] = 2.0 ** 20; s[:, k[1], :, W - 1] = 2.0 ** 20
    return pack(x, an, of, s, wk, snd)
def check_inputs(d):
    bad = []
    for k, lo, hi in (("x", -2 ** 20, 2 ** 20), ("s0", -2 ** 20, 2 ** 20), ("wk", 0, 255), ("an0", 0, M - 1), ("of0", 0, W - 1), ("snd", 0, V - 1)):
        v = np.asarray(d[k]).astype(np.float64)
        if not (np.min(v) >= lo and np.max(v) <= hi): bad.append("range of " + k)
        elif k == "wk" and np.any(v != np.floor(v)): bad.append("whole numbers of wk")
        elif k in ("x", "s0") and np.any((v != 0) & (np.abs(v) < 2.0 ** -100)): bad.append("tiny numbers of " + k)
    return bad
def best(S, K, x, D):
    c = (D + 7 * K[:, D]) & (W - 1)
    e = np.sum((x[:, None, :] > S[:, c]).astype(np.int64), axis=0)
    k = np.argmax(e, axis=0); i = np.arange(len(D))
    return c[k, i], e[k, i]
def put(S, c, x):
    u, i = np.unique(c, return_index=True)
    S[:, u] = x[:, i]
def reference(x, an0, of0, s0, wk, snd):
    X = x.astype(np.float32).reshape(N, 8, 16, V); S = s0.astype(np.float32).reshape(N, 8, 16, W).copy(); K = wk.astype(np.float32).astype(np.int64).reshape(N, 8, 16, W)
    A, O = nodes(np.stack([gentries(e) for e in an0]).astype(np.int64), np.stack([gentries(e) for e in of0]).astype(np.int64))
    sl = np.stack([gentries(e) for e in snd]).astype(np.int64).reshape(N, 8, N - 1, G)
    odd = np.zeros(N, np.int64)
    for t in range(RO):
        D = dates(A, O)[..., :V]
        a = np.sum((X >= np.take_along_axis(S, D[:, :, None, :], 3)).astype(np.int64), axis=2)
        moves = np.zeros(N, np.int64); go = {}
        for q in range(N):
            for g in range(8):
                v = np.flatnonzero(a[q, g] < 5)[:P]
                c, e = best(S[q, g], K[q, g], X[q, g][:, v], D[q, g, v])
                ok = e >= 9 + odd[q]; w = v[ok]
                A[q, g, w] = M - 1; O[q, g, w] = c[ok]
                put(S[q, g], c[ok], X[q, g][:, w])
                moves[q] += len(w)
                r = v[~ok][:Q]; go[q, g] = (X[q, g][:, r], D[q, g, r])
        for q in range(N):
            for g in range(8):
                y, b = go[(q - 1 - t % (N - 1)) % N, g]
                c, e = best(S[q, g], K[q, g], y, b)
                ok = e >= 9 + odd[q]
                put(S[q, g], c[ok], y[:, ok])
        odd = moves & 1
        for q in range(N):
            for d in range(1, N):
                p = (q - d) % N
                O[q, :, V + (d - 1) * G:V + d * G] = np.take_along_axis(D[p], sl[p, :, d - 1], 1)
    return {"ys": S.reshape(N, 128, W).astype(BF), "yan": A[..., :V].astype(np.float32), "yof": O[..., :V].astype(np.float32)}

@@ -1,0 +1,487 @@
+from concourse.mybir import AluOpType as A, ActivationFunctionType as AF, AxisListType as AX
+
+FLAG = 262144.0
+BIG = 65536.0
+LOW = -1073741824.0
+RO = 4
+F, B, H, I, U = "float32", "bfloat16", "float16", "int32", "uint16"
+SB = {
+    "anI": (64, I), "ofI": (112, I), "snI": (48, I), "wkb": (2048, B), "xw": (1040, B), "sd": (2320, B),
+    "pI": (3, I), "pp": (3, F), "tc": (8, F), "lmc": (16, F), "n512": (512, I), "kI": (256, I), "m4": (128, I),
+    "id16": (128, H), "idb": (128, B), "idF": (128, F), "jF": (128, F), "j16": (128, H), "upr": (128, B),
+    "one": (128, B), "seven": (128, B), "m1k": (128, B), "gb16": (128, H), "gi16": (8, H), "gib": (8, B), "gik": (8, B), "pm0": (256, F), "pm1": (256, F), "pmg": (128, F),
+    "mk": (256, H), "mkg": (256, H), "lane": (256, B), "ct8": (128, B), "selb": (2048, B), "selF": (2048, F),
+    "ex": (16, U), "exg": (16, U), "ex8": (8, U), "dgt": (6, U), "v1c": (16, F), "smI": (1024, F), "smk": (1024, B), "du": (32, F), "lo16": (512, H),
+    "an1": (64, F), "of16": (112, H), "ofE": (1792, H), "pw": (1800, F), "p2w": (1800, F), "rf16": (1024, H), "w1": (2064, F), "w2": (1800, F), "w3": (1800, F), "t8": (1032, F),
+    "fl": (1024, B), "wd": (1024, F), "p1h": (64, H), "p2h": (64, H), "p3h": (64, H), "l1": (64, U), "l2": (64, U), "l3": (64, U), "sl": (48, U), "cw": (2056, F), "cq": (256, F), "sg": (2048, B),
+    "ldI": (64, I), "lfd": (64, U), "cv": (1032, F), "cmp": (4096, B), "xr": (4096, B), "bz": (120, B), "rz": (24, B), "rkI": (64, I), "loI": (64, I), "hiI": (16, I),
+    "oa": (1024, H), "ob": (128, H), "th": (1088, B), "win": (144, F), "wg": (128, F), "g1": (16, F), "lv": (16, U), "lvf": (16, F), "nb": (8, F), "vld": (16, F),
+    "xg": (272, B), "cg": (256, U), "cgf": (256, F), "dbf": (256, F), "dbi": (264, I), "kb": (128, F), "ka": (128, F), "ks": (112, F), "sm": (128, F), "smi": (64, I), "u16s": (64, U),
+    "rdb": (2, B), "thr": (4, F), "xe": (256, H), "xf": (256, F), "rr": (256, H), "wv": (256, F), "eq": (2048, B), "scn": (2048, B), "gl": (16, U), "dgh": (128, H), "yb": (384, F),
+    "ghs": (2304, F), "ghl": (2304, F), "gxs": (512, B), "gxl": (512, B), "gds": (64, U), "gdl": (64, U),
+}
+SCRATCH = {k: ("sbuf", [128, n], d) for k, (n, d) in SB.items()}
+SCRATCH.update({"ck": ("sbuf", [1, 256], B), "ckg": ("sbuf", [1, 128], B)})
+PS = ("pA", "pB", "pC", "pD", "pE", "pF", "pG", "pH")
+SCRATCH.update({k: ("psum", [128, 512], F) for k in PS})
+SEMAPHORES = ["qV", "qS", "qP", "qG", "ls"] + ["d%d" % i for i in range(11)] + ["gh%d" % t for t in range(3)] + ["gx%d" % t for t in range(RO)] + ["gd%d" % t for t in range(RO)]
+
+
+def layer(g, T):
+    eng = {"V": g.vector, "S": g.scalar, "P": g.tensor, "G": g, "Y": g.sync}
+    cnt = {"V": 0, "S": 0, "P": 0, "G": 0}
+    seen = {q: {} for q in eng}
+    hist = {}
+    dma = [0]
+
+    def reg(r):
+        return (r, 0, 1 << 20) if isinstance(r, str) else r
+
+    def prepare(q, reads, writes):
+        best = {}
+        for rs, w in ((reads, False), (writes, True)):
+            for r in rs:
+                name, lo, hi = reg(r)
+                for e in hist.get(name, ()):
+                    other = e[3] != q
+                    bank = name in PS and other
+                    if not (lo < e[1] and e[0] < hi) and not bank:
+                        continue
+                    if not (w or e[2] or bank) or (q == "P" and not other and name in PS):
+                        continue
+                    if seen[q].get(e[4], 0) < e[5] and (e[4] not in best or best[e[4]][5] < e[5]):
+                        best[e[4]] = e
+        for s in best:
+            e = best[s]
+            if not any(o != s and best[o][6].get(s, 0) >= e[5] for o in best):
+                eng[q].wait_ge(T.sem[s], e[5])
+        for e in best.values():
+            for s, n in list(e[6].items()) + [(e[4], e[5])]:
+                if seen[q].get(s, 0) < n:
+                    seen[q][s] = n
+
+    def record(q, sem, count, reads, writes):
+        clock = dict(seen[q[0]])
+        for rs, w in ((reads, False), (writes, True)):
+            for r in rs:
+                name, lo, hi = reg(r)
+                h = hist.setdefault(name, [])
+                h[:] = [e for e in h if not (lo <= e[0] and e[1] <= hi and (w or (e[3] == q and not e[2])))]
+                h.append((lo, hi, w, q, sem, count, clock))
+
+    def op(q, fns, reads, writes):
+        prepare(q, reads, writes)
+        for f in fns if isinstance(fns, list) else [fns]:
+            f().then_inc(T.sem["q" + q], 1)
+            cnt[q] += 1
+        record(q, "q" + q, cnt[q], reads, writes)
+
+    def copy(q, out, in_, reads, writes):
+        prepare(q, reads, writes)
+        sem = "d%d" % dma[0]
+        dma[0] += 1
+        eng[q].dma_start(out, in_).then_inc(T.sem[sem], 16)
+        record(q + "*", sem, 16, reads, writes)
+
+    def landed(region, sem, count):
+        hist.setdefault(region[0], []).append((region[1], region[2], True, "net", sem, count, {}))
+
+    def finish(extra):
+        for q in cnt:
+            if cnt[q]:
+                g.wait_ge(T.sem["q" + q], cnt[q])
+        for i in range(dma[0]):
+            g.wait_ge(T.sem["d%d" % i], 16)
+        for s, n in extra:
+            g.wait_ge(T.sem[s], n)
+
+    return op, copy, landed, prepare, finish
+
+
+def alternate(a, b):
+    for i in range(max(len(a), len(b))):
+        for c in (a, b):
+            if i < len(c):
+                c[i]()
+
+
+def rank_program(g, core, T, topo):
+    rank = T.rank_of(core)
+    if rank is None:
+        return
+    cores = T.cores
+    N = len(cores)
+    op, copy, landed, prepare, finish = layer(g, T)
+    V, S, P = g.vector, g.scalar, g.tensor
+    sent = [0]
+
+    def v(f, r, w):
+        op("V", f, r, w)
+
+    def s(f, r, w):
+        op("S", f, r, w)
+
+    def p(f, r, w):
+        op("P", f, r, w)
+
+    def tc(o, i):
+        return lambda: V.tensor_copy(o, i)
+
+    def tt(o, a, b, f):
+        return lambda: V.tensor_tensor(o, a, b, f)
+
+    def ts(o, a, s1, f1, s2=None, f2=None):
+        if f2 is None:
+            return lambda: V.tensor_scalar(o, a, s1, None, f1)
+        return lambda: V.tensor_scalar(o, a, s1, s2, f1, f2)
+
+    def ms(o, c):
+        return lambda: V.memset(o, c)
+
+    def act(o, i, f=AF.Copy, bias=0.0, scale=1.0):
+        return lambda: S.activation(o, i, f, bias=bias, scale=scale)
+
+    def mm(o, l, r, st=True, sp=True):
+        return lambda: P.matmul(o, l, r, st, sp)
+
+    def send(dst, out, in_, reads, sem):
+        d = cores[dst]
+        prepare("G", reads, [])
+        rid, pid = topo.addr(d, core)
+        g.remote_dma(out, in_, T.sem[sem], T.sem.ls, pid, rid, topo.mask(core, d))
+        sent[0] += len(topo.engines(core, d))
+
+    def iota(name, view, pat, base, ch, fl=False):
+        if fl:
+            op("G", lambda: g.iota(view, pat, base, ch, allow_small_or_imprecise_dtypes=True), [], [name])
+        else:
+            op("G", lambda: g.iota(view, pat, base, ch), [], [name])
+
+    v([ms(T.xw[:, 0:1], LOW), ms(T.sd[:, 0:1], 0.0)], [], [("xw", 0, 16), ("sd", 0, 16)])
+    copy("Y", T.anI[:], T.an0[:], [], ["anI"])
+    copy("Y", T.ofI[:], T.of0[:], [], ["ofI"])
+    copy("S", T.wkb[:], T.wk[:], [], ["wkb"])
+    copy("Y", T.sd[:, 1:2049], T.s0[:], [], [("sd", 1, 2049)])
+    copy("Y", T.xw[:, 1:1025], T.x[:], [], [("xw", 1, 1025)])
+    copy("Y", T.snI[:], T.snd[:], [], ["snI"])
+    iota("pI", T.pI[:, 0:1], [[0, 1]], 0, 1)
+    iota("n512", T.n512[:], [[1, 512]], 0, 0)
+    iota("v1c", T.v1c[:, 0:8], [[128, 8]], 1, 1, True)
+    iota(("pw", 1025, 1794), T.pw[:, 1025:1794], [[0, 769]], 1793, 0, True)
+    iota(("p2w", 1025, 1794), T.p2w[:, 1025:1794], [[0, 769]], 1793, 0, True)
+    iota("ct8", T.ct8[:], [[0, 16], [1, 8]], -256, 0, True)
+    iota("ck", T.ck[:], [[-4096, 16], [0, 16]], 61440, 0, True)
+    iota("ckg", T.ckg[:], [[-4096, 16], [0, 8]], 61440, 0, True)
+    iota("du", T.du[:, 0:16], [[16, 16]], 2056, 0, True)
+    iota("smI", T.smI[:], [[16, 8], [1, 128]], -127, 0, True)
+
+    P15, P4, PC = T.pp[:, 0:1], T.pp[:, 1:2], T.pp[:, 2:3]
+    N1, G8, K1 = T.n512[:, 0:128], T.n512[:, 0:8], T.kI[:, 0:128]
+    v(ms(T.one[:], 1.0), [], ["one"])
+    v([ts(T.pI[:, 1:2], T.pI[:, 0:1], 15, A.bitwise_and), ts(T.pI[:, 2:3], T.pI[:, 0:1], 4, A.arith_shift_right)], ["pI"], ["pI2"])
+    v([tc(P15, T.pI[:, 1:2]), tc(P4, T.pI[:, 2:3]), tc(PC, T.pI[:, 0:1])], ["pI", "pI2"], ["pp"])
+    v([ts(T.lmc[:], T.n512[:, 0:16], P15, A.is_equal), ts(T.m4[:], N1, 4, A.arith_shift_right), ts(T.kI[:], T.n512[:, 0:256], 15, A.bitwise_and)], ["n512", "pp"], ["lmc", "m4", "kI"])
+    v([ts(T.idb[:], N1, PC, A.is_equal), ts(T.id16[:], N1, PC, A.is_equal), ts(T.idF[:], N1, PC, A.is_equal)], ["n512", "pp"], ["idb", "id16", "idF"])
+    s([act(T.selb[:, 128 * k:128 * k + 128], T.idb[:], AF.Copy, 0.0, T.lmc[:, k:k + 1]) for k in range(16)], ["idb", "lmc"], ["selb"])
+    v(ts(T.an1[:], T.anI[:], 1.0, A.add), ["anI"], ["an1"])
+    v([ts(T.gb16[:], T.m4[:], P4, A.is_equal), tc(T.l1[:], T.an1[:])], ["m4", "pp", "an1"], ["gb16", "l1"])
+    v([ms(T.pw[:, 0:1], 1793.0), ms(T.p2w[:, 0:1], 1793.0)], [], [("pw", 0, 1), ("p2w", 0, 1)])
+    v([ts(T.rf16[:, k::16], T.an1[:], T.lmc[:, k:k + 1], A.mult) for k in range(16)], ["an1", "lmc"], ["rf16"])
+    p([mm(T.pG[:], T.gb16[:], T.rf16[:, 0:512]), mm(T.pH[:], T.gb16[:], T.rf16[:, 512:1024])], ["gb16", "rf16"], ["pG", "pH"])
+    s(act(T.pw[:, 1:513], T.pG[:]), ["pG"], [("pw", 1, 513)])
+    s(act(T.pw[:, 513:1025], T.pH[:]), ["pH"], [("pw", 513, 1025)])
+    v(tc(T.of16[:], T.ofI[:]), ["ofI"], ["of16"])
+    v([ts(T.ofE[:, k::16], T.of16[:], T.lmc[:, k:k + 1], A.mult) for k in range(16)], ["of16", "lmc"], ["ofE"])
+    OFB = [(bank, 512 * b, min(512 * b + 512, 1792)) for b, bank in enumerate(("pA", "pB", "pC", "pD"))]
+    for bank, lo, hi in OFB:
+        p(mm(T[bank][:, 0:hi - lo], T.gb16[:], T.ofE[:, lo:hi]), ["gb16", "ofE"], [bank])
+    for bank, lo, hi in OFB[:2]:
+        s(act(T.wd[:, lo:hi], T[bank][:]), [bank], [("wd", lo, hi)])
+    for bank, lo, hi in OFB:
+        s(act(T.w1[:, lo + 1:hi + 1], T[bank][:, 0:hi - lo]), [bank], [("w1", lo + 1, hi + 1)])
+    v(lambda: V.tensor_copy(T.p2w[:, 1:1025], T.pw[:, 0:1794].indirect(T.l1[:])), ["pw", "l1"], [("p2w", 1, 1025)])
+    v(tc(T.rf16[:], T.p2w[:, 1:1025]), ["p2w"], ["rf16"])
+
+    def conv(src, name, c0, cols, sel, bank, extra=None):
+        o = T[bank][:, 0:cols]
+        fs = [mm(o, T[sel][:, 128 * k:128 * k + 128], src[:, c0 + k:c0 + 16 * cols:16], k == 0, k == 15 and extra is None) for k in range(16)]
+        if extra is not None:
+            fs.append(mm(o, T.id16[:], T[extra][:], False, True))
+        p(fs, [(name, c0, c0 + 16 * cols), sel, "id16"] + ([extra] if extra else []), [bank])
+
+    conv(T.rf16, "rf16", 0, 64, "selb", "pF")
+    v([ts(T.seven[:], N1, PC, A.is_equal, 7.0, A.mult), ts(T.m1k[:], N1, PC, A.is_equal, -1024.0, A.mult), ts(T.lo16[:], T.n512[:], 1.0, A.add)], ["n512", "pp"], ["seven", "m1k", "lo16"])
+
+    def weeks(b, second):
+        bank, c = ("pE", "pH", "pA", "pB")[b], 512 * b
+        f = [mm(T[bank][:], T.seven[:], T.wkb[:, c:c + 512], True, False), mm(T[bank][:], T.id16[:], T.lo16[:], False, not second)]
+        if second:
+            f.append(mm(T[bank][:], T.m1k[:], T.sg[:, c:c + 512], False, True))
+        p(f, ["seven", "wkb", "id16", "lo16", "m1k"] + ([("sg", c, c + 512)] if second else []), [bank])
+        if second:
+            s(act(T.cw[:, 1 + c:513 + c], T[bank][:], AF.Copy, c - 1024.0), [bank], [("cw", 1 + c, 513 + c)])
+        else:
+            s(act(T.sg[:, c:c + 512], T[bank][:], AF.Sign, c - 2048.5), [bank], [("sg", c, c + 512)])
+            if b > 1:
+                s(act(T.sg[:, c:c + 512], T.sg[:, c:c + 512], AF.Copy, c - 1024.0, -1024.0), [("sg", c, c + 512)], [("sg", c, c + 512)])
+
+    zs = [("w1", 1793, 2064), ("w1", 0, 1), ("w2", 1793, 1794), ("w2", 0, 1), ("w3", 1793, 1794), ("w3", 0, 1), ("t8", 0, 1)]
+    v([ms(T[n][:, a:b], 0.0) for n, a, b in zs] + [ms(T.dbi[:, 0:1], 0), ms(T.cv[:, 0:1], 1.0), ms(T.cw[:, 0:1], 1.0), ms(T.xg[:, 0:1], LOW)], [],
+      zs + [("dbi", 0, 1), ("cv", 0, 1), ("cw", 0, 1), ("xg", 0, 1)])
+    for n in ("w2", "w3"):
+        s(act(T[n][:, 1025:1537], T.pC[:]), ["pC"], [(n, 1025, 1537)])
+        s(act(T[n][:, 1537:1793], T.pD[:, 0:256]), ["pD"], [(n, 1537, 1793)])
+    W = ("w1", "w2", "w3")
+    PH = ("p1h", "p2h", "p3h")
+    LL = ("l1", "l2", "l3")
+
+    def addend(l):
+        for h in (0, 1):
+            a = 512 * h
+            s(act(T.wd[:, a:a + 512], T[W[l]][:, 1 + a:513 + a]), [(W[l], 1 + a, 513 + a)], [("wd", a, a + 512)])
+
+    def jump(l, halves=(0, 1)):
+        nm = "t8" if l == 2 else W[l + 1]
+        for h in halves:
+            a = 512 * h
+            v(tt(T[nm][:, a + 1:a + 513], T[W[l]][:, 0:1794].indirect(T[LL[l]][:, 32 * h:32 * h + 32]), T.wd[:, a:a + 512], A.add),
+              [(W[l], 0, 1794), LL[l], ("wd", a, a + 512)], [(nm, a + 1, a + 513)])
+
+    def jumplist(l):
+        for h in (0, 1):
+            a = 512 * h
+            s(act(T.fl[:, a:a + 512], T[W[l]][:, 1 + a:513 + a], AF.Relu, -2048.0, 0.015625), [(W[l], 1 + a, 513 + a)], [("fl", a, a + 512)])
+        conv(T.fl, "fl", 0, 64, "selb", "pF", PH[l])
+        addend(l)
+
+    def jumplist2(l):
+        v(ts(T[LL[l]][:], T.pF[:, 0:64], 1793.0, A.min), ["pF"], [LL[l]])
+
+    s([act(T.selF[:, 128 * k:128 * k + 128], T.idF[:], AF.Copy, 0.0, T.lmc[:, k:k + 1]) for k in range(16)], ["idF", "lmc"], ["selF"])
+    weeks(0, False)
+    weeks(1, False)
+    v(tc(T.l2[:], T.pF[:, 0:64]), ["pF"], ["l2"])
+    v(tc(T.p2h[:], T.pF[:, 0:64]), ["pF"], ["p2h"])
+    v(lambda: V.tensor_copy(T.rf16[:], T.p2w[:, 0:1794].indirect(T.l2[:])), ["p2w", "l2"], ["rf16"])
+    conv(T.rf16, "rf16", 0, 64, "selb", "pF")
+    jump(0)
+    addend(1)
+    jump(1)
+    addend(2)
+    weeks(2, False)
+    weeks(3, False)
+    weeks(0, True)
+    weeks(1, True)
+    v(tc(T.l3[:], T.pF[:, 0:64]), ["pF"], ["l3"])
+    v([tc(T.p3h[:], T.pF[:, 0:64]), tc(T.p1h[:], T.an1[:])], ["pF", "an1"], ["p3h", "p1h"])
+    jump(2)
+    conv(T.t8, "t8", 1, 64, "selF", "pG")
+    v(ts(T.sl[:], T.snI[:], 1.0, A.add), ["snI"], ["sl"])
+    for bank, c in (("pA", 1024), ("pB", 1536)):
+        v(tt(T.cw[:, 1 + c:513 + c], T[bank][:], T.sg[:, c:c + 512], A.add), [bank, ("sg", c, c + 512)], [("cw", 1 + c, 513 + c)])
+    v([ts(T.gib[:], G8, P4, A.is_equal), ts(T.gi16[:], G8, P4, A.is_equal), ts(T.gik[:], G8, P4, A.is_equal, BIG, A.mult)], ["n512", "pp"], ["gib", "gi16", "gik"])
+    v([ts(T.cq[:, 0:128], N1, PC, A.is_equal, -4096.0, A.mult), ts(T.cq[:, 128:256], N1, PC, A.is_gt)], ["n512", "pp"], ["cq"])
+    v(tt(T.upr[:], T.cq[:, 0:128], T.cq[:, 128:256], A.add), ["cq"], ["upr"])
+    v([ms(T.bz[:, 0:56], 0.0), ms(T.rz[:, 0:8], 0.0), ms(T.wg[:, 64:128], 0.0)], [], [("bz", 0, 56), ("rz", 0, 8), ("wg", 64, 128)])
+    v([ts(T.tc[:, 5:6], P4, 17.0, A.mult), ts(T.v1c[:, 8:16], T.v1c[:, 0:8], 0.5, A.mult)], ["pp", "v1c"], ["tcd", "v1c"])
+    v(tt(T.tc[:, 7:8], T.tc[:, 5:6], P15, A.add), ["tcd", "pp"], ["tce"])
+    v([tc(T.dgt[:, 0:1], T.tc[:, 7:8]), ts(T.dgt[:, 2:3], T.tc[:, 7:8], 1.0, A.add), tc(T.ex[:], T.n512[:, 0:16])], ["tce", "n512"], ["dgl", "ex"])
+
+    def constants2():
+        v([tc(T.lane[:], T.kI[:]), ts(T.mk[:], T.kI[:], P15, A.is_equal), ts(T.mkg[:, 0:128], K1, 0.0, A.is_ge), ts(T.mkg[:, 128:256], K1, P15, A.is_equal)], ["kI", "pp"], ["lane", "mk", "mkg"])
+        v([ts(T.tc[:, 0:1], P15, 16.0, A.mult), ts(T.tc[:, 1:2], P15, 8.0, A.mult), ts(T.tc[:, 3:4], P4, 8.0, A.mult), ts(T.tc[:, 2:3], P15, 8.0, A.is_ge),
+           ts(T.smi[:, 0:16], T.n512[:, 0:16], 7, A.bitwise_and)], ["pp", "n512"], ["tc", "smi"])
+        v([tt(T.sm[:, 0:1], T.tc[:, 0:1], P4, A.add), tt(T.sm[:, 1:2], T.tc[:, 1:2], P4, A.add), tt(T.sm[:, 3:4], T.tc[:, 3:4], P15, A.add)], ["tc", "pp"], ["sm"])
+        v([ts(T.sm[:, 2:3], T.sm[:, 0:1], 8.0, A.add), tc(T.dgt[:, 4:5], T.sm[:, 3:4])], ["sm"], ["dg8", "sm2"])
+        v([ts(T.pm0[:], T.n512[:, 0:256], T.sm[:, 0:1], A.is_equal), ts(T.pm1[:], T.n512[:, 0:256], T.sm[:, 2:3], A.is_equal), ts(T.pmg[:], N1, T.sm[:, 1:2], A.is_equal)],
+          ["n512", "sm", "sm2"], ["pm0", "pm1", "pmg"])
+        v([ts(T.j16[:], N1, PC, A.add, 127.0, A.is_equal), ts(T.jF[:], N1, PC, A.add, 127.0, A.is_equal), tc(T.exg[:], T.smi[:, 0:16]), ts(T.ex8[:], G8, 2.0, A.mult, T.tc[:, 2:3], A.add),
+           ts(T.du[:, 0:16], T.du[:, 0:16], P15, A.add)], ["n512", "pp", "smi", "tc", "du"], ["j16", "jF", "exg", "ex8", "du"])
+        v(ts(T.du[:, 16:32], T.du[:, 0:16], -256.0, A.add), ["du"], ["du"])
+        v(ms(T.thr[:, 0:1], 9.0 * BIG), [], ["thr"])
+
+    DUS, DUW = T.du[:, 0:16], T.du[:, 16:32]
+
+    def tree(w):
+        v(tc(T.kb[:, 0:8 * w], T.pD[:, 8 * w:16 * w]), ["pD"], ["kb"])
+        v(tt(T.ka[:, 0:8 * w], T.pD[:, 0:8 * w], T.kb[:, 0:8 * w], A.max), ["pD", "kb"], ["ka"])
+        v(tt(T.kb[:, 0:4 * w], T.ka[:, 0:4 * w], T.ka[:, 4 * w:8 * w], A.max), ["ka"], ["kb"])
+        v(tt(T.ka[:, 0:2 * w], T.kb[:, 0:2 * w], T.kb[:, 2 * w:4 * w], A.max), ["kb"], ["ka"])
+        v(tt(T.ks[:, 0:w], T.ka[:, 0:w], T.ka[:, w:2 * w], A.max), ["ka"], [("ks", 0, 16)])
+        v([ts(T.ks[:, 16:16 + w], T.ks[:, 0:w], T.thr[:, 0:1], A.is_ge), tc(T.smi[:, 0:w], T.ks[:, 0:w])], [("ks", 0, 16), "thr"], [("ks", 16, 32), ("smi", 0, 16)])
+
+    def chosen(w):
+        v(ts(T.smi[:, 16:16 + w], T.smi[:, 0:w], 4095, A.bitwise_and), [("smi", 0, 16)], [("smi", 16, 32)])
+        v(tt(T.ks[:, 48:48 + w], T.smi[:, 16:16 + w], T.ks[:, 16:16 + w], A.mult), [("smi", 16, 32), ("ks", 16, 32)], [("ks", 48, 64)])
+
+    def eqdays(nh):
+        for h in range(nh):
+            v([ts(T.eq[:, b * 128:b * 128 + 128], T.rr[:, 128 * h:128 * h + 128], T.sm[:, 112 + b:113 + b], A.is_equal) for b in range(8 * h, 8 * h + 8)],
+              ["rr", ("sm", 112, 128)], [("eq", 1024 * h, 1024 * h + 1024)])
+
+    def scan(h):
+        a = slice(1024 * h, 1024 * h + 1024)
+        v(lambda: V.tensor_tensor_scan(T.scn[:, a], T.eq[:, a], T.smk[:], 0.0, A.max, A.mult), [("eq", a.start, a.stop), "smk"], [("scn", a.start, a.stop)])
+
+    def dayoffsets(w):
+        return [
+            lambda: v(tt(T.sm[:, 80:80 + w], T.scn[:, 127:128 * w:128], T.du[:, 0:w], A.mult), ["scn", "du"], [("sm", 80, 96)]),
+            lambda: v(tt(T.sm[:, 96:96 + w], T.sm[:, 64:64 + w], T.sm[:, 80:80 + w], A.max), [("sm", 64, 96)], [("sm", 96, 112)]),
+            lambda: v(tc(T.u16s[:, 16:16 + w], T.sm[:, 96:96 + w]), [("sm", 96, 112)], [("u16s", 16, 32)])]
+
+    def copies(q, src, sname, so, dst, n, ks):
+        f = act if q == "S" else tc
+        op(q, [f(T.xr[:, dst + k:dst + 16 * n:16], src[:, so:so + n]) for k in ks], [(sname, so, so + n)], [("xr" + q, dst, dst + 1)])
+
+    for t in range(RO):
+        last = t == RO - 1
+        gxa, gda, gha = (128 * t, 128 * t + 128), (16 * t, 16 * t + 8), (768 * t, 768 * t + 768)
+        to, fro = (rank + 1 + t % (N - 1)) % N, (rank - 1 - t % (N - 1)) % N
+        if not last:
+            s(act(T.ghs[:, gha[0]:gha[1]], T.t8[:, 0:1025].indirect(T.sl[:])), [("t8", 0, 1025), "sl"], [("ghs",) + gha])
+            for d in range(1, N):
+                a = gha[0] + 256 * (d - 1)
+                send((rank + d) % N, T.ghl[:, a:a + 256], T.ghs[:, a:a + 256], [("ghs", a, a + 256)], "gh%d" % t)
+            landed(("ghl",) + gha, "gh%d" % t, sum(len(topo.engines(cores[(rank - d) % N], core)) for d in range(1, N)))
+        v(tc(T.ldI[:], T.pG[:, 0:64]), ["pG"], ["ldI"])
+        v(ts(T.ldI[:], T.ldI[:], 2047, A.bitwise_and), ["ldI"], ["ldI"])
+        v(ts(T.lfd[:], T.ldI[:], 1.0, A.add), ["ldI"], ["lfd"])
+        for h in (0, 1):
+            s(act(T.cv[:, 1 + 512 * h:513 + 512 * h], T.cw[:, 0:2049].indirect(T.lfd[:, 32 * h:32 * h + 32])), ["cw", "lfd"], [("cv", 1 + 512 * h, 513 + 512 * h)])
+            v(tt(T.cmp[:, 512 * h:512 * h + 512], T.sd[:, 0:2049].indirect(T.lfd[:, 32 * h:32 * h + 32]), T.xw[:, 1 + 512 * h:513 + 512 * h], A.is_le),
+              [("sd", 0, 2049), "lfd", ("xw", 1, 1025)], [("cmp", 512 * h, 512 * h + 512)])
+            p([mm(T.pA[:, 8 * c:8 * c + 8], T.cmp[:, 128 * c:128 * c + 128], T.gib[:]) for c in range(4 * h, 4 * h + 4)], [("cmp", 512 * h, 512 * h + 512), "gib"], ["pA"])
+        v(ts(T.bz[:, 56:120], T.pA[:, 0:64], 4.5, A.is_lt), ["pA"], [("bz", 56, 120)])
+        p([mm(T.pB[:, 0:64], T.upr[:], T.bz[:, 56:120], True, False)] + [mm(T.pB[:, 0:64], T.one[:], T.bz[:, 56 - 8 * q:120 - 8 * q], False, q == 7) for q in range(1, 8)],
+          ["upr", "one", "bz"], ["pB"])
+        v(tc(T.rkI[:], T.pB[:, 0:64]), ["pB"], ["rkI"])
+        s([act(T.th[:, c::17], T.pB[:, 0:64], AF.Sign, 16.0 * c - 4096.5, -1.0) for c in range(17)], ["pB"], ["th"])
+        p([mm(T.pH[:, 0:8], T.one[:], T.bz[:, 56 + 8 * c:64 + 8 * c], c == 0, c == 7) for c in range(8)], ["one", "bz"], ["pH"])
+        v(ts(T.loI[:], T.rkI[:], 15, A.bitwise_and), ["rkI"], ["loI"])
+        v([ts(T.oa[:, i::16], T.loI[:], float(i), A.is_equal) for i in range(16)], ["loI"], ["oa"])
+        for c in range(8):
+            a = slice(128 * c, 128 * c + 128)
+            v(ts(T.oa[:, a], T.oa[:, a], T.v1c[:, 8 + c:9 + c], A.mult), [("oa", a.start, a.stop), "v1c"], [("oa", a.start, a.stop)])
+            p(mm(T.pC[:, 0:136], T.oa[:, a], T.th[:, 136 * c:136 * c + 136], c == 0, c == 7), [("oa", a.start, a.stop), "th"], ["pC"])
+        if t == 0:
+            s(act(T.smI[:], T.smI[:], AF.Sign, P15), ["smI", "pp"], ["smI"])
+            s(act(T.smk[:], T.smI[:], AF.Relu), ["smI"], ["smk"])
+            constants2()
+        v(tc(T.win[:, 0:136], T.pC[:, 0:136]), ["pC"], ["win"])
+        v(tc(T.g1[:], T.win[:, 0:136].indirect(T.dgt[:, 0:1])), ["win", "dgl"], ["g1"])
+        v(tt(T.lvf[:], T.win[:, 0:136].indirect(T.dgt[:, 2:3]), T.g1[:], A.subtract), ["win", "dgl", "g1"], ["lvf"])
+        v(tc(T.lv[:], T.lvf[:]), ["lvf"], ["lv"])
+        s(act(T.xg[:, 1:257], T.xw[:, 0:1025].indirect(T.lv[:])), ["xw", "lv"], [("xg", 1, 257)])
+        v(tc(T.cg[:], T.cv[:, 0:1025].indirect(T.lv[:])), ["cv", "lv"], ["cg"])
+        copies("S", T.xg, "xg", 1, 0, 128, range(11, 16))
+        copies("V", T.xg, "xg", 1, 0, 128, range(0, 11))
+        copies("S", T.xg, "xg", 129, 2048, 128, range(0, 16))
+        s(act(T.cgf[:], T.cv[:, 0:1025].indirect(T.lv[:])), ["cv", "lv"], ["cgf"])
+        s(act(T.dbf[:], T.t8[:, 0:1025].indirect(T.lv[:])), [("t8", 0, 1025), "lv"], ["dbf"])
+        p([mm(T.pD[:, 0:256], T.cgf[:, 0:128], T.pm0[:], True, False), mm(T.pD[:, 0:256], T.cgf[:, 128:256], T.pm1[:], False, False)], ["cgf", "pm0", "pm1"], ["pD"])
+        for h in (0, 1):
+            a = slice(2048 * h, 2048 * h + 2048)
+            v(tt(T.cmp[:, a], T.sd[:, 0:2049].indirect(T.cg[:, 128 * h:128 * h + 128]), T.xr[:, a], A.is_lt),
+              [("sd", 0, 2049), "cg", ("xrS", a.start, a.start + 1), ("xrV", a.start, a.start + 1)], [("cmp", a.start, a.stop)])
+            p([mm(T.pD[:, 16 * k + 8 * h:16 * k + 8 * h + 8], T.cmp[:, a.start + k:a.stop:16], T.gik[:], False, False) for k in range(16)], [("cmp", a.start, a.stop), "gik"], ["pD"])
+        p(mm(T.pD[:, 0:256], T.one[0:1, :], T.ck[:], False, True), ["one", "ck"], ["pD"])
+        if not last:
+            for wn in W:
+                s(act(T[wn][:, 1025:1793], T.ghl[:, gha[0]:gha[1]]), [("ghl",) + gha], [(wn, 1025, 1793)])
+        v(tc(T.dbi[:, 1:257], T.dbf[:]), ["dbf"], [("dbi", 1, 257)])
+        v(tc(T.nb[:], T.pH[:, 0:8]), ["pH"], ["nb"])
+        v(ts(T.dbi[:, 1:257], T.dbi[:, 1:257], 2047, A.bitwise_and), [("dbi", 1, 257)], [("dbi", 1, 257)])
+        v([ts(T.vld[:, 8 * q:8 * q + 8], T.nb[:], T.v1c[:, q:q + 1], A.is_ge) for q in (0, 1)], ["nb", "v1c"], ["vld"])
+        tree(16)
+        v(tt(T.rz[:, 8:24], T.vld[:], T.ks[:, 16:32], A.subtract), ["vld", ("ks", 16, 32)], [("rz", 8, 24)])
+        p([mm(T.pB[:, 0:16], T.upr[:], T.rz[:, 8:24], True, False), mm(T.pB[:, 0:16], T.one[:], T.rz[:, 0:16], False, True)], ["upr", "one", "rz"], ["pB"])
+        chosen(16)
+        s(act(T.xf[:], T.ks[:, 48:64].indirect(T.ex[:])), [("ks", 48, 64), "ex"], ["xf"])
+        v(tc(T.rkI[:, 0:16], T.pB[:, 0:16]), ["pB"], ["rkI"])
+        v([ts(T.loI[:, 0:16], T.rkI[:, 0:16], 15, A.bitwise_and), ts(T.hiI[:, 0:16], T.rkI[:, 0:16], 4, A.arith_shift_right)], ["rkI"], ["loI", "hiI"])
+        v(tt(T.oa[:, 0:256], T.loI[:, 0:16].indirect(T.ex[:]), T.lane[:], A.is_equal), ["loI", "ex", "lane"], [("oa", 0, 256)])
+        v(tt(T.ob[:], T.hiI[:, 0:16].indirect(T.ex8[:]), T.ct8[:], A.is_equal), ["hiI", "ex8", "ct8"], ["ob"])
+        v([ts(T.oa[:, 256 + 128 * q:384 + 128 * q], T.oa[:, 128 * q:128 * q + 128], T.v1c[:, q:q + 1], A.mult) for q in (0, 1)], [("oa", 0, 256), "v1c"], [("oa", 256, 512)])
+        p([mm(T.pE[:, 128 * q:128 * q + 128], T.xf[:, 128 * q:128 * q + 128], T.idF[:]) for q in (0, 1)], ["xf", "idF"], ["pE"])
+        p([mm(T.pC[:, 0:64], T.oa[:, 256 + 128 * q:384 + 128 * q], T.ob[:, 64 * q:64 * q + 64], q == 0, q == 1) for q in (0, 1)], [("oa", 256, 512), "ob"], ["pC"])
+        v(tt(T.xe[:], T.ks[:, 48:64].indirect(T.ex[:]), T.mk[:], A.mult), [("ks", 48, 64), "ex", "mk"], ["xe"])
+        p([mm(T.pA[:, 8 * q:8 * q + 8], T.xe[:, 128 * q:128 * q + 128], T.gi16[:]) for q in (0, 1)], ["xe", "gi16"], ["pA"])
+        v(tc(T.wg[:, 0:64], T.pC[:, 0:64]), ["pC"], [("wg", 0, 64)])
+        v(lambda: V.tensor_reduce(T.thr[:, 1:2], T.ks[:, 16:32], AX.X, A.add), [("ks", 16, 32)], ["thr1"])
+        v(tc(T.gl[:], T.wg[:].indirect(T.dgt[:, 4:5])), ["wg", "dg8"], ["gl"])
+        v(tc(T.rdb[:, 0:1], T.thr[:, 1:2]), ["thr1"], ["rdb"])
+        v(tc(T.dgh[:], T.dbi[:, 0:257].indirect(T.gl[:, 0:8])), ["dbi", "gl"], ["dgh"])
+        conv(T.dgh, "dgh", 0, 8, "selb", "pF")
+        p([mm(T.pH[:, 256 + 128 * q:384 + 128 * q], T.xf[:, 128 * q:128 * q + 128], T.jF[:]) for q in (0, 1)], ["xf", "jF"], ["pH"])
+        if not last:
+            p(mm(T.pB[:, 64:65], T.one[:], T.rdb[:, 0:1]), ["one", "rdb"], ["pB"])
+        v(tc(T.gxs[:, gxa[0]:gxa[1]], T.xg[:, 0:257].indirect(T.gl[:, 0:8])), ["xg", "gl"], [("gxs",) + gxa])
+        send(to, T.gxl[:, gxa[0]:gxa[1]], T.gxs[:, gxa[0]:gxa[1]], [("gxs",) + gxa], "gx%d" % t)
+        s(act(T.wv[:], T.pE[:, 0:256], AF.Copy, FLAG - 1.0), ["pE"], ["wv"])
+        v(tc(T.sm[:, 112:128], T.pA[:, 0:16]), ["pA"], [("sm", 112, 128)])
+        v(ts(T.sm[:, 0:16], T.sm[:, 112:128], 0.5, A.is_lt), [("sm", 112, 128)], [("sm", 0, 16)])
+        v([tt(T.sm[:, 32:48], T.sm[:, 0:16], DUW, A.mult), tt(T.sm[:, 16:32], T.sm[:, 0:16], DUS, A.mult)], [("sm", 0, 16), "du"], [("sm", 16, 48)])
+        v(ts(T.gds[:, gda[0]:gda[1]], T.pF[:, 0:8], 1.0, A.add), ["pF"], [("gds",) + gda])
+        send(to, T.gdl[:, gda[0]:gda[1]], T.gds[:, gda[0]:gda[1]], [("gds",) + gda], "gd%d" % t)
+        ne = len(topo.engines(cores[fro], core))
+        landed(("gxl",) + gxa, "gx%d" % t, ne)
+        landed(("gdl",) + gda, "gd%d" % t, ne)
+        v([tt(T.sm[:, 48:64], T.sm[:, 32:48], T.lvf[:], A.max), tt(T.sm[:, 64:80], T.sm[:, 16:32], T.sm[:, 112:128], A.max)], [("sm", 16, 48), ("sm", 112, 128), "lvf"], [("sm", 48, 80)])
+        v(tc(T.u16s[:, 0:16], T.sm[:, 48:64]), [("sm", 48, 64)], [("u16s", 0, 16)])
+        v(lambda: V.tensor_copy(T.w1[:, 0:2064].indirect(T.u16s[:, 0:16]), T.wv[:]), ["wv", ("u16s", 0, 16)], ["w1"])
+        if last:
+            copy("Y", T.yb[:, 256:320], T.w1[0:128:16, 1:1025], [("w1", 1, 1025)], [("yb", 256, 320)])
+            copy("Y", T.yb[:, 320:384], T.pw[0:128:16, 1:1025], [("pw", 1, 1025)], [("yb", 320, 384)])
+        else:
+            jumplist(0)
+        v(tc(T.rr[:], T.pH[:, 256:512]), ["pH"], ["rr"])
+        eqdays(2)
+        scan(0)
+        scan(1)
+        alternate(dayoffsets(16), [] if last else [lambda: jumplist2(0), lambda: jump(0, (0,)), lambda: jump(0, (1,)), lambda: jumplist(1)])
+        v(lambda: V.tensor_copy(T.sd[:, 0:2320].indirect(T.u16s[:, 24:32]), T.xg[:, 129:257]), [("xg", 1, 257), ("u16s", 16, 32)], ["sd"])
+        if not last:
+            v(tc(T.smi[:, 40:41], T.pB[:, 64:65]), ["pB"], [("smi", 40, 41)])
+        v(lambda: V.tensor_copy(T.sd[:, 0:2320].indirect(T.u16s[:, 16:24]), T.xg[:, 1:129]), [("xg", 1, 257), ("u16s", 16, 32)], ["sd"])
+        copies("S", T.gxl, "gxl", gxa[0], 0, 128, range(0, 16))
+        gl = T.gdl[:, gda[0]:gda[1]]
+        s(act(T.cgf[:, 0:128], T.cw[:, 0:2049].indirect(gl)), ["cw", ("gdl",) + gda], ["cgf"])
+        if not last:
+            v(ts(T.smi[:, 41:42], T.smi[:, 40:41], 1, A.bitwise_and), [("smi", 40, 41)], [("smi", 41, 42)])
+            jumplist2(1)
+            jump(1)
+            jumplist(2)
+        v(tc(T.cg[:, 0:128], T.cw[:, 0:2049].indirect(gl)), ["cw", ("gdl",) + gda], ["cg"])
+        p(mm(T.pD[:, 0:128], T.cgf[:, 0:128], T.pmg[:], True, False), ["cgf", "pmg"], ["pD"])
+        v(tt(T.cmp[:, 0:2048], T.sd[:, 0:2049].indirect(T.cg[:, 0:128]), T.xr[:, 0:2048], A.is_lt),
+          [("sd", 0, 2049), "cg", ("xrS", 0, 1), ("xrV", 0, 1)], [("cmp", 0, 2048)])
+        p([mm(T.pD[:, 8 * k:8 * k + 8], T.cmp[:, k:2048:16], T.gik[:], False, False) for k in range(16)] +
+          [mm(T.pD[:, 0:128], T.one[0:1, :], T.ckg[:], False, True)], [("cmp", 0, 2048), "gik", "one", "ckg"], ["pD"])
+        if not last:
+            jumplist2(2)
+            jump(2)
+        else:
+            wf, pf = T.yb[:, 256:320], T.yb[:, 320:384]
+            v([ts(T.yb[:, 0:64], wf, 131072.0, A.is_ge, 1792.0, A.mult), ts(T.yb[:, 64:128], wf, 131072.0, A.is_ge, -FLAG, A.mult), ts(pf, pf, -1.0, A.add)], [("yb", 256, 384)], [("yb", 0, 128), ("yb", 320, 384)])
+            v([tt(T.yb[:, 128:192], T.yb[:, 0:64], pf, A.max), tt(T.yb[:, 192:256], T.yb[:, 64:128], wf, A.add)], [("yb", 0, 128), ("yb", 256, 384)], [("yb", 128, 256)])
+            copy("Y", T.yan[:], T.yb[:, 128:192], [("yb", 128, 192)], [])
+            copy("Y", T.yof[:], T.yb[:, 192:256], [("yb", 192, 256)], [])
+        tree(8)
+        chosen(8)
+        v(tt(T.xe[:], T.ks[:, 48:56].indirect(T.exg[:]), T.mkg[:], A.mult), [("ks", 48, 64), "exg", "mkg"], ["xe"])
+        p(mm(T.pA[:, 0:8], T.xe[:, 128:256], T.gi16[:]), ["xe", "gi16"], ["pA"])
+        p(mm(T.pH[:, 256:384], T.xe[:, 0:128], T.j16[:]), ["xe", "j16"], ["pH"])
+        if not last:
+            conv(T.t8, "t8", 1, 64, "selF", "pG")
+            v(ts(T.thr[:, 0:1], T.smi[:, 41:42], BIG, A.mult, 9.0 * BIG, A.add), [("smi", 41, 42)], ["thr"])
+        v(tc(T.sm[:, 112:120], T.pA[:, 0:8]), ["pA"], [("sm", 112, 128)])
+        v(tc(T.rr[:, 0:128], T.pH[:, 256:384]), ["pH"], ["rr"])
+        v(ts(T.sm[:, 0:8], T.sm[:, 112:120], 0.5, A.is_lt), [("sm", 112, 128)], [("sm", 0, 16)])
+        eqdays(1)
+        v(tt(T.sm[:, 16:24], T.sm[:, 0:8], T.du[:, 0:8], A.mult), [("sm", 0, 16), "du"], [("sm", 16, 48)])
+        scan(0)
+        v(tt(T.sm[:, 64:72], T.sm[:, 16:24], T.sm[:, 112:120], A.max), [("sm", 16, 48), ("sm", 112, 128)], [("sm", 48, 80)])
+        alternate(dayoffsets(8), [])
+        v(lambda a=gxa[0]: V.tensor_copy(T.sd[:, 0:2320].indirect(T.u16s[:, 16:24]), T.gxl[:, a:a + 128]), [("gxl",) + gxa, ("u16s", 16, 32)], ["sd"])
+    copy("Y", T.ys[:], T.sd[:, 1:2049], ["sd"], [])
+    finish([("ls", sent[0])])

@@ -1,27 +1,31 @@
-from concourse.mybir import AluOpType as A, ActivationFunctionType as AF, AxisListType as AX
+from concourse.mybir import AluOpType as A, ActivationFunctionType as AF
 
-FLAG = 262144.0
 BIG = 65536.0
 LOW = -1073741824.0
+TINY = 2.0 ** -110
 RO = 4
 F, B, H, I, U = "float32", "bfloat16", "float16", "int32", "uint16"
+W3A, W2A, GA, W1, DUMP, GB, W2B, W3B, WEND = 0, 1024, 2048, 2833, 3857, 4128, 4912, 5936, 6960
+WIN = (((GA, DUMP, W1), (W2A, GA + 769, W2A), (W3A, GA + 769, W3A)), ((W1 - 1, GB + 769, W1), (GB, W3B, W2B), (GB, WEND, W3B)))
+GH = (GA, GB)
+EW = [16 * (b + 1) for b in range(8)]
+EO = [8 * b * (b + 1) for b in range(9)]
 SB = {
     "anI": (64, I), "ofI": (112, I), "snI": (48, I), "wkb": (2048, B), "xw": (1040, B), "sd": (2320, B),
-    "pI": (3, I), "pp": (3, F), "tc": (8, F), "lmc": (16, F), "n512": (512, I), "kI": (256, I), "m4": (128, I),
-    "id16": (128, H), "idb": (128, B), "idF": (128, F), "jF": (128, F), "j16": (128, H), "upr": (128, B),
-    "one": (128, B), "seven": (128, B), "m1k": (128, B), "gb16": (128, H), "gi16": (8, H), "gib": (8, B), "gik": (8, B), "pm0": (256, F), "pm1": (256, F), "pmg": (128, F),
-    "mk": (256, H), "mkg": (256, H), "lane": (256, B), "ct8": (128, B), "selb": (2048, B), "selF": (2048, F),
-    "ex": (16, U), "exg": (16, U), "ex8": (8, U), "dgt": (6, U), "v1c": (16, F), "smI": (1024, F), "smk": (1024, B), "du": (32, F), "lo16": (512, H),
-    "an1": (64, F), "of16": (112, H), "ofE": (1792, H), "pw": (1800, F), "p2w": (1800, F), "rf16": (1024, H), "w1": (2064, F), "w2": (1800, F), "w3": (1800, F), "t8": (1032, F),
-    "fl": (1024, B), "wd": (1024, F), "p1h": (64, H), "p2h": (64, H), "p3h": (64, H), "l1": (64, U), "l2": (64, U), "l3": (64, U), "sl": (48, U), "cw": (2056, F), "cq": (256, F), "sg": (2048, B),
-    "ldI": (64, I), "lfd": (64, U), "cv": (1032, F), "cmp": (4096, B), "xr": (4096, B), "bz": (120, B), "rz": (24, B), "rkI": (64, I), "loI": (64, I), "hiI": (16, I),
-    "oa": (1024, H), "ob": (128, H), "th": (1088, B), "win": (144, F), "wg": (128, F), "g1": (16, F), "lv": (16, U), "lvf": (16, F), "nb": (8, F), "vld": (16, F),
-    "xg": (272, B), "cg": (256, U), "cgf": (256, F), "dbf": (256, F), "dbi": (264, I), "kb": (128, F), "ka": (128, F), "ks": (112, F), "sm": (128, F), "smi": (64, I), "u16s": (64, U),
-    "rdb": (2, B), "thr": (4, F), "xe": (256, H), "xf": (256, F), "rr": (256, H), "wv": (256, F), "eq": (2048, B), "scn": (2048, B), "gl": (16, U), "dgh": (128, H), "yb": (384, F),
-    "ghs": (2304, F), "ghl": (2304, F), "gxs": (512, B), "gxl": (512, B), "gds": (64, U), "gdl": (64, U),
+    "pI": (3, I), "pp": (3, F), "n144": (144, I), "n512": (512, I), "kI": (256, I), "lmc": (16, F), "pw": (16, F), "cc": (32, F), "col": (24, F), "hi16": (16, F), "tc": (16, F),
+    "tab": (2048, B), "id16": (128, H), "idb": (128, B), "idF": (128, F), "jF": (128, F), "j16": (128, H), "upr": (128, B), "amb": (128, B), "nid": (128, B),
+    "one": (128, B), "seven": (128, B), "m1k": (128, B), "gi16": (8, H), "gin": (8, H), "gib": (8, B), "gik": (16, B), "zp": (864, H), "zd": (144, H), "dec": (16, H),
+    "mk": (256, H), "mkg": (256, H), "lane": (256, B), "segm": (256, B), "ct8": (128, B), "ex": (16, U), "exg": (16, U), "ex8": (8, U), "dgt": (8, U), "v1c": (16, F),
+    "smk": (576, B), "du": (16, F), "duw": (16, H), "lo16": (512, H), "anl": (64, U), "ofl": (112, U), "an1": (128, F),
+    "wb": (WEND, B), "g0": (1024, B), "g1": (1024, B), "t8": (1040, B), "l0": (64, U), "l1": (64, U), "l2": (64, U), "sl": (48, U), "cw": (2056, F), "cq": (256, F), "sg": (2048, B),
+    "ldI": (64, I), "lfd": (64, U), "cv": (1032, F), "cmp": (3072, B), "xr": (3072, B), "sgb": (1024, B), "sgn": (1024, B), "bz": (120, B), "rz": (24, B), "rkI": (64, I), "loI": (64, I), "hiI": (16, I),
+    "oa": (1024, H), "ob": (128, H), "th": (1088, B), "win": (144, F), "wg": (128, F), "g16": (16, F), "lv": (16, U), "lvf": (16, F),
+    "xg": (272, B), "cg": (256, U), "cgf": (256, F), "db": (272, B), "kx": (256, F), "ki": (32, I), "sm": (64, F), "smi": (32, I), "u16s": (64, U),
+    "thr": (2, F), "xe": (256, H), "xf": (256, F), "wv": (256, B), "eq": (1152, B), "scn": (1152, B), "gl": (16, U), "dgh": (128, B), "yb": (1024, F),
+    "ghs": (2304, B), "gxs": (512, B), "gxl": (512, B), "gds": (64, U), "gdl": (64, U),
 }
 SCRATCH = {k: ("sbuf", [128, n], d) for k, (n, d) in SB.items()}
-SCRATCH.update({"ck": ("sbuf", [1, 256], B), "ckg": ("sbuf", [1, 128], B)})
+SCRATCH.update({"ck": ("sbuf", [1, 256], B), "c8": ("sbuf", [1, 128], B)})
 PS = ("pA", "pB", "pC", "pD", "pE", "pF", "pG", "pH")
 SCRATCH.update({k: ("psum", [128, 512], F) for k in PS})
 SEMAPHORES = ["qV", "qS", "qP", "qG", "ls"] + ["d%d" % i for i in range(11)] + ["gh%d" % t for t in range(3)] + ["gx%d" % t for t in range(RO)] + ["gd%d" % t for t in range(RO)]
@@ -98,9 +102,9 @@ def layer(g, T):
     return op, copy, landed, prepare, finish
 
 
-def alternate(a, b):
-    for i in range(max(len(a), len(b))):
-        for c in (a, b):
+def weave(*chains):
+    for i in range(max(len(c) for c in chains)):
+        for c in chains:
             if i < len(c):
                 c[i]()
 
@@ -144,6 +148,9 @@ def rank_program(g, core, T, topo):
     def mm(o, l, r, st=True, sp=True):
         return lambda: P.matmul(o, l, r, st, sp)
 
+    def later(q, f, r, w):
+        return lambda: op(q, f, r, w)
+
     def send(dst, out, in_, reads, sem):
         d = cores[dst]
         prepare("G", reads, [])
@@ -157,6 +164,12 @@ def rank_program(g, core, T, topo):
         else:
             op("G", lambda: g.iota(view, pat, base, ch), [], [name])
 
+    def col(i):
+        return T.col[:, i:i + 1]
+
+    def lm(i):
+        return T.lmc[:, i:i + 1]
+
     v([ms(T.xw[:, 0:1], LOW), ms(T.sd[:, 0:1], 0.0)], [], [("xw", 0, 16), ("sd", 0, 16)])
     copy("Y", T.anI[:], T.an0[:], [], ["anI"])
     copy("Y", T.ofI[:], T.of0[:], [], ["ofI"])
@@ -165,55 +178,92 @@ def rank_program(g, core, T, topo):
     copy("Y", T.xw[:, 1:1025], T.x[:], [], [("xw", 1, 1025)])
     copy("Y", T.snI[:], T.snd[:], [], ["snI"])
     iota("pI", T.pI[:, 0:1], [[0, 1]], 0, 1)
+    iota("n144", T.n144[:], [[1, 144]], 0, 0)
     iota("n512", T.n512[:], [[1, 512]], 0, 0)
     iota("v1c", T.v1c[:, 0:8], [[128, 8]], 1, 1, True)
-    iota(("pw", 1025, 1794), T.pw[:, 1025:1794], [[0, 769]], 1793, 0, True)
-    iota(("p2w", 1025, 1794), T.p2w[:, 1025:1794], [[0, 769]], 1793, 0, True)
     iota("ct8", T.ct8[:], [[0, 16], [1, 8]], -256, 0, True)
-    iota("ck", T.ck[:], [[-4096, 16], [0, 16]], 61440, 0, True)
-    iota("ckg", T.ckg[:], [[-4096, 16], [0, 8]], 61440, 0, True)
-    iota("du", T.du[:, 0:16], [[16, 16]], 2056, 0, True)
-    iota("smI", T.smI[:], [[16, 8], [1, 128]], -127, 0, True)
+    iota("ck", T.ck[:], [[0, 16], [-2048, 16]], 30720, 0, True)
+    iota("du", T.du[:], [[16, 16]], 2056, 0, True)
 
     P15, P4, PC = T.pp[:, 0:1], T.pp[:, 1:2], T.pp[:, 2:3]
-    N1, G8, K1 = T.n512[:, 0:128], T.n512[:, 0:8], T.kI[:, 0:128]
-    v(ms(T.one[:], 1.0), [], ["one"])
+    N1, G8, N16, K1 = T.n144[:, 0:128], T.n144[:, 0:8], T.n144[:, 0:16], T.kI[:, 0:128]
+    ZC, MB, MP, BP, RB, WL, WD, DB = (col(i) for i in range(8))
     v([ts(T.pI[:, 1:2], T.pI[:, 0:1], 15, A.bitwise_and), ts(T.pI[:, 2:3], T.pI[:, 0:1], 4, A.arith_shift_right)], ["pI"], ["pI2"])
+    v([ms(T.pw[:, b:b + 1], float(1 << b)) for b in range(5)] + [ms(T.tab[:, 0:1], 0.0), ms(T.hi16[:, 0:1], 0.0)], [], ["pw", ("tab", 0, 1), ("hi16", 0, 1)])
     v([tc(P15, T.pI[:, 1:2]), tc(P4, T.pI[:, 2:3]), tc(PC, T.pI[:, 0:1])], ["pI", "pI2"], ["pp"])
-    v([ts(T.lmc[:], T.n512[:, 0:16], P15, A.is_equal), ts(T.m4[:], N1, 4, A.arith_shift_right), ts(T.kI[:], T.n512[:, 0:256], 15, A.bitwise_and)], ["n512", "pp"], ["lmc", "m4", "kI"])
-    v([ts(T.idb[:], N1, PC, A.is_equal), ts(T.id16[:], N1, PC, A.is_equal), ts(T.idF[:], N1, PC, A.is_equal)], ["n512", "pp"], ["idb", "id16", "idF"])
-    s([act(T.selb[:, 128 * k:128 * k + 128], T.idb[:], AF.Copy, 0.0, T.lmc[:, k:k + 1]) for k in range(16)], ["idb", "lmc"], ["selb"])
-    v(ts(T.an1[:], T.anI[:], 1.0, A.add), ["anI"], ["an1"])
-    v([ts(T.gb16[:], T.m4[:], P4, A.is_equal), tc(T.l1[:], T.an1[:])], ["m4", "pp", "an1"], ["gb16", "l1"])
-    v([ms(T.pw[:, 0:1], 1793.0), ms(T.p2w[:, 0:1], 1793.0)], [], [("pw", 0, 1), ("p2w", 0, 1)])
-    v([ts(T.rf16[:, k::16], T.an1[:], T.lmc[:, k:k + 1], A.mult) for k in range(16)], ["an1", "lmc"], ["rf16"])
-    p([mm(T.pG[:], T.gb16[:], T.rf16[:, 0:512]), mm(T.pH[:], T.gb16[:], T.rf16[:, 512:1024])], ["gb16", "rf16"], ["pG", "pH"])
-    s(act(T.pw[:, 1:513], T.pG[:]), ["pG"], [("pw", 1, 513)])
-    s(act(T.pw[:, 513:1025], T.pH[:]), ["pH"], [("pw", 513, 1025)])
-    v(tc(T.of16[:], T.ofI[:]), ["ofI"], ["of16"])
-    v([ts(T.ofE[:, k::16], T.of16[:], T.lmc[:, k:k + 1], A.mult) for k in range(16)], ["of16", "lmc"], ["ofE"])
-    OFB = [(bank, 512 * b, min(512 * b + 512, 1792)) for b, bank in enumerate(("pA", "pB", "pC", "pD"))]
-    for bank, lo, hi in OFB:
-        p(mm(T[bank][:, 0:hi - lo], T.gb16[:], T.ofE[:, lo:hi]), ["gb16", "ofE"], [bank])
-    for bank, lo, hi in OFB[:2]:
-        s(act(T.wd[:, lo:hi], T[bank][:]), [bank], [("wd", lo, hi)])
-    for bank, lo, hi in OFB:
-        s(act(T.w1[:, lo + 1:hi + 1], T[bank][:, 0:hi - lo]), [bank], [("w1", lo + 1, hi + 1)])
-    v(lambda: V.tensor_copy(T.p2w[:, 1:1025], T.pw[:, 0:1794].indirect(T.l1[:])), ["pw", "l1"], [("p2w", 1, 1025)])
-    v(tc(T.rf16[:], T.p2w[:, 1:1025]), ["p2w"], ["rf16"])
+    v(ts(T.lmc[:], N16, P15, A.is_equal), ["n144", "pp"], ["lmc"])
+    v([ts(T.pw[:, 5:10], T.pw[:, 0:5], 32.0, A.mult), ms(T.pw[:, 10:11], 1024.0)], ["pw"], ["pw2"])
+    v([ts(T.cc[:, 16:21], T.pw[:, 0:5], lm(11), A.mult), ts(T.cc[:, 21:26], T.pw[:, 0:5], lm(12), A.mult), tc(T.cc[:, 26:27], lm(13))], ["pw", "lmc"], [("cc", 16, 32)])
+    v([ts(MB, P15, 11.0, A.is_lt), ts(MP, P15, 11.0, A.is_ge), ts(ZC, P4, 16.0, A.mult, 15.0, A.add),
+       ts(WL, lm(12), 32.0, A.mult, lm(11), A.add), ts(WD, lm(12), 24.0, A.mult, lm(13), A.add)], ["pp", "lmc"], ["col"])
+    v(tt(T.cc[:, 0:11], T.cc[:, 16:27], T.lmc[:, 0:11], A.add), [("cc", 16, 32), "lmc"], [("cc", 0, 16)])
 
-    def conv(src, name, c0, cols, sel, bank, extra=None):
-        o = T[bank][:, 0:cols]
-        fs = [mm(o, T[sel][:, 128 * k:128 * k + 128], src[:, c0 + k:c0 + 16 * cols:16], k == 0, k == 15 and extra is None) for k in range(16)]
-        if extra is not None:
-            fs.append(mm(o, T.id16[:], T[extra][:], False, True))
-        p(fs, [(name, c0, c0 + 16 * cols), sel, "id16"] + ([extra] if extra else []), [bank])
+    def double(name, first, n):
+        return [later("V", ts(T[name][:, 1 << b:2 << b], T[name][:, 0:1 << b], T.cc[:, first + b:first + b + 1], A.add), [(name, 0, 1 << b), ("cc", 0, 16)], [(name, 1 << b, 2 << b)]) for b in range(n)]
 
-    conv(T.rf16, "rf16", 0, 64, "selb", "pF")
-    v([ts(T.seven[:], N1, PC, A.is_equal, 7.0, A.mult), ts(T.m1k[:], N1, PC, A.is_equal, -1024.0, A.mult), ts(T.lo16[:], T.n512[:], 1.0, A.add)], ["n512", "pp"], ["seven", "m1k", "lo16"])
+    more = [
+        later("V", [ts(BP, MP, 65.0, A.mult, -1.0, A.add), ts(RB, MP, 64.0, A.mult, WD, A.add)], ["col"], ["col"]),
+        later("V", [ts(T.idb[:], N1, PC, A.is_equal), ts(T.amb[:], N1, PC, A.is_equal, MB, A.mult)], ["n144", "pp", "col"], ["idb", "amb"]),
+        later("V", [ts(col(8 + 3 * a + l), lm(13), float(GH[a] - WIN[a][l][2]), A.mult, WL, A.add) for a in (0, 1) for l in range(3)], ["lmc", "col"], ["col2"])]
+    weave(double("tab", 0, 7), double("hi16", 7, 4) + more)
+    v([tc(T.anl[:], T.anI[:]), tc(T.ofl[:], T.ofI[:])], ["anI", "ofI"], ["anl", "ofl"])
+    s([act(T.tab[:, 128 * a:128 * a + 128], T.tab[:, 0:128], AF.Identity, T.hi16[:, a:a + 1]) for a in range(11, 16)], [("tab", 0, 128), "hi16"], [("tab", 1408, 2048)])
+    v([ts(T.tab[:, 128 * a:128 * a + 128], T.tab[:, 0:128], T.hi16[:, a:a + 1], A.add) for a in range(1, 11)], [("tab", 0, 128), "hi16"], [("tab", 128, 1408)])
+    for h in (0, 1):
+        s(act(T.g1[:, 512 * h:512 * h + 512], T.tab[:].indirect(T.anl[:, 32 * h:32 * h + 32]), AF.Identity, BP, MP), ["tab", "anl", "col"], [("g1", 512 * h, 512 * h + 512)])
+    v(ts(T.wb[:, GA:GA + 384], T.tab[:].indirect(T.ofl[:, 64:88]), MB, A.mult, RB, A.add), ["tab", "ofl", "col"], [("wb", GA, GA + 384)])
+    s(act(T.wb[:, GA + 384:GA + 768], T.tab[:].indirect(T.ofl[:, 88:112]), AF.Identity, RB, MB), ["tab", "ofl", "col"], [("wb", GA + 384, GA + 768)])
+    v(ts(T.an1[:, 0:64], T.anI[:], 1024.0, A.is_ge, float(GA - W1 - 1024), A.mult), ["anI"], [("an1", 0, 64)])
+    pads = [(GA + 769, W1), (DUMP, GB), (GB + 769, W2B)]
+    v([ms(T.wb[:, a:b], 0.0) for a, b in pads] + [tc(T.wb[:, a + 768:a + 769], RB) for a in GH], ["col"], [("wb",) + a for a in pads] + [("wb", a + 768, a + 769) for a in GH])
+    v(tt(T.an1[:, 64:128], T.an1[:, 0:64], T.anI[:], A.add), [("an1", 0, 64), "anI"], [("an1", 64, 128)])
+    v(tt(T.wb[:, W1:W1 + 512], T.tab[:].indirect(T.ofl[:, 0:32]), T.g1[:, 0:512], A.max), ["tab", "ofl", ("g1", 0, 512)], [("wb", W1, W1 + 512)])
+    v(ts(T.l0[:], T.an1[:, 64:128], float(W1 - GA), A.add), [("an1", 64, 128)], ["l0"])
+    v(tt(T.wb[:, W1 + 512:DUMP], T.tab[:].indirect(T.ofl[:, 32:64]), T.g1[:, 512:1024], A.max), ["tab", "ofl", ("g1", 512, 1024)], [("wb", W1 + 512, DUMP)])
+
+    BK = ("pE", "pF")
+
+    def conv(o, bank, src, name, c0, cols, z, z0, st=True, sp=True):
+        p([mm(o, T[z][:, z0 + 15 - k:z0 + 143 - k], src[:, c0 + k:c0 + 16 * cols:16], st and k == 0, sp and k == 15) for k in range(16)], [(name, c0, c0 + 16 * cols), z], [bank])
+
+    def pointers(a, l, src, name, c0):
+        conv(T.pG[:, 0:64], "pG", src, name, c0, 64, "zp", 144 * (3 * a + l))
+
+    def pointers2(a, l):
+        lo, hi, f = WIN[a][l]
+        v(ts(T["l%d" % l][:], T.pG[:, 0:64], float(f - lo - 64 * (33 + GH[a] - f)), A.add), ["pG"], ["l%d" % l])
+
+    def own(a, l):
+        f = WIN[a][l][2]
+        for h in (0, 1):
+            p(mm(T[BK[h]][:], T.amb[:], T.wb[:, f + 512 * h:f + 512 * h + 512], True, False), ["amb", ("wb", f + 512 * h, f + 512 * h + 512)], [BK[h]])
+        if l == 2:
+            conv(T.pG[:, 0:64], "pG", T.wb, "wb", f, 64, "zd", 0, True, False)
+
+    def jump(a, l, h, q="S"):
+        lo, hi, f = WIN[a][l]
+        gn, c = "g%d" % (l % 2), 512 * h
+        op(q, (act if q == "S" else tc)(T[gn][:, c:c + 512], T.wb[:, lo:hi].indirect(T["l%d" % l][:, 32 * h:32 * h + 32])), [("wb", lo, hi), "l%d" % l], [(gn, c, c + 512)])
+        p(mm(T[BK[h]][:], T["amb" if l == 2 else "idb"][:], T[gn][:, c:c + 512], False, True), ["amb", "idb", (gn, c, c + 512)], [BK[h]])
+
+    def after(a, l):
+        if l < 2:
+            pointers(a, l + 1, T["g%d" % (l % 2)], "g%d" % (l % 2), 0)
+        else:
+            conv(T.pG[:, 0:64], "pG", T.g0, "g0", 0, 64, "zd", 0, False, True)
+
+    def sums(a, l, h, q="S"):
+        c = 512 * h
+        if l < 2:
+            f = WIN[a][l + 1][2] + c
+            op(q, (act if q == "S" else tc)(T.wb[:, f:f + 512], T[BK[h]][:]), [BK[h]], [("wb", f, f + 512)])
+        elif q == "S":
+            s(act(T.t8[:, 1 + c:513 + c], T[BK[h]][:], AF.Identity, RB), [BK[h], "col"], [("t8", 1 + c, 513 + c)])
+        else:
+            v(ts(T.t8[:, 1 + c:513 + c], T[BK[h]][:], RB, A.add), [BK[h], "col"], [("t8", 1 + c, 513 + c)])
 
     def weeks(b, second):
-        bank, c = ("pE", "pH", "pA", "pB")[b], 512 * b
+        bank, c = PS[b], 512 * b
         f = [mm(T[bank][:], T.seven[:], T.wkb[:, c:c + 512], True, False), mm(T[bank][:], T.id16[:], T.lo16[:], False, not second)]
         if second:
             f.append(mm(T[bank][:], T.m1k[:], T.sg[:, c:c + 512], False, True))
@@ -222,266 +272,289 @@ def rank_program(g, core, T, topo):
             s(act(T.cw[:, 1 + c:513 + c], T[bank][:], AF.Copy, c - 1024.0), [bank], [("cw", 1 + c, 513 + c)])
         else:
             s(act(T.sg[:, c:c + 512], T[bank][:], AF.Sign, c - 2048.5), [bank], [("sg", c, c + 512)])
-            if b > 1:
-                s(act(T.sg[:, c:c + 512], T.sg[:, c:c + 512], AF.Copy, c - 1024.0, -1024.0), [("sg", c, c + 512)], [("sg", c, c + 512)])
 
-    zs = [("w1", 1793, 2064), ("w1", 0, 1), ("w2", 1793, 1794), ("w2", 0, 1), ("w3", 1793, 1794), ("w3", 0, 1), ("t8", 0, 1)]
-    v([ms(T[n][:, a:b], 0.0) for n, a, b in zs] + [ms(T.dbi[:, 0:1], 0), ms(T.cv[:, 0:1], 1.0), ms(T.cw[:, 0:1], 1.0), ms(T.xg[:, 0:1], LOW)], [],
-      zs + [("dbi", 0, 1), ("cv", 0, 1), ("cw", 0, 1), ("xg", 0, 1)])
-    for n in ("w2", "w3"):
-        s(act(T[n][:, 1025:1537], T.pC[:]), ["pC"], [(n, 1025, 1537)])
-        s(act(T[n][:, 1537:1793], T.pD[:, 0:256]), ["pD"], [(n, 1537, 1793)])
-    W = ("w1", "w2", "w3")
-    PH = ("p1h", "p2h", "p3h")
-    LL = ("l1", "l2", "l3")
+    def zed(i):
+        return ts(T.zp[:, 144 * i:144 * i + 143], T.n144[:, 0:143], ZC, A.is_equal, col(8 + i), A.mult)
 
-    def addend(l):
-        for h in (0, 1):
-            a = 512 * h
-            s(act(T.wd[:, a:a + 512], T[W[l]][:, 1 + a:513 + a]), [(W[l], 1 + a, 513 + a)], [("wd", a, a + 512)])
+    fill = [[
+        later("V", [zed(1), zed(2), tt(T.cc[:, 16:27], T.pw[:, 0:11], T.lmc[:, 0:11], A.mult)], ["n144", "col", "col2", "pw", "pw2", "lmc"], ["zp", ("cc", 16, 32)]),
+        later("V", [ts(T.seven[:], N1, PC, A.is_equal, 7.0, A.mult), ts(T.m1k[:], N1, PC, A.is_equal, -1024.0, A.mult), ts(T.id16[:], N1, PC, A.is_equal), ts(T.lo16[:], T.n512[:], 1.0, A.add)],
+              ["n144", "n512", "pp"], ["seven", "m1k", "id16", "lo16"]),
+    ], [
+        later("V", lambda: V.tensor_tensor_scan(T.cc[:, 0:11], T.cc[:, 16:27], T.cc[:, 16:27], 0.0, A.max, A.max), [("cc", 16, 32)], [("cc", 0, 16)]),
+        later("V", [ms(T.one[:], 1.0), ms(T.t8[:, 0:1], 0.0), ms(T.db[:, 0:1], 0.0), ms(T.cv[:, 0:1], 1.0), ms(T.cw[:, 0:1], 1.0), ms(T.xg[:, 0:1], LOW)], [],
+              ["one", ("t8", 0, 1), ("db", 0, 1), ("cv", 0, 1), ("cw", 0, 1), ("xg", 0, 1)]),
+        later("V", ts(T.zd[:, 0:143], T.n144[:, 0:143], ZC, A.is_equal, T.cc[:, 10:11], A.mult), ["n144", "col", ("cc", 0, 16)], ["zd"]),
+        later("V", [ts(T.cq[:, 0:128], N1, PC, A.is_equal, -4096.0, A.mult), ts(T.cq[:, 128:256], N1, PC, A.is_gt), ts(T.gib[:], G8, P4, A.is_equal)], ["n144", "pp"], ["cq", "gib"]),
+    ], [
+        later("V", tt(T.upr[:], T.cq[:, 0:128], T.cq[:, 128:256], A.add), ["cq"], ["upr"]),
+        later("V", [ms(T.bz[:, 0:56], 0.0), ts(T.tc[:, 5:6], P4, 17.0, A.mult, P15, A.add), ts(T.v1c[:, 8:16], T.v1c[:, 0:8], 0.5, A.mult), ts(T.sl[:], T.snI[:], 1.0, A.add)],
+              ["pp", "v1c", "snI"], [("bz", 0, 56), "tcd", "v1h", "sl"]),
+        later("V", [tc(T.dgt[:, 0:1], T.tc[:, 5:6]), ts(T.dgt[:, 2:3], T.tc[:, 5:6], 1.0, A.add)], ["tcd"], ["dgl"]),
+    ]]
+    for l in range(3):
+        if l == 0:
+            fill[0][0]()
+        own(0, l)
+        jump(0, l, 0, "V")
+        jump(0, l, 1, "S")
+        after(0, l)
+        for f in fill[l][(1 if l == 0 else 0):]:
+            f()
+        if l < 2:
+            sums(0, l, 0, "V")
+            sums(0, l, 1, "S")
+            pointers2(0, l + 1)
+            weeks(2 * l, False)
+            weeks(2 * l + 1, False)
 
-    def jump(l, halves=(0, 1)):
-        nm = "t8" if l == 2 else W[l + 1]
-        for h in halves:
-            a = 512 * h
-            v(tt(T[nm][:, a + 1:a + 513], T[W[l]][:, 0:1794].indirect(T[LL[l]][:, 32 * h:32 * h + 32]), T.wd[:, a:a + 512], A.add),
-              [(W[l], 0, 1794), LL[l], ("wd", a, a + 512)], [(nm, a + 1, a + 513)])
-
-    def jumplist(l):
-        for h in (0, 1):
-            a = 512 * h
-            s(act(T.fl[:, a:a + 512], T[W[l]][:, 1 + a:513 + a], AF.Relu, -2048.0, 0.015625), [(W[l], 1 + a, 513 + a)], [("fl", a, a + 512)])
-        conv(T.fl, "fl", 0, 64, "selb", "pF", PH[l])
-        addend(l)
-
-    def jumplist2(l):
-        v(ts(T[LL[l]][:], T.pF[:, 0:64], 1793.0, A.min), ["pF"], [LL[l]])
-
-    s([act(T.selF[:, 128 * k:128 * k + 128], T.idF[:], AF.Copy, 0.0, T.lmc[:, k:k + 1]) for k in range(16)], ["idF", "lmc"], ["selF"])
-    weeks(0, False)
-    weeks(1, False)
-    v(tc(T.l2[:], T.pF[:, 0:64]), ["pF"], ["l2"])
-    v(tc(T.p2h[:], T.pF[:, 0:64]), ["pF"], ["p2h"])
-    v(lambda: V.tensor_copy(T.rf16[:], T.p2w[:, 0:1794].indirect(T.l2[:])), ["p2w", "l2"], ["rf16"])
-    conv(T.rf16, "rf16", 0, 64, "selb", "pF")
-    jump(0)
-    addend(1)
-    jump(1)
-    addend(2)
-    weeks(2, False)
-    weeks(3, False)
-    weeks(0, True)
-    weeks(1, True)
-    v(tc(T.l3[:], T.pF[:, 0:64]), ["pF"], ["l3"])
-    v([tc(T.p3h[:], T.pF[:, 0:64]), tc(T.p1h[:], T.an1[:])], ["pF", "an1"], ["p3h", "p1h"])
-    jump(2)
-    conv(T.t8, "t8", 1, 64, "selF", "pG")
-    v(ts(T.sl[:], T.snI[:], 1.0, A.add), ["snI"], ["sl"])
-    for bank, c in (("pA", 1024), ("pB", 1536)):
-        v(tt(T.cw[:, 1 + c:513 + c], T[bank][:], T.sg[:, c:c + 512], A.add), [bank, ("sg", c, c + 512)], [("cw", 1 + c, 513 + c)])
-    v([ts(T.gib[:], G8, P4, A.is_equal), ts(T.gi16[:], G8, P4, A.is_equal), ts(T.gik[:], G8, P4, A.is_equal, BIG, A.mult)], ["n512", "pp"], ["gib", "gi16", "gik"])
-    v([ts(T.cq[:, 0:128], N1, PC, A.is_equal, -4096.0, A.mult), ts(T.cq[:, 128:256], N1, PC, A.is_gt)], ["n512", "pp"], ["cq"])
-    v(tt(T.upr[:], T.cq[:, 0:128], T.cq[:, 128:256], A.add), ["cq"], ["upr"])
-    v([ms(T.bz[:, 0:56], 0.0), ms(T.rz[:, 0:8], 0.0), ms(T.wg[:, 64:128], 0.0)], [], [("bz", 0, 56), ("rz", 0, 8), ("wg", 64, 128)])
-    v([ts(T.tc[:, 5:6], P4, 17.0, A.mult), ts(T.v1c[:, 8:16], T.v1c[:, 0:8], 0.5, A.mult)], ["pp", "v1c"], ["tcd", "v1c"])
-    v(tt(T.tc[:, 7:8], T.tc[:, 5:6], P15, A.add), ["tcd", "pp"], ["tce"])
-    v([tc(T.dgt[:, 0:1], T.tc[:, 7:8]), ts(T.dgt[:, 2:3], T.tc[:, 7:8], 1.0, A.add), tc(T.ex[:], T.n512[:, 0:16])], ["tce", "n512"], ["dgl", "ex"])
+    def constants1():
+        v([ts(T.kI[:], T.n512[:, 0:256], 15, A.bitwise_and), ts(T.idF[:], N1, PC, A.is_equal), ts(T.nid[:], N1, PC, A.is_equal, -1.0, A.mult),
+           ts(T.gik[:, 0:8], G8, P4, A.is_equal, BIG, A.mult), ts(T.gik[:, 8:16], G8, P4, A.is_equal, BIG / 2, A.mult), ms(T.c8[:], 8 * BIG), ms(T.thr[:, 0:1], 9.0 * BIG)],
+          ["n144", "n512", "pp"], ["kI", "idF", "nid", "gik", "c8", ("thr", 0, 1)])
+        v(ts(T.segm[:], T.kI[:], 0.5, A.is_ge), ["kI"], ["segm"])
 
     def constants2():
-        v([tc(T.lane[:], T.kI[:]), ts(T.mk[:], T.kI[:], P15, A.is_equal), ts(T.mkg[:, 0:128], K1, 0.0, A.is_ge), ts(T.mkg[:, 128:256], K1, P15, A.is_equal)], ["kI", "pp"], ["lane", "mk", "mkg"])
-        v([ts(T.tc[:, 0:1], P15, 16.0, A.mult), ts(T.tc[:, 1:2], P15, 8.0, A.mult), ts(T.tc[:, 3:4], P4, 8.0, A.mult), ts(T.tc[:, 2:3], P15, 8.0, A.is_ge),
-           ts(T.smi[:, 0:16], T.n512[:, 0:16], 7, A.bitwise_and)], ["pp", "n512"], ["tc", "smi"])
-        v([tt(T.sm[:, 0:1], T.tc[:, 0:1], P4, A.add), tt(T.sm[:, 1:2], T.tc[:, 1:2], P4, A.add), tt(T.sm[:, 3:4], T.tc[:, 3:4], P15, A.add)], ["tc", "pp"], ["sm"])
-        v([ts(T.sm[:, 2:3], T.sm[:, 0:1], 8.0, A.add), tc(T.dgt[:, 4:5], T.sm[:, 3:4])], ["sm"], ["dg8", "sm2"])
-        v([ts(T.pm0[:], T.n512[:, 0:256], T.sm[:, 0:1], A.is_equal), ts(T.pm1[:], T.n512[:, 0:256], T.sm[:, 2:3], A.is_equal), ts(T.pmg[:], N1, T.sm[:, 1:2], A.is_equal)],
-          ["n512", "sm", "sm2"], ["pm0", "pm1", "pmg"])
-        v([ts(T.j16[:], N1, PC, A.add, 127.0, A.is_equal), ts(T.jF[:], N1, PC, A.add, 127.0, A.is_equal), tc(T.exg[:], T.smi[:, 0:16]), ts(T.ex8[:], G8, 2.0, A.mult, T.tc[:, 2:3], A.add),
-           ts(T.du[:, 0:16], T.du[:, 0:16], P15, A.add)], ["n512", "pp", "smi", "tc", "du"], ["j16", "jF", "exg", "ex8", "du"])
-        v(ts(T.du[:, 16:32], T.du[:, 0:16], -256.0, A.add), ["du"], ["du"])
-        v(ms(T.thr[:, 0:1], 9.0 * BIG), [], ["thr"])
+        v([tc(T.lane[:], T.kI[:]), ts(T.mk[:], T.kI[:], P15, A.is_equal), ts(T.mkg[:, 0:128], K1, 0.0, A.is_ge), ts(T.mkg[:, 128:256], K1, P15, A.is_equal),
+           ts(T.gi16[:], G8, P4, A.is_equal), ts(T.gin[:], G8, P4, A.is_equal, -4096.0, A.mult), tc(T.ex[:], N16), ms(T.rz[:, 0:8], 0.0), ms(T.wg[:, 64:128], 0.0)],
+          ["kI", "pp", "n144"], ["lane", "mk", "mkg", "gi16", "gin", "ex", ("rz", 0, 8), ("wg", 64, 128)])
+        v([ts(T.tc[:, 3:4], P4, 8.0, A.mult, P15, A.add), ts(T.tc[:, 2:3], P15, 8.0, A.is_ge), ts(T.smi[:, 0:16], N16, 7, A.bitwise_and), ts(T.smi[:, 16:17], T.pI[:, 0:1], 7, A.bitwise_and),
+           ts(T.j16[:], N1, PC, A.add, 127.0, A.is_equal), ts(T.jF[:], N1, PC, A.add, 127.0, A.is_equal), ms(T.smk[:], 1.0), ts(T.du[:], T.du[:], P15, A.add)],
+          ["pp", "n144", "pI", "du"], ["tc", "smi", "j16", "jF", "smk", "du"])
+        v([tc(T.dgt[:, 4:5], T.tc[:, 3:4]), tc(T.exg[:], T.smi[:, 0:16]), ts(T.ex8[:], G8, 2.0, A.mult, T.tc[:, 2:3], A.add), ts(T.duw[:], T.du[:], float(DUMP - W1 + 1 - 2056), A.add),
+           ts(T.tc[:, 6:7], T.smi[:, 16:17], 1.0, A.add), ts(T.tc[:, 7:8], T.smi[:, 16:17], 2.0, A.add, 8.0, A.mult), ts(T.tc[:, 8:9], T.tc[:, 2:3], float(EO[8]), A.mult, -1.0, A.add)] +
+          [ts(T.smk[:, EO[b]:EO[b] + 16], N16, P15, A.add, 15.0, A.is_gt) for b in range(8)], ["tc", "smi", "n144", "pp", "du", "smk"], ["dg8", "exg", "ex8", "duw", "tc2", "smk"])
+        v([ts(T.dgt[:, 6:7], T.tc[:, 6:7], T.tc[:, 7:8], A.mult, T.tc[:, 8:9], A.add), zed(0), zed(3), zed(4), zed(5),
+           ts(T.dec[:, 0:8], G8, P4, A.is_equal, col(9), A.mult), ts(T.dec[:, 8:16], G8, P4, A.is_equal, T.cc[:, 10:11], A.mult), ts(DB, PC, 8.0, A.is_lt, -64.0 * 1057, A.mult)],
+          ["tc2", "n144", "col", "col2", "pp", ("cc", 0, 16)], ["pick", "zp", "dec", "dcb"])
 
-    DUS, DUW = T.du[:, 0:16], T.du[:, 16:32]
+    def keys(w, t):
+        p(mm(T.pD[:, 0:16 * w], T.one[0:1, :], T.ck[:, 0:16 * w], False, True), ["one", "ck"], ["pD"])
+        v(lambda: V.tensor_tensor_scan(T.kx[:, 0:16 * w], T.segm[:, 0:16 * w], T.pD[:, 0:16 * w], 0.0, A.mult, A.max), ["segm", "pD"], ["kx"])
 
-    def tree(w):
-        v(tc(T.kb[:, 0:8 * w], T.pD[:, 8 * w:16 * w]), ["pD"], ["kb"])
-        v(tt(T.ka[:, 0:8 * w], T.pD[:, 0:8 * w], T.kb[:, 0:8 * w], A.max), ["pD", "kb"], ["ka"])
-        v(tt(T.kb[:, 0:4 * w], T.ka[:, 0:4 * w], T.ka[:, 4 * w:8 * w], A.max), ["ka"], ["kb"])
-        v(tt(T.ka[:, 0:2 * w], T.kb[:, 0:2 * w], T.kb[:, 2 * w:4 * w], A.max), ["kb"], ["ka"])
-        v(tt(T.ks[:, 0:w], T.ka[:, 0:w], T.ka[:, w:2 * w], A.max), ["ka"], [("ks", 0, 16)])
-        v([ts(T.ks[:, 16:16 + w], T.ks[:, 0:w], T.thr[:, 0:1], A.is_ge), tc(T.smi[:, 0:w], T.ks[:, 0:w])], [("ks", 0, 16), "thr"], [("ks", 16, 32), ("smi", 0, 16)])
+    def excess(w, t):
+        return ts(T.ki[:, 0:w], T.kx[:, 15:16 * w:16], T.thr[:, t % 2:t % 2 + 1], A.subtract, 0.0, A.max)
 
     def chosen(w):
-        v(ts(T.smi[:, 16:16 + w], T.smi[:, 0:w], 4095, A.bitwise_and), [("smi", 0, 16)], [("smi", 16, 32)])
-        v(tt(T.ks[:, 48:48 + w], T.smi[:, 16:16 + w], T.ks[:, 16:16 + w], A.mult), [("smi", 16, 32), ("ks", 16, 32)], [("ks", 48, 64)])
+        v(ts(T.ki[:, 16:16 + w], T.ki[:, 0:w], 4095, A.bitwise_and), [("ki", 0, 16)], [("ki", 16, 32)])
 
-    def eqdays(nh):
-        for h in range(nh):
-            v([ts(T.eq[:, b * 128:b * 128 + 128], T.rr[:, 128 * h:128 * h + 128], T.sm[:, 112 + b:113 + b], A.is_equal) for b in range(8 * h, 8 * h + 8)],
-              ["rr", ("sm", 112, 128)], [("eq", 1024 * h, 1024 * h + 1024)])
+    def eqdays(h):
+        o = EO[8] * h
+        v([ts(T.eq[:, o + EO[b]:o + EO[b + 1]], T.pH[:, 128 * h + 128 - EW[b]:128 * h + 128], T.pA[:, 8 * h + b:8 * h + b + 1], A.is_equal) for b in range(8)], ["pH", "pA"], [("eq", o, o + EO[8])])
 
     def scan(h):
-        a = slice(1024 * h, 1024 * h + 1024)
+        a = slice(EO[8] * h, EO[8] * h + EO[8])
         v(lambda: V.tensor_tensor_scan(T.scn[:, a], T.eq[:, a], T.smk[:], 0.0, A.max, A.mult), [("eq", a.start, a.stop), "smk"], [("scn", a.start, a.stop)])
 
     def dayoffsets(w):
         return [
-            lambda: v(tt(T.sm[:, 80:80 + w], T.scn[:, 127:128 * w:128], T.du[:, 0:w], A.mult), ["scn", "du"], [("sm", 80, 96)]),
-            lambda: v(tt(T.sm[:, 96:96 + w], T.sm[:, 64:64 + w], T.sm[:, 80:80 + w], A.max), [("sm", 64, 96)], [("sm", 96, 112)]),
-            lambda: v(tc(T.u16s[:, 16:16 + w], T.sm[:, 96:96 + w]), [("sm", 96, 112)], [("u16s", 16, 32)])]
+            later("V", tt(T.sm[:, 0:16], T.scn[:].indirect(T.dgt[:, 6:7]), T.du[:], A.mult), ["scn", "pick", "du"], [("sm", 0, 16)]),
+            later("V", tt(T.sm[:, 16:16 + w], T.sm[:, 0:w], T.pA[:, 0:w], A.max), [("sm", 0, 16), "pA"], [("sm", 16, 32)]),
+            later("V", tc(T.u16s[:, 16:16 + w], T.sm[:, 16:16 + w]), [("sm", 16, 32)], [("u16s", 16, 32)])]
 
     def copies(q, src, sname, so, dst, n, ks):
         f = act if q == "S" else tc
-        op(q, [f(T.xr[:, dst + k:dst + 16 * n:16], src[:, so:so + n]) for k in ks], [(sname, so, so + n)], [("xr" + q, dst, dst + 1)])
+        op(q, [f(T.xr[:, dst + k:dst + 16 * n:16], src[:, so:so + n]) for k in ks], [(sname, so, so + n)], [("xr" + q, dst, dst + 16 * n)])
+
+    def compare(c0, n):
+        a = slice(16 * c0, 16 * c0 + 16 * n)
+        v(tt(T.cmp[:, a], T.sd[:, 0:2049].indirect(T.cg[:, c0:c0 + n]), T.xr[:, a], A.is_lt), [("sd", 0, 2049), "cg", ("xrS", a.start, a.stop), ("xrV", a.start, a.stop)], [("cmp", a.start, a.stop)])
+
+    def count(c0, n, stop=False):
+        o = 128 * (c0 // 128)
+        p([mm(T.pD[c0 % 128:c0 % 128 + n, o + k:o + 128:16], T.cmp[:, 16 * c0 + k:16 * c0 + 16 * n:16], T.gik[:, 0:8], False, stop and k == 15) for k in range(16)],
+          [("cmp", 16 * c0, 16 * c0 + 16 * n), "gik"], ["pD"])
+
+    def fetch(c0):
+        s(act(T.sgb[:], T.sd[:, 0:2049].indirect(T.cg[:, c0:c0 + 64])), [("sd", 0, 2049), "cg"], ["sgb"])
+
+    def differ(src, sname, so):
+        for h in (0, 1):
+            p([f for k in range(8) for f in (mm(T[BK[h]][:, 64 * k:64 * k + 64], T.idb[:], src[:, so:so + 64], True, False),
+                                              mm(T[BK[h]][:, 64 * k:64 * k + 64], T.nid[:], T.sgb[:, 8 * h + k:1024:16], False, True))], [(sname, so, so + 64), "sgb", "idb", "nid"], [BK[h]])
+
+    def signs(c0, stop=False):
+        o = 128 * (c0 // 128)
+        for h in (0, 1):
+            s(act(T.sgn[:, 512 * h:512 * h + 512], T[BK[h]][:], AF.Sign, -TINY), [BK[h]], [("sgn", 512 * h, 512 * h + 512)])
+            p([mm(T.pD[64:128, o + k:o + 128:16], T.sgn[:, 64 * k:64 * k + 64], T.gik[:, 8:16], False, stop and k == 15) for k in range(8 * h, 8 * h + 8)],
+              [("sgn", 512 * h, 512 * h + 512), "gik"], ["pD"])
+
+    def open_keys(w, signed):
+        f = [mm(T.pD[:, 0:16 * w], T.one[0:1, :], T.ck[:, 0:16 * w], True, False)]
+        if signed:
+            f.append(mm(T.pD[64:128, 16 * w - 128:16 * w], T.one[0:1, 0:64], T.c8[:], False, False))
+        p(f, ["one", "ck", "c8"], ["pD"])
 
     for t in range(RO):
         last = t == RO - 1
+        a1 = (t + 1) % 2
         gxa, gda, gha = (128 * t, 128 * t + 128), (16 * t, 16 * t + 8), (768 * t, 768 * t + 768)
         to, fro = (rank + 1 + t % (N - 1)) % N, (rank - 1 - t % (N - 1)) % N
-        if not last:
-            s(act(T.ghs[:, gha[0]:gha[1]], T.t8[:, 0:1025].indirect(T.sl[:])), [("t8", 0, 1025), "sl"], [("ghs",) + gha])
-            for d in range(1, N):
-                a = gha[0] + 256 * (d - 1)
-                send((rank + d) % N, T.ghl[:, a:a + 256], T.ghs[:, a:a + 256], [("ghs", a, a + 256)], "gh%d" % t)
-            landed(("ghl",) + gha, "gh%d" % t, sum(len(topo.engines(cores[(rank - d) % N], core)) for d in range(1, N)))
         v(tc(T.ldI[:], T.pG[:, 0:64]), ["pG"], ["ldI"])
         v(ts(T.ldI[:], T.ldI[:], 2047, A.bitwise_and), ["ldI"], ["ldI"])
         v(ts(T.lfd[:], T.ldI[:], 1.0, A.add), ["ldI"], ["lfd"])
+        if t == 0:
+            for b in range(4):
+                weeks(b, True)
         for h in (0, 1):
-            s(act(T.cv[:, 1 + 512 * h:513 + 512 * h], T.cw[:, 0:2049].indirect(T.lfd[:, 32 * h:32 * h + 32])), ["cw", "lfd"], [("cv", 1 + 512 * h, 513 + 512 * h)])
+            if t > 0:
+                s(act(T.cv[:, 1 + 512 * h:513 + 512 * h], T.cw[:, 0:2049].indirect(T.lfd[:, 32 * h:32 * h + 32])), ["cw", "lfd"], [("cv", 1 + 512 * h, 513 + 512 * h)])
             v(tt(T.cmp[:, 512 * h:512 * h + 512], T.sd[:, 0:2049].indirect(T.lfd[:, 32 * h:32 * h + 32]), T.xw[:, 1 + 512 * h:513 + 512 * h], A.is_le),
               [("sd", 0, 2049), "lfd", ("xw", 1, 1025)], [("cmp", 512 * h, 512 * h + 512)])
             p([mm(T.pA[:, 8 * c:8 * c + 8], T.cmp[:, 128 * c:128 * c + 128], T.gib[:]) for c in range(4 * h, 4 * h + 4)], [("cmp", 512 * h, 512 * h + 512), "gib"], ["pA"])
+        if t > 0:
+            sums(t % 2, 2, 0)
         v(ts(T.bz[:, 56:120], T.pA[:, 0:64], 4.5, A.is_lt), ["pA"], [("bz", 56, 120)])
         p([mm(T.pB[:, 0:64], T.upr[:], T.bz[:, 56:120], True, False)] + [mm(T.pB[:, 0:64], T.one[:], T.bz[:, 56 - 8 * q:120 - 8 * q], False, q == 7) for q in range(1, 8)],
           ["upr", "one", "bz"], ["pB"])
         v(tc(T.rkI[:], T.pB[:, 0:64]), ["pB"], ["rkI"])
         s([act(T.th[:, c::17], T.pB[:, 0:64], AF.Sign, 16.0 * c - 4096.5, -1.0) for c in range(17)], ["pB"], ["th"])
-        p([mm(T.pH[:, 0:8], T.one[:], T.bz[:, 56 + 8 * c:64 + 8 * c], c == 0, c == 7) for c in range(8)], ["one", "bz"], ["pH"])
         v(ts(T.loI[:], T.rkI[:], 15, A.bitwise_and), ["rkI"], ["loI"])
         v([ts(T.oa[:, i::16], T.loI[:], float(i), A.is_equal) for i in range(16)], ["loI"], ["oa"])
         for c in range(8):
             a = slice(128 * c, 128 * c + 128)
-            v(ts(T.oa[:, a], T.oa[:, a], T.v1c[:, 8 + c:9 + c], A.mult), [("oa", a.start, a.stop), "v1c"], [("oa", a.start, a.stop)])
+            v(ts(T.oa[:, a], T.oa[:, a], T.v1c[:, 8 + c:9 + c], A.mult), [("oa", a.start, a.stop), "v1h"], [("oa", a.start, a.stop)])
             p(mm(T.pC[:, 0:136], T.oa[:, a], T.th[:, 136 * c:136 * c + 136], c == 0, c == 7), [("oa", a.start, a.stop), "th"], ["pC"])
         if t == 0:
-            s(act(T.smI[:], T.smI[:], AF.Sign, P15), ["smI", "pp"], ["smI"])
-            s(act(T.smk[:], T.smI[:], AF.Relu), ["smI"], ["smk"])
-            constants2()
+            for h in (0, 1):
+                s(act(T.cv[:, 1 + 512 * h:513 + 512 * h], T.cw[:, 0:2049].indirect(T.lfd[:, 32 * h:32 * h + 32])), ["cw", "lfd"], [("cv", 1 + 512 * h, 513 + 512 * h)])
+            sums(0, 2, 0, "V")
+            sums(0, 2, 1, "V")
+            constants1()
+        else:
+            sums(t % 2, 2, 1)
+
+        def ghosts():
+            s(act(T.ghs[:, gha[0]:gha[1]], T.t8[:, 0:1025].indirect(T.sl[:])), [("t8", 0, 1025), "sl"], [("ghs",) + gha])
+            for d in range(1, N):
+                a, b = gha[0] + 256 * (d - 1), GH[a1] + 256 * (d - 1)
+                send((rank + d) % N, T.wb[:, b:b + 256], T.ghs[:, a:a + 256], [("ghs", a, a + 256)], "gh%d" % t)
+            landed(("wb", GH[a1], GH[a1] + 768), "gh%d" % t, sum(len(topo.engines(cores[(rank - d) % N], core)) for d in range(1, N)))
+
+        if 0 < t < RO - 1:
+            ghosts()
         v(tc(T.win[:, 0:136], T.pC[:, 0:136]), ["pC"], ["win"])
-        v(tc(T.g1[:], T.win[:, 0:136].indirect(T.dgt[:, 0:1])), ["win", "dgl"], ["g1"])
-        v(tt(T.lvf[:], T.win[:, 0:136].indirect(T.dgt[:, 2:3]), T.g1[:], A.subtract), ["win", "dgl", "g1"], ["lvf"])
+        v(tc(T.g16[:], T.win[:, 0:136].indirect(T.dgt[:, 0:1])), ["win", "dgl"], ["g16"])
+        v(tt(T.lvf[:], T.win[:, 0:136].indirect(T.dgt[:, 2:3]), T.g16[:], A.subtract), ["win", "dgl", "g16"], ["lvf"])
         v(tc(T.lv[:], T.lvf[:]), ["lvf"], ["lv"])
+        open_keys(16, True)
         s(act(T.xg[:, 1:257], T.xw[:, 0:1025].indirect(T.lv[:])), ["xw", "lv"], [("xg", 1, 257)])
         v(tc(T.cg[:], T.cv[:, 0:1025].indirect(T.lv[:])), ["cv", "lv"], ["cg"])
         copies("S", T.xg, "xg", 1, 0, 128, range(11, 16))
         copies("V", T.xg, "xg", 1, 0, 128, range(0, 11))
-        copies("S", T.xg, "xg", 129, 2048, 128, range(0, 16))
+        fetch(192)
+        differ(T.xg, "xg", 193)
+        copies("S", T.xg, "xg", 129, 2048, 64, range(0, 16))
+        compare(0, 128)
+        count(0, 128)
+        signs(192)
         s(act(T.cgf[:], T.cv[:, 0:1025].indirect(T.lv[:])), ["cv", "lv"], ["cgf"])
-        s(act(T.dbf[:], T.t8[:, 0:1025].indirect(T.lv[:])), [("t8", 0, 1025), "lv"], ["dbf"])
-        p([mm(T.pD[:, 0:256], T.cgf[:, 0:128], T.pm0[:], True, False), mm(T.pD[:, 0:256], T.cgf[:, 128:256], T.pm1[:], False, False)], ["cgf", "pm0", "pm1"], ["pD"])
-        for h in (0, 1):
-            a = slice(2048 * h, 2048 * h + 2048)
-            v(tt(T.cmp[:, a], T.sd[:, 0:2049].indirect(T.cg[:, 128 * h:128 * h + 128]), T.xr[:, a], A.is_lt),
-              [("sd", 0, 2049), "cg", ("xrS", a.start, a.start + 1), ("xrV", a.start, a.start + 1)], [("cmp", a.start, a.stop)])
-            p([mm(T.pD[:, 16 * k + 8 * h:16 * k + 8 * h + 8], T.cmp[:, a.start + k:a.stop:16], T.gik[:], False, False) for k in range(16)], [("cmp", a.start, a.stop), "gik"], ["pD"])
-        p(mm(T.pD[:, 0:256], T.one[0:1, :], T.ck[:], False, True), ["one", "ck"], ["pD"])
-        if not last:
-            for wn in W:
-                s(act(T[wn][:, 1025:1793], T.ghl[:, gha[0]:gha[1]]), [("ghl",) + gha], [(wn, 1025, 1793)])
-        v(tc(T.dbi[:, 1:257], T.dbf[:]), ["dbf"], [("dbi", 1, 257)])
-        v(tc(T.nb[:], T.pH[:, 0:8]), ["pH"], ["nb"])
-        v(ts(T.dbi[:, 1:257], T.dbi[:, 1:257], 2047, A.bitwise_and), [("dbi", 1, 257)], [("dbi", 1, 257)])
-        v([ts(T.vld[:, 8 * q:8 * q + 8], T.nb[:], T.v1c[:, q:q + 1], A.is_ge) for q in (0, 1)], ["nb", "v1c"], ["vld"])
-        tree(16)
-        v(tt(T.rz[:, 8:24], T.vld[:], T.ks[:, 16:32], A.subtract), ["vld", ("ks", 16, 32)], [("rz", 8, 24)])
+        p([mm(T.pD[:, 128 * q:128 * q + 128], T.cgf[:, 128 * q:128 * q + 128], T.idF[:], False, False) for q in (0, 1)], ["cgf", "idF"], ["pD"])
+        compare(128, 64)
+        count(128, 64)
+        s(act(T.db[:, 1:257], T.t8[:, 0:1025].indirect(T.lv[:])), [("t8", 0, 1025), "lv"], [("db", 1, 257)])
+        if t == 0:
+            ghosts()
+            constants2()
+        keys(16, t)
+        v([excess(16, t), ts(T.rz[:, 8:24], T.kx[:, 15:256:16], T.thr[:, t % 2:t % 2 + 1], A.is_lt)], ["kx", ("thr", t % 2, t % 2 + 1)], [("ki", 0, 16), ("rz", 8, 24)])
         p([mm(T.pB[:, 0:16], T.upr[:], T.rz[:, 8:24], True, False), mm(T.pB[:, 0:16], T.one[:], T.rz[:, 0:16], False, True)], ["upr", "one", "rz"], ["pB"])
         chosen(16)
-        s(act(T.xf[:], T.ks[:, 48:64].indirect(T.ex[:])), [("ks", 48, 64), "ex"], ["xf"])
+        s(act(T.xf[:], T.ki[:, 16:32].indirect(T.ex[:])), [("ki", 16, 32), "ex"], ["xf"])
         v(tc(T.rkI[:, 0:16], T.pB[:, 0:16]), ["pB"], ["rkI"])
+        v(tt(T.xe[:], T.ki[:, 16:32].indirect(T.ex[:]), T.mk[:], A.mult), [("ki", 16, 32), "ex", "mk"], ["xe"])
+        p([mm(T.pA[:, 8 * q:8 * q + 8], T.xe[:, 128 * q:128 * q + 128], T.gi16[:]) for q in (0, 1)] + [mm(T.pA[:, 16:32], T.id16[:], T.duw[:], True, False)] +
+          [mm(T.pA[:, 16 + 8 * q:24 + 8 * q], T.xe[:, 128 * q:128 * q + 128], T.gin[:], False, q == 1) for q in (0, 1)], ["xe", "gi16", "gin", "id16", "duw"], ["pA"])
         v([ts(T.loI[:, 0:16], T.rkI[:, 0:16], 15, A.bitwise_and), ts(T.hiI[:, 0:16], T.rkI[:, 0:16], 4, A.arith_shift_right)], ["rkI"], ["loI", "hiI"])
         v(tt(T.oa[:, 0:256], T.loI[:, 0:16].indirect(T.ex[:]), T.lane[:], A.is_equal), ["loI", "ex", "lane"], [("oa", 0, 256)])
+        v([ts(T.u16s[:, 32:48], T.pA[:, 0:16], -1.0, A.add), tt(T.sm[:, 32:48], T.pA[:, 16:32], T.lvf[:], A.max)], ["pA", "lvf"], [("u16s", 32, 48), ("sm", 32, 48)])
+        s(act(T.wv[:], T.tab[:].indirect(T.u16s[:, 32:48]), AF.Identity, RB, MB), ["tab", ("u16s", 32, 48), "col"], ["wv"])
+        p([mm(T.pH[:, 128 * q:128 * q + 128], T.xf[:, 128 * q:128 * q + 128], T.jF[:]) for q in (0, 1)], ["xf", "jF"], ["pH"])
         v(tt(T.ob[:], T.hiI[:, 0:16].indirect(T.ex8[:]), T.ct8[:], A.is_equal), ["hiI", "ex8", "ct8"], ["ob"])
         v([ts(T.oa[:, 256 + 128 * q:384 + 128 * q], T.oa[:, 128 * q:128 * q + 128], T.v1c[:, q:q + 1], A.mult) for q in (0, 1)], [("oa", 0, 256), "v1c"], [("oa", 256, 512)])
-        p([mm(T.pE[:, 128 * q:128 * q + 128], T.xf[:, 128 * q:128 * q + 128], T.idF[:]) for q in (0, 1)], ["xf", "idF"], ["pE"])
         p([mm(T.pC[:, 0:64], T.oa[:, 256 + 128 * q:384 + 128 * q], T.ob[:, 64 * q:64 * q + 64], q == 0, q == 1) for q in (0, 1)], [("oa", 256, 512), "ob"], ["pC"])
-        v(tt(T.xe[:], T.ks[:, 48:64].indirect(T.ex[:]), T.mk[:], A.mult), [("ks", 48, 64), "ex", "mk"], ["xe"])
-        p([mm(T.pA[:, 8 * q:8 * q + 8], T.xe[:, 128 * q:128 * q + 128], T.gi16[:]) for q in (0, 1)], ["xe", "gi16"], ["pA"])
+        v(tc(T.u16s[:, 0:16], T.sm[:, 32:48]), [("sm", 32, 48)], [("u16s", 0, 16)])
         v(tc(T.wg[:, 0:64], T.pC[:, 0:64]), ["pC"], [("wg", 0, 64)])
-        v(lambda: V.tensor_reduce(T.thr[:, 1:2], T.ks[:, 16:32], AX.X, A.add), [("ks", 16, 32)], ["thr1"])
         v(tc(T.gl[:], T.wg[:].indirect(T.dgt[:, 4:5])), ["wg", "dg8"], ["gl"])
-        v(tc(T.rdb[:, 0:1], T.thr[:, 1:2]), ["thr1"], ["rdb"])
-        v(tc(T.dgh[:], T.dbi[:, 0:257].indirect(T.gl[:, 0:8])), ["dbi", "gl"], ["dgh"])
-        conv(T.dgh, "dgh", 0, 8, "selb", "pF")
-        p([mm(T.pH[:, 256 + 128 * q:384 + 128 * q], T.xf[:, 128 * q:128 * q + 128], T.jF[:]) for q in (0, 1)], ["xf", "jF"], ["pH"])
-        if not last:
-            p(mm(T.pB[:, 64:65], T.one[:], T.rdb[:, 0:1]), ["one", "rdb"], ["pB"])
-        v(tc(T.gxs[:, gxa[0]:gxa[1]], T.xg[:, 0:257].indirect(T.gl[:, 0:8])), ["xg", "gl"], [("gxs",) + gxa])
+        s(act(T.dgh[:], T.db[:, 0:257].indirect(T.gl[:, 0:8])), ["db", "gl"], ["dgh"])
+        conv(T.pC[:, 128:136], "pC", T.dgh, "dgh", 0, 8, "zd", 0)
+        s(act(T.gxs[:, gxa[0]:gxa[1]], T.xg[:, 0:257].indirect(T.gl[:, 0:8])), ["xg", "gl"], [("gxs",) + gxa])
         send(to, T.gxl[:, gxa[0]:gxa[1]], T.gxs[:, gxa[0]:gxa[1]], [("gxs",) + gxa], "gx%d" % t)
-        s(act(T.wv[:], T.pE[:, 0:256], AF.Copy, FLAG - 1.0), ["pE"], ["wv"])
-        v(tc(T.sm[:, 112:128], T.pA[:, 0:16]), ["pA"], [("sm", 112, 128)])
-        v(ts(T.sm[:, 0:16], T.sm[:, 112:128], 0.5, A.is_lt), [("sm", 112, 128)], [("sm", 0, 16)])
-        v([tt(T.sm[:, 32:48], T.sm[:, 0:16], DUW, A.mult), tt(T.sm[:, 16:32], T.sm[:, 0:16], DUS, A.mult)], [("sm", 0, 16), "du"], [("sm", 16, 48)])
-        v(ts(T.gds[:, gda[0]:gda[1]], T.pF[:, 0:8], 1.0, A.add), ["pF"], [("gds",) + gda])
+        v(lambda: V.tensor_copy(T.wb[:, W1 - 1:DUMP + 256].indirect(T.u16s[:, 0:16]), T.wv[:]), ["wv", ("u16s", 0, 16)], [("wb", W1 - 1, DUMP + 256)])
+        if last:
+            for h in (0, 1):
+                p(mm(T[BK[h]][0:16, :], T.dec[:], T.wb[:, W1 + 512 * h:W1 + 512 * h + 512]), ["dec", ("wb", W1, DUMP)], [BK[h]])
+                s(act(T.yb[0:16, 512 * h:512 * h + 512], T[BK[h]][0:16, :], AF.Identity, T.col[0:16, 7:8]), [BK[h], "dcb"], [("yb", 512 * h, 512 * h + 512)])
+            copy("Y", T.yan[:], T.yb[0:8, :], ["yb"], [])
+            copy("Y", T.yof[:], T.yb[8:16, :], ["yb"], [])
+        else:
+            pointers(a1, 0, T.wb, "wb", W1)
+            own(a1, 0)
+            p([mm(T.pB[:, 64:65], T.one[:], T.rz[:, 8 + c:9 + c], c == 0, c == 15) for c in range(16)], ["one", "rz"], ["pB"])
+        weave([later("V", tc(T.smi[:, 0:8], T.pC[:, 128:136]), ["pC"], [("smi", 0, 8)]),
+               later("V", ts(T.smi[:, 8:16], T.smi[:, 0:8], 2047, A.bitwise_and), [("smi", 0, 8)], [("smi", 8, 16)]),
+               later("V", ts(T.gds[:, gda[0]:gda[1]], T.smi[:, 8:16], 1.0, A.add), [("smi", 8, 16)], [("gds",) + gda])],
+              [lambda: eqdays(1)] + ([] if last else [lambda: pointers2(a1, 0)]))
         send(to, T.gdl[:, gda[0]:gda[1]], T.gds[:, gda[0]:gda[1]], [("gds",) + gda], "gd%d" % t)
         ne = len(topo.engines(cores[fro], core))
         landed(("gxl",) + gxa, "gx%d" % t, ne)
         landed(("gdl",) + gda, "gd%d" % t, ne)
-        v([tt(T.sm[:, 48:64], T.sm[:, 32:48], T.lvf[:], A.max), tt(T.sm[:, 64:80], T.sm[:, 16:32], T.sm[:, 112:128], A.max)], [("sm", 16, 48), ("sm", 112, 128), "lvf"], [("sm", 48, 80)])
-        v(tc(T.u16s[:, 0:16], T.sm[:, 48:64]), [("sm", 48, 64)], [("u16s", 0, 16)])
-        v(lambda: V.tensor_copy(T.w1[:, 0:2064].indirect(T.u16s[:, 0:16]), T.wv[:]), ["wv", ("u16s", 0, 16)], ["w1"])
-        if last:
-            copy("Y", T.yb[:, 256:320], T.w1[0:128:16, 1:1025], [("w1", 1, 1025)], [("yb", 256, 320)])
-            copy("Y", T.yb[:, 320:384], T.pw[0:128:16, 1:1025], [("pw", 1, 1025)], [("yb", 320, 384)])
-        else:
-            jumplist(0)
-        v(tc(T.rr[:], T.pH[:, 256:512]), ["pH"], ["rr"])
-        eqdays(2)
-        scan(0)
+        if not last:
+            jump(a1, 0, 0)
+            jump(a1, 0, 1)
+            after(a1, 0)
+            sums(a1, 0, 0)
+            sums(a1, 0, 1)
+            own(a1, 1)
+        eqdays(0)
         scan(1)
-        alternate(dayoffsets(16), [] if last else [lambda: jumplist2(0), lambda: jump(0, (0,)), lambda: jump(0, (1,)), lambda: jumplist(1)])
+        scan(0)
+        hh = [] if last else [later("V", tc(T.smi[:, 16:17], T.pB[:, 64:65]), ["pB"], [("smi", 16, 17)]),
+                              later("V", ts(T.smi[:, 17:18], T.smi[:, 16:17], 1, A.bitwise_and), [("smi", 16, 17)], [("smi", 17, 18)]),
+                              later("V", ts(T.thr[:, a1:a1 + 1], T.smi[:, 17:18], BIG, A.mult, 9.0 * BIG, A.add), [("smi", 17, 18)], [("thr", a1, a1 + 1)])]
+        weave(dayoffsets(16), hh)
         v(lambda: V.tensor_copy(T.sd[:, 0:2320].indirect(T.u16s[:, 24:32]), T.xg[:, 129:257]), [("xg", 1, 257), ("u16s", 16, 32)], ["sd"])
         if not last:
-            v(tc(T.smi[:, 40:41], T.pB[:, 64:65]), ["pB"], [("smi", 40, 41)])
+            pointers2(a1, 1)
         v(lambda: V.tensor_copy(T.sd[:, 0:2320].indirect(T.u16s[:, 16:24]), T.xg[:, 1:129]), [("xg", 1, 257), ("u16s", 16, 32)], ["sd"])
-        copies("S", T.gxl, "gxl", gxa[0], 0, 128, range(0, 16))
         gl = T.gdl[:, gda[0]:gda[1]]
-        s(act(T.cgf[:, 0:128], T.cw[:, 0:2049].indirect(gl)), ["cw", ("gdl",) + gda], ["cgf"])
-        if not last:
-            v(ts(T.smi[:, 41:42], T.smi[:, 40:41], 1, A.bitwise_and), [("smi", 40, 41)], [("smi", 41, 42)])
-            jumplist2(1)
-            jump(1)
-            jumplist(2)
-        v(tc(T.cg[:, 0:128], T.cw[:, 0:2049].indirect(gl)), ["cw", ("gdl",) + gda], ["cg"])
-        p(mm(T.pD[:, 0:128], T.cgf[:, 0:128], T.pmg[:], True, False), ["cgf", "pmg"], ["pD"])
-        v(tt(T.cmp[:, 0:2048], T.sd[:, 0:2049].indirect(T.cg[:, 0:128]), T.xr[:, 0:2048], A.is_lt),
-          [("sd", 0, 2049), "cg", ("xrS", 0, 1), ("xrV", 0, 1)], [("cmp", 0, 2048)])
-        p([mm(T.pD[:, 8 * k:8 * k + 8], T.cmp[:, k:2048:16], T.gik[:], False, False) for k in range(16)] +
-          [mm(T.pD[:, 0:128], T.one[0:1, :], T.ckg[:], False, True)], [("cmp", 0, 2048), "gik", "one", "ckg"], ["pD"])
-        if not last:
-            jumplist2(2)
-            jump(2)
+        open_keys(8, last)
+        if last:
+            copies("S", T.gxl, "gxl", gxa[0], 0, 64, range(0, 16))
+            v(tc(T.cg[:, 0:128], T.cw[:, 0:2049].indirect(gl)), ["cw", ("gdl",) + gda], ["cg"])
+            fetch(64)
+            differ(T.gxl, "gxl", gxa[0] + 64)
+            s(act(T.cgf[:, 0:128], T.cw[:, 0:2049].indirect(gl)), ["cw", ("gdl",) + gda], ["cgf"])
+            compare(0, 64)
+            count(0, 64)
+            p(mm(T.pD[:, 0:128], T.cgf[:, 0:128], T.idF[:], False, False), ["cgf", "idF"], ["pD"])
+            signs(64)
         else:
-            wf, pf = T.yb[:, 256:320], T.yb[:, 320:384]
-            v([ts(T.yb[:, 0:64], wf, 131072.0, A.is_ge, 1792.0, A.mult), ts(T.yb[:, 64:128], wf, 131072.0, A.is_ge, -FLAG, A.mult), ts(pf, pf, -1.0, A.add)], [("yb", 256, 384)], [("yb", 0, 128), ("yb", 320, 384)])
-            v([tt(T.yb[:, 128:192], T.yb[:, 0:64], pf, A.max), tt(T.yb[:, 192:256], T.yb[:, 64:128], wf, A.add)], [("yb", 0, 128), ("yb", 256, 384)], [("yb", 128, 256)])
-            copy("Y", T.yan[:], T.yb[:, 128:192], [("yb", 128, 192)], [])
-            copy("Y", T.yof[:], T.yb[:, 192:256], [("yb", 192, 256)], [])
-        tree(8)
+            jump(a1, 1, 0)
+            jump(a1, 1, 1)
+            after(a1, 1)
+            copies("V", T.gxl, "gxl", gxa[0], 0, 128, range(0, 16))
+            v(tc(T.cg[:, 0:128], T.cw[:, 0:2049].indirect(gl)), ["cw", ("gdl",) + gda], ["cg"])
+            sums(a1, 1, 0)
+            sums(a1, 1, 1)
+            pointers2(a1, 2)
+            own(a1, 2)
+            s(act(T.cgf[:, 0:128], T.cw[:, 0:2049].indirect(gl)), ["cw", ("gdl",) + gda], ["cgf"])
+            p(mm(T.pD[:, 0:128], T.cgf[:, 0:128], T.idF[:], False, False), ["cgf", "idF"], ["pD"])
+            compare(0, 128)
+            jump(a1, 2, 0)
+            count(0, 128)
+            jump(a1, 2, 1)
+            after(a1, 2)
+        keys(8, t)
+        v(excess(8, t), ["kx", ("thr", t % 2, t % 2 + 1)], [("ki", 0, 16)])
         chosen(8)
-        v(tt(T.xe[:], T.ks[:, 48:56].indirect(T.exg[:]), T.mkg[:], A.mult), [("ks", 48, 64), "exg", "mkg"], ["xe"])
-        p(mm(T.pA[:, 0:8], T.xe[:, 128:256], T.gi16[:]), ["xe", "gi16"], ["pA"])
-        p(mm(T.pH[:, 256:384], T.xe[:, 0:128], T.j16[:]), ["xe", "j16"], ["pH"])
-        if not last:
-            conv(T.t8, "t8", 1, 64, "selF", "pG")
-            v(ts(T.thr[:, 0:1], T.smi[:, 41:42], BIG, A.mult, 9.0 * BIG, A.add), [("smi", 41, 42)], ["thr"])
-        v(tc(T.sm[:, 112:120], T.pA[:, 0:8]), ["pA"], [("sm", 112, 128)])
-        v(tc(T.rr[:, 0:128], T.pH[:, 256:384]), ["pH"], ["rr"])
-        v(ts(T.sm[:, 0:8], T.sm[:, 112:120], 0.5, A.is_lt), [("sm", 112, 128)], [("sm", 0, 16)])
-        eqdays(1)
-        v(tt(T.sm[:, 16:24], T.sm[:, 0:8], T.du[:, 0:8], A.mult), [("sm", 0, 16), "du"], [("sm", 16, 48)])
+        v(tt(T.xe[:], T.ki[:, 16:24].indirect(T.exg[:]), T.mkg[:], A.mult), [("ki", 16, 32), "exg", "mkg"], ["xe"])
+        p([mm(T.pA[:, 0:8], T.xe[:, 128:256], T.gi16[:]), mm(T.pH[:, 0:128], T.xe[:, 0:128], T.j16[:])], ["xe", "gi16", "j16"], ["pA", "pH"])
+        eqdays(0)
         scan(0)
-        v(tt(T.sm[:, 64:72], T.sm[:, 16:24], T.sm[:, 112:120], A.max), [("sm", 16, 48), ("sm", 112, 128)], [("sm", 48, 80)])
-        alternate(dayoffsets(8), [])
+        weave(dayoffsets(8))
         v(lambda a=gxa[0]: V.tensor_copy(T.sd[:, 0:2320].indirect(T.u16s[:, 16:24]), T.gxl[:, a:a + 128]), [("gxl",) + gxa, ("u16s", 16, 32)], ["sd"])
     copy("Y", T.ys[:], T.sd[:, 1:2049], ["sd"], [])
     finish([("ls", sent[0])])

@@ -3,6 +3,7 @@ from concourse.mybir import AluOpType as A, ActivationFunctionType as AF
 BIG = 65536.0
 LOW = -1073741824.0
 TINY = 2.0 ** -110
+FAR = 4096.0
 RO = 4
 F, B, H, I, U = "float32", "bfloat16", "float16", "int32", "uint16"
 W3A, W2A, GA, W1, DUMP, GB, W2B, W3B, WEND = 0, 1024, 2048, 2833, 3857, 4128, 4912, 5936, 6960
@@ -12,20 +13,20 @@ EW = [16 * (b + 1) for b in range(8)]
 EO = [8 * b * (b + 1) for b in range(9)]
 SB = {
     "anI": (64, I), "ofI": (112, I), "snI": (48, I), "wkb": (2048, B), "xw": (1040, B), "sd": (2320, B),
-    "pI": (3, I), "pp": (3, F), "n144": (144, I), "n512": (512, I), "kI": (256, I), "lmc": (16, F), "pw": (16, F), "cc": (32, F), "col": (24, F), "hi16": (16, F), "tc": (16, F),
-    "tab": (2048, B), "id16": (128, H), "idb": (128, B), "idF": (128, F), "jF": (128, F), "j16": (128, H), "upr": (128, B), "amb": (128, B), "nid": (128, B),
-    "one": (128, B), "seven": (128, B), "m1k": (128, B), "gi16": (8, H), "gin": (8, H), "gib": (8, B), "gik": (16, B), "zp": (864, H), "zd": (144, H), "dec": (16, H),
-    "mk": (256, H), "mkg": (256, H), "lane": (256, B), "segm": (256, B), "ct8": (128, B), "ex": (16, U), "exg": (16, U), "ex8": (8, U), "dgt": (8, U), "v1c": (16, F),
-    "smk": (576, B), "du": (16, F), "duw": (16, H), "lo16": (512, H), "anl": (64, U), "ofl": (112, U), "an1": (128, F),
-    "wb": (WEND, B), "g0": (1024, B), "g1": (1024, B), "t8": (1040, B), "l0": (64, U), "l1": (64, U), "l2": (64, U), "sl": (48, U), "cw": (2056, F), "cq": (256, F), "sg": (2048, B),
-    "ldI": (64, I), "lfd": (64, U), "cv": (1032, F), "cmp": (3072, B), "xr": (3072, B), "sgb": (1024, B), "sgn": (1024, B), "bz": (120, B), "rz": (24, B), "rkI": (64, I), "loI": (64, I), "hiI": (16, I),
-    "oa": (1024, H), "ob": (128, H), "th": (1088, B), "win": (144, F), "wg": (128, F), "g16": (16, F), "lv": (16, U), "lvf": (16, F),
-    "xg": (272, B), "cg": (256, U), "cgf": (256, F), "db": (272, B), "kx": (256, F), "ki": (32, I), "sm": (64, F), "smi": (32, I), "u16s": (64, U),
-    "thr": (2, F), "xe": (256, H), "xf": (256, F), "wv": (256, B), "eq": (1152, B), "scn": (1152, B), "gl": (16, U), "dgh": (128, B), "yb": (1024, F),
+    "pI": (3, I), "pp": (3, F), "n16": (16, I), "n144": (144, B), "lmc": (16, F), "pw": (16, F), "cc": (32, F), "col": (24, F), "hi16": (16, F), "tc": (16, F),
+    "tab": (2048, B), "idb": (128, B), "idF": (128, F), "jF": (128, F), "jb": (128, B), "upr": (256, B), "amb": (128, B), "nid": (128, B),
+    "one": (256, B), "seven": (128, B), "m1k": (128, B), "gin": (16, B), "gib": (16, B), "gik": (16, B), "zp": (864, H), "zd": (144, H), "dec": (16, B),
+    "mkg": (384, B), "lane": (256, B), "segm": (256, B), "ct8": (128, B), "ex": (16, U), "exg": (16, U), "ex8": (8, U), "dgt": (8, U), "v1c": (16, F),
+    "smk": (576, B), "tri": (16, F), "du": (16, F), "duw": (16, H), "anl": (64, U), "ofl": (112, U), "an1": (128, F),
+    "wb": (WEND, B), "g0": (1024, B), "g1": (1024, B), "t8": (1040, B), "l0": (64, U), "l1": (64, U), "l2": (64, U), "sl": (48, U), "cw": (2056, F), "sg": (2048, B),
+    "ldI": (128, I), "lfd": (64, U), "cv": (1032, F), "cmp": (3072, B), "xr": (3072, B), "sgb": (1024, B), "sgn": (1024, B), "bz": (120, B), "rz": (24, B), "rkI": (64, I), "loI": (64, I), "hiI": (16, I), "lo2": (128, B), "obj": (128, B), "c8b": (16, B),
+    "oa": (1024, H), "ob": (128, B), "th": (1088, B), "win": (144, F), "wg": (128, F), "g16": (16, F), "lv": (16, U), "lvf": (16, F),
+    "xg": (272, B), "cg": (256, U), "cgf": (256, F), "db": (256, B), "dI": (32, I), "kx": (256, F), "ki": (32, I), "sm": (64, F), "smi": (32, I), "u16s": (64, U),
+    "thr": (2, F), "xe": (256, H), "xf": (256, F), "wv": (256, B), "eq": (1152, B), "scn": (1152, B), "yb": (1024, F),
     "ghs": (2304, B), "gxs": (512, B), "gxl": (512, B), "gds": (64, U), "gdl": (64, U),
 }
 SCRATCH = {k: ("sbuf", [128, n], d) for k, (n, d) in SB.items()}
-SCRATCH.update({"ck": ("sbuf", [1, 256], B), "c8": ("sbuf", [1, 128], B)})
+SCRATCH.update({"ck": ("sbuf", [1, 256], B), "c8": ("sbuf", [1, 128], B), "n256": ("sbuf", [1, 512], B)})
 PS = ("pA", "pB", "pC", "pD", "pE", "pF", "pG", "pH")
 SCRATCH.update({k: ("psum", [128, 512], F) for k in PS})
 SEMAPHORES = ["qV", "qS", "qP", "qG", "ls"] + ["d%d" % i for i in range(11)] + ["gh%d" % t for t in range(3)] + ["gx%d" % t for t in range(RO)] + ["gd%d" % t for t in range(RO)]
@@ -158,11 +159,14 @@ def rank_program(g, core, T, topo):
         g.remote_dma(out, in_, T.sem[sem], T.sem.ls, pid, rid, topo.mask(core, d))
         sent[0] += len(topo.engines(core, d))
 
-    def iota(name, view, pat, base, ch, fl=False):
+    def iota(name, view, pat, base, ch, fl=True):
         if fl:
             op("G", lambda: g.iota(view, pat, base, ch, allow_small_or_imprecise_dtypes=True), [], [name])
         else:
             op("G", lambda: g.iota(view, pat, base, ch), [], [name])
+
+    def select(name, view, src, sname, pat, cmp, fill, base, ch):
+        op("G", lambda: g.affine_select(view, src, pat, cmp, fill, base, ch), [sname], [name])
 
     def col(i):
         return T.col[:, i:i + 1]
@@ -170,61 +174,87 @@ def rank_program(g, core, T, topo):
     def lm(i):
         return T.lmc[:, i:i + 1]
 
-    v([ms(T.xw[:, 0:1], LOW), ms(T.sd[:, 0:1], 0.0)], [], [("xw", 0, 16), ("sd", 0, 16)])
+    v([ms(T.xw[:, 0:1], LOW), ms(T.sd[:, 0:1], 0.0), ms(T.one[:], 1.0)], [], [("xw", 0, 16), ("sd", 0, 16), "one"])
     copy("Y", T.anI[:], T.an0[:], [], ["anI"])
     copy("Y", T.ofI[:], T.of0[:], [], ["ofI"])
     copy("S", T.wkb[:], T.wk[:], [], ["wkb"])
     copy("Y", T.sd[:, 1:2049], T.s0[:], [], [("sd", 1, 2049)])
     copy("Y", T.xw[:, 1:1025], T.x[:], [], [("xw", 1, 1025)])
     copy("Y", T.snI[:], T.snd[:], [], ["snI"])
-    iota("pI", T.pI[:, 0:1], [[0, 1]], 0, 1)
+    ONE = T.one[:, 0:128]
+    iota("pI", T.pI[:, 0:1], [[0, 1]], 0, 1, False)
+    iota("n16", T.n16[:], [[1, 16]], 0, 0, False)
+    select("idb", T.idb[:], ONE, "one", [[-1, 128]], A.is_equal, 0.0, 0, 1)
     iota("n144", T.n144[:], [[1, 144]], 0, 0)
-    iota("n512", T.n512[:], [[1, 512]], 0, 0)
-    iota("v1c", T.v1c[:, 0:8], [[128, 8]], 1, 1, True)
-    iota("ct8", T.ct8[:], [[0, 16], [1, 8]], -256, 0, True)
-    iota("ck", T.ck[:], [[0, 16], [-2048, 16]], 30720, 0, True)
-    iota("du", T.du[:], [[16, 16]], 2056, 0, True)
+    iota("n256", T.n256[:], [[0, 2], [1, 256]], 0, 0)
+    select("up0", T.upr[:, 128:256], ONE, "one", [[1, 128]], A.is_gt, 0.0, 0, -1)
+    select("upr", T.upr[:, 0:128], T.upr[:, 128:256], "up0", [[-1, 128]], A.not_equal, -4096.0, 0, 1)
+    iota("v1c", T.v1c[:, 0:8], [[128, 8]], 1, 1)
+    iota("du", T.du[:], [[16, 16]], 2056, 0)
+    iota("ck", T.ck[:], [[0, 16], [-2048, 16]], 30720, 0)
+    iota("c8", T.c8[:], [[0, 128]], 8 * 65536, 0)
+    iota("lane", T.lane[:], [[0, 16], [1, 16]], 0, 0)
+    select("segm", T.segm[:], T.one[:], "one", [[0, 16], [1, 16]], A.is_gt, 0.0, 0, 0)
+    iota("ct8", T.ct8[:], [[0, 16], [1, 8]], -256, 0)
+    select("jb0", T.jb[:], ONE, "one", [[1, 128]], A.not_equal, -1.0, -127, 1)
+    select("jb", T.jb[:], T.jb[:], "jb0", [[1, 128]], A.is_equal, 0.0, -127, 1)
+    iota("smk0", T.smk[:], [[0, 576]], 0, 0)
 
     P15, P4, PC = T.pp[:, 0:1], T.pp[:, 1:2], T.pp[:, 2:3]
-    N1, G8, N16, K1 = T.n144[:, 0:128], T.n144[:, 0:8], T.n144[:, 0:16], T.kI[:, 0:128]
+    G8, N16 = T.n16[:, 0:8], T.n16[:]
     ZC, MB, MP, BP, RB, WL, WD, DB = (col(i) for i in range(8))
     v([ts(T.pI[:, 1:2], T.pI[:, 0:1], 15, A.bitwise_and), ts(T.pI[:, 2:3], T.pI[:, 0:1], 4, A.arith_shift_right)], ["pI"], ["pI2"])
-    v([ms(T.pw[:, b:b + 1], float(1 << b)) for b in range(5)] + [ms(T.tab[:, 0:1], 0.0), ms(T.hi16[:, 0:1], 0.0)], [], ["pw", ("tab", 0, 1), ("hi16", 0, 1)])
+    v([ms(T.pw[:, 0:1], 1.0), ms(T.pw[:, 1:2], 2.0)], [], ["pwa"])
     v([tc(P15, T.pI[:, 1:2]), tc(P4, T.pI[:, 2:3]), tc(PC, T.pI[:, 0:1])], ["pI", "pI2"], ["pp"])
-    v(ts(T.lmc[:], N16, P15, A.is_equal), ["n144", "pp"], ["lmc"])
-    v([ts(T.pw[:, 5:10], T.pw[:, 0:5], 32.0, A.mult), ms(T.pw[:, 10:11], 1024.0)], ["pw"], ["pw2"])
-    v([ts(T.cc[:, 16:21], T.pw[:, 0:5], lm(11), A.mult), ts(T.cc[:, 21:26], T.pw[:, 0:5], lm(12), A.mult), tc(T.cc[:, 26:27], lm(13))], ["pw", "lmc"], [("cc", 16, 32)])
-    v([ts(MB, P15, 11.0, A.is_lt), ts(MP, P15, 11.0, A.is_ge), ts(ZC, P4, 16.0, A.mult, 15.0, A.add),
-       ts(WL, lm(12), 32.0, A.mult, lm(11), A.add), ts(WD, lm(12), 24.0, A.mult, lm(13), A.add)], ["pp", "lmc"], ["col"])
+    v([ms(T.pw[:, b:b + 1], float(1 << b)) for b in range(2, 5)], [], ["pw"])
+    v(ts(T.lmc[:], N16, P15, A.is_equal), ["n16", "pp"], ["lmc"])
+    v([ms(T.tab[:, 0:1], 0.0), ms(T.hi16[:, 0:1], 0.0)], [], [("tab", 0, 1), ("hi16", 0, 1)])
+    v([ts(T.cc[:, 16:21], T.pw[:, 0:5], lm(11), A.mult), ts(T.cc[:, 21:26], T.pw[:, 0:5], lm(12), A.mult), tc(T.cc[:, 26:27], lm(13))], ["pw", "pwa", "lmc"], [("cc", 16, 32)])
+    v([ts(MB, P15, 11.0, A.is_lt), ts(MP, P15, 11.0, A.is_ge)], ["pp"], [("col", 1, 3)])
     v(tt(T.cc[:, 0:11], T.cc[:, 16:27], T.lmc[:, 0:11], A.add), [("cc", 16, 32), "lmc"], [("cc", 0, 16)])
+    s([act(T.seven[:], T.idb[:], AF.Copy, 0.0, 7.0), act(T.m1k[:], T.idb[:], AF.Copy, 0.0, -1024.0), act(T.nid[:], T.idb[:], AF.Copy, 0.0, -1.0), act(T.idF[:], T.idb[:]),
+       act(T.amb[:], T.idb[:], AF.Copy, 0.0, MB)], ["idb", ("col", 1, 3)], ["seven", "m1k", "nid", "idF", "amb"])
 
     def double(name, first, n):
         return [later("V", ts(T[name][:, 1 << b:2 << b], T[name][:, 0:1 << b], T.cc[:, first + b:first + b + 1], A.add), [(name, 0, 1 << b), ("cc", 0, 16)], [(name, 1 << b, 2 << b)]) for b in range(n)]
 
     more = [
-        later("V", [ts(BP, MP, 65.0, A.mult, -1.0, A.add), ts(RB, MP, 64.0, A.mult, WD, A.add)], ["col"], ["col"]),
-        later("V", [ts(T.idb[:], N1, PC, A.is_equal), ts(T.amb[:], N1, PC, A.is_equal, MB, A.mult)], ["n144", "pp", "col"], ["idb", "amb"]),
-        later("V", [ts(col(8 + 3 * a + l), lm(13), float(GH[a] - WIN[a][l][2]), A.mult, WL, A.add) for a in (0, 1) for l in range(3)], ["lmc", "col"], ["col2"])]
+        later("V", [ts(WD, lm(12), 24.0, A.mult, lm(13), A.add), ts(BP, MP, 65.0, A.mult, -1.0, A.add)], ["lmc", ("col", 1, 3)], [("col", 3, 4), ("col", 6, 7)]),
+        later("V", [tc(T.anl[:], T.anI[:]), tc(T.ofl[:], T.ofI[:])], ["anI", "ofI"], ["anl", "ofl"]),
+        later("V", ts(RB, MP, 64.0, A.mult, WD, A.add), [("col", 1, 3), ("col", 6, 7)], [("col", 4, 5)])]
     weave(double("tab", 0, 7), double("hi16", 7, 4) + more)
-    v([tc(T.anl[:], T.anI[:]), tc(T.ofl[:], T.ofI[:])], ["anI", "ofI"], ["anl", "ofl"])
-    s([act(T.tab[:, 128 * a:128 * a + 128], T.tab[:, 0:128], AF.Identity, T.hi16[:, a:a + 1]) for a in range(11, 16)], [("tab", 0, 128), "hi16"], [("tab", 1408, 2048)])
-    v([ts(T.tab[:, 128 * a:128 * a + 128], T.tab[:, 0:128], T.hi16[:, a:a + 1], A.add) for a in range(1, 11)], [("tab", 0, 128), "hi16"], [("tab", 128, 1408)])
+    v([ts(T.tab[:, 128 * a:128 * a + 128], T.tab[:, 0:128], T.hi16[:, a:a + 1], A.add) for a in range(1, 16)], [("tab", 0, 128), "hi16"], [("tab", 128, 2048)])
+
+    WKB = ("pH", "pD", "pC", "pB")
+
+    def weeks(b):
+        bank = WKB[b]
+        p([mm(T[bank][:], T.seven[:], T.wkb[:, 512 * b:512 * b + 512], True, False), mm(T[bank][:], T.one[0:1, 0:128], T.n256[:], False, True)], ["seven", "wkb", "one", "n256"], [bank])
+        s([act(T.sg[:, 512 * b + c:512 * b + c + 256], T[bank][:, c:c + 256], AF.Sign, 512 * b + c - 2047.5) for c in (0, 256)], [bank], [("sg", 512 * b, 512 * b + 512)])
+
+    def weeks2(b):
+        bank = WKB[b]
+        p([mm(T[bank][:], T.seven[:], T.wkb[:, 512 * b:512 * b + 512], True, False), mm(T[bank][:], T.one[0:1, 0:128], T.n256[:], False, False),
+           mm(T[bank][:], T.m1k[:], T.sg[:, 512 * b:512 * b + 512], False, True)], ["seven", "wkb", "one", "n256", "m1k", ("sg", 512 * b, 512 * b + 512)], [bank])
+        s([act(T.cw[:, 1 + 512 * b + c:257 + 512 * b + c], T[bank][:, c:c + 256], AF.Copy, 512 * b + c - 1023.0) for c in (0, 256)], [bank], [("cw", 1 + 512 * b, 513 + 512 * b)])
+
     for h in (0, 1):
-        s(act(T.g1[:, 512 * h:512 * h + 512], T.tab[:].indirect(T.anl[:, 32 * h:32 * h + 32]), AF.Identity, BP, MP), ["tab", "anl", "col"], [("g1", 512 * h, 512 * h + 512)])
-    v(ts(T.wb[:, GA:GA + 384], T.tab[:].indirect(T.ofl[:, 64:88]), MB, A.mult, RB, A.add), ["tab", "ofl", "col"], [("wb", GA, GA + 384)])
-    s(act(T.wb[:, GA + 384:GA + 768], T.tab[:].indirect(T.ofl[:, 88:112]), AF.Identity, RB, MB), ["tab", "ofl", "col"], [("wb", GA + 384, GA + 768)])
-    v(ts(T.an1[:, 0:64], T.anI[:], 1024.0, A.is_ge, float(GA - W1 - 1024), A.mult), ["anI"], [("an1", 0, 64)])
-    pads = [(GA + 769, W1), (DUMP, GB), (GB + 769, W2B)]
-    v([ms(T.wb[:, a:b], 0.0) for a, b in pads] + [tc(T.wb[:, a + 768:a + 769], RB) for a in GH], ["col"], [("wb",) + a for a in pads] + [("wb", a + 768, a + 769) for a in GH])
-    v(tt(T.an1[:, 64:128], T.an1[:, 0:64], T.anI[:], A.add), [("an1", 0, 64), "anI"], [("an1", 64, 128)])
+        s(act(T.g1[:, 512 * h:512 * h + 512], T.tab[:].indirect(T.anl[:, 32 * h:32 * h + 32]), AF.Identity, BP, MP), ["tab", "anl", ("col", 1, 4)], [("g1", 512 * h, 512 * h + 512)])
+    v(ts(T.wb[:, GA:GA + 512], T.tab[:].indirect(T.ofl[:, 64:96]), MB, A.mult, RB, A.add), ["tab", "ofl", ("col", 1, 5)], [("wb", GA, GA + 512)])
+    s(act(T.wb[:, GA + 512:GA + 768], T.tab[:].indirect(T.ofl[:, 96:112]), AF.Identity, RB, MB), ["tab", "ofl", ("col", 1, 5)], [("wb", GA + 512, GA + 768)])
+    v([ts(T.an1[:, 0:64], T.anI[:], 1024.0, A.is_ge, float(GA - W1 - 1024), A.mult), ms(T.wb[:, GA + 769:W1], 0.0), tc(T.wb[:, GA + 768:GA + 769], RB)],
+      ["anI", ("col", 4, 5)], [("an1", 0, 64), ("wb", GA + 768, W1)])
     v(tt(T.wb[:, W1:W1 + 512], T.tab[:].indirect(T.ofl[:, 0:32]), T.g1[:, 0:512], A.max), ["tab", "ofl", ("g1", 0, 512)], [("wb", W1, W1 + 512)])
-    v(ts(T.l0[:], T.an1[:, 64:128], float(W1 - GA), A.add), [("an1", 64, 128)], ["l0"])
+    v([tt(T.an1[:, 64:128], T.an1[:, 0:64], T.anI[:], A.add), ts(ZC, P4, 16.0, A.mult, 15.0, A.add), ts(WL, lm(12), 32.0, A.mult, lm(11), A.add)],
+      [("an1", 0, 64), "anI", "pp", "lmc"], [("an1", 64, 128), ("col", 0, 1), ("col", 5, 6)])
     v(tt(T.wb[:, W1 + 512:DUMP], T.tab[:].indirect(T.ofl[:, 32:64]), T.g1[:, 512:1024], A.max), ["tab", "ofl", ("g1", 512, 1024)], [("wb", W1 + 512, DUMP)])
+    v(ts(T.l0[:], T.an1[:, 64:128], float(W1 - GA), A.add), [("an1", 64, 128)], ["l0"])
+    weeks(0)
 
     BK = ("pE", "pF")
 
     def conv(o, bank, src, name, c0, cols, z, z0, st=True, sp=True):
-        p([mm(o, T[z][:, z0 + 15 - k:z0 + 143 - k], src[:, c0 + k:c0 + 16 * cols:16], st and k == 0, sp and k == 15) for k in range(16)], [(name, c0, c0 + 16 * cols), z], [bank])
+        p([mm(o, T[z][:, z0 + 15 - k:z0 + 143 - k], src[:, c0 + k:c0 + 16 * cols:16], st and k == 0, sp and k == 15) for k in range(16)], [(name, c0, c0 + 16 * cols), (z, z0, z0 + 144)], [bank])
 
     def pointers(a, l, src, name, c0):
         conv(T.pG[:, 0:64], "pG", src, name, c0, 64, "zp", 144 * (3 * a + l))
@@ -244,6 +274,9 @@ def rank_program(g, core, T, topo):
         lo, hi, f = WIN[a][l]
         gn, c = "g%d" % (l % 2), 512 * h
         op(q, (act if q == "S" else tc)(T[gn][:, c:c + 512], T.wb[:, lo:hi].indirect(T["l%d" % l][:, 32 * h:32 * h + 32])), [("wb", lo, hi), "l%d" % l], [(gn, c, c + 512)])
+
+    def join(l, h):
+        gn, c = "g%d" % (l % 2), 512 * h
         p(mm(T[BK[h]][:], T["amb" if l == 2 else "idb"][:], T[gn][:, c:c + 512], False, True), ["amb", "idb", (gn, c, c + 512)], [BK[h]])
 
     def after(a, l):
@@ -257,79 +290,78 @@ def rank_program(g, core, T, topo):
         if l < 2:
             f = WIN[a][l + 1][2] + c
             op(q, (act if q == "S" else tc)(T.wb[:, f:f + 512], T[BK[h]][:]), [BK[h]], [("wb", f, f + 512)])
-        elif q == "S":
-            s(act(T.t8[:, 1 + c:513 + c], T[BK[h]][:], AF.Identity, RB), [BK[h], "col"], [("t8", 1 + c, 513 + c)])
         else:
-            v(ts(T.t8[:, 1 + c:513 + c], T[BK[h]][:], RB, A.add), [BK[h], "col"], [("t8", 1 + c, 513 + c)])
+            s(act(T.t8[:, 1 + c:513 + c], T[BK[h]][:], AF.Identity, RB), [BK[h], ("col", 4, 5)], [("t8", 1 + c, 513 + c)])
 
-    def weeks(b, second):
-        bank, c = PS[b], 512 * b
-        f = [mm(T[bank][:], T.seven[:], T.wkb[:, c:c + 512], True, False), mm(T[bank][:], T.id16[:], T.lo16[:], False, not second)]
-        if second:
-            f.append(mm(T[bank][:], T.m1k[:], T.sg[:, c:c + 512], False, True))
-        p(f, ["seven", "wkb", "id16", "lo16", "m1k"] + ([("sg", c, c + 512)] if second else []), [bank])
-        if second:
-            s(act(T.cw[:, 1 + c:513 + c], T[bank][:], AF.Copy, c - 1024.0), [bank], [("cw", 1 + c, 513 + c)])
-        else:
-            s(act(T.sg[:, c:c + 512], T[bank][:], AF.Sign, c - 2048.5), [bank], [("sg", c, c + 512)])
+    def datelist():
+        return [later("V", tc(T.ldI[:, 0:64], T.pG[:, 0:64]), ["pG"], [("ldI", 0, 64)]),
+                later("V", ts(T.ldI[:, 64:128], T.ldI[:, 0:64], 2047, A.bitwise_and), [("ldI", 0, 64)], [("ldI", 64, 128)]),
+                later("V", ts(T.lfd[:], T.ldI[:, 64:128], 1.0, A.add), [("ldI", 64, 128)], ["lfd"])]
 
-    def zed(i):
-        return ts(T.zp[:, 144 * i:144 * i + 143], T.n144[:, 0:143], ZC, A.is_equal, col(8 + i), A.mult)
+    def zed(*ids):
+        v([ts(col(8 + i), lm(13), float(GH[i // 3] - WIN[i // 3][i % 3][2]), A.mult, WL, A.add) for i in ids], ["lmc", ("col", 5, 6)], [("col", 8 + i, 9 + i) for i in ids])
+        return later("V", [ts(T.zp[:, 144 * i:144 * i + 144], T.n144[:], ZC, A.is_equal, col(8 + i), A.mult) for i in ids],
+                     ["n144", ("col", 0, 1)] + [("col", 8 + i, 9 + i) for i in ids], [("zp", 144 * i, 144 * i + 144) for i in ids])
 
-    fill = [[
-        later("V", [zed(1), zed(2), tt(T.cc[:, 16:27], T.pw[:, 0:11], T.lmc[:, 0:11], A.mult)], ["n144", "col", "col2", "pw", "pw2", "lmc"], ["zp", ("cc", 16, 32)]),
-        later("V", [ts(T.seven[:], N1, PC, A.is_equal, 7.0, A.mult), ts(T.m1k[:], N1, PC, A.is_equal, -1024.0, A.mult), ts(T.id16[:], N1, PC, A.is_equal), ts(T.lo16[:], T.n512[:], 1.0, A.add)],
-              ["n144", "n512", "pp"], ["seven", "m1k", "id16", "lo16"]),
-    ], [
-        later("V", lambda: V.tensor_tensor_scan(T.cc[:, 0:11], T.cc[:, 16:27], T.cc[:, 16:27], 0.0, A.max, A.max), [("cc", 16, 32)], [("cc", 0, 16)]),
-        later("V", [ms(T.one[:], 1.0), ms(T.t8[:, 0:1], 0.0), ms(T.db[:, 0:1], 0.0), ms(T.cv[:, 0:1], 1.0), ms(T.cw[:, 0:1], 1.0), ms(T.xg[:, 0:1], LOW)], [],
-              ["one", ("t8", 0, 1), ("db", 0, 1), ("cv", 0, 1), ("cw", 0, 1), ("xg", 0, 1)]),
-        later("V", ts(T.zd[:, 0:143], T.n144[:, 0:143], ZC, A.is_equal, T.cc[:, 10:11], A.mult), ["n144", "col", ("cc", 0, 16)], ["zd"]),
-        later("V", [ts(T.cq[:, 0:128], N1, PC, A.is_equal, -4096.0, A.mult), ts(T.cq[:, 128:256], N1, PC, A.is_gt), ts(T.gib[:], G8, P4, A.is_equal)], ["n144", "pp"], ["cq", "gib"]),
-    ], [
-        later("V", tt(T.upr[:], T.cq[:, 0:128], T.cq[:, 128:256], A.add), ["cq"], ["upr"]),
-        later("V", [ms(T.bz[:, 0:56], 0.0), ts(T.tc[:, 5:6], P4, 17.0, A.mult, P15, A.add), ts(T.v1c[:, 8:16], T.v1c[:, 0:8], 0.5, A.mult), ts(T.sl[:], T.snI[:], 1.0, A.add)],
-              ["pp", "v1c", "snI"], [("bz", 0, 56), "tcd", "v1h", "sl"]),
-        later("V", [tc(T.dgt[:, 0:1], T.tc[:, 5:6]), ts(T.dgt[:, 2:3], T.tc[:, 5:6], 1.0, A.add)], ["tcd"], ["dgl"]),
-    ]]
+    TC = [T.tc[:, i:i + 1] for i in range(16)]
+    WB = T.cc[:, 10:11]
+
+    def fill0():
+        v([ts(T.pw[:, 5:10], T.pw[:, 0:5], 32.0, A.mult), ms(T.pw[:, 10:11], 1024.0), ms(T.t8[:, 0:1], 0.0), ms(T.cv[:, 0:1], 1.0), ms(T.cw[:, 0:1], 1.0), ms(T.xg[:, 0:1], LOW),
+           ts(T.gib[:, 0:8], G8, P4, A.is_equal), ts(T.gib[:, 8:16], G8, P4, A.is_equal, 0.5, A.mult), ms(T.c8b[:], 8.0), ms(T.bz[:, 0:56], 0.0)],
+          ["pw", "pwa", "n16", "pp"], ["pw2", ("t8", 0, 1), ("cv", 0, 1), ("cw", 0, 1), ("xg", 0, 1), "gib", "c8b", ("bz", 0, 56)])
+        v([tt(T.cc[:, 16:27], T.pw[:, 0:11], T.lmc[:, 0:11], A.mult), ts(TC[5], P4, 17.0, A.mult, P15, A.add), ts(T.v1c[:, 8:16], T.v1c[:, 0:8], 0.5, A.mult)],
+          ["pw", "pwa", "pw2", "lmc", "pp", "v1c"], [("cc", 16, 32), ("tc", 5, 6), "v1h"])
+        v([lambda: V.tensor_tensor_scan(T.cc[:, 0:11], T.cc[:, 16:27], T.cc[:, 16:27], 0.0, A.max, A.max), tc(T.dgt[:, 0:1], TC[5]), ts(T.dgt[:, 2:3], TC[5], 1.0, A.add)],
+          [("cc", 16, 32), ("tc", 5, 6)], [("cc", 0, 16), "dgl"])
+
+    def fill1():
+        v([ts(T.zd[:], T.n144[:], ZC, A.is_equal, WB, A.mult), ts(T.sl[:], T.snI[:], 1.0, A.add), ts(T.gik[:, 0:8], G8, P4, A.is_equal, BIG, A.mult), ts(T.gik[:, 8:16], G8, P4, A.is_equal, BIG / 2, A.mult),
+           ms(T.thr[:, 0:1], 9.0 * BIG), ts(T.gin[:, 0:8], G8, P4, A.is_equal, -1.0, A.mult), ts(T.gin[:, 8:16], G8, P4, A.is_equal, -FAR, A.mult), tc(T.ex[:], N16), ms(T.rz[:, 0:8], 0.0),
+           ts(T.dec[:, 8:16], G8, P4, A.is_equal, WB, A.mult), ts(TC[2], P15, 8.0, A.is_ge), ts(TC[3], P4, 8.0, A.mult, P15, A.add), ts(T.smi[:, 0:16], N16, 7, A.bitwise_and),
+           ts(T.smi[:, 16:17], T.pI[:, 0:1], 7, A.bitwise_and)], ["n144", "n16", "pp", "pI", "snI", ("col", 0, 1), ("cc", 0, 16)],
+          ["zd", "sl", "gik", ("thr", 0, 1), "gin", "ex", ("rz", 0, 8), ("dec", 8, 16), ("tc", 2, 4), "smi"])
+
+    def fill2():
+        v([tc(T.exg[:], T.smi[:, 0:16]), ts(T.ex8[:], G8, 2.0, A.mult, TC[2], A.add), ts(T.dgt[:, 4:5], TC[2], 56.0, A.mult, TC[3], A.add), ts(T.du[:], T.du[:], P15, A.add),
+           ts(TC[6], T.smi[:, 16:17], 1.0, A.add), ts(TC[7], T.smi[:, 16:17], 2.0, A.add, 8.0, A.mult), ts(TC[8], TC[2], float(EO[8]), A.mult, -1.0, A.add),
+           ts(T.tri[:], N16, P15, A.add, 15.5, A.is_lt), ms(T.mkg[:, 0:128], 1.0), ts(T.mkg[:, 128:384], T.lane[:], P15, A.is_equal)],
+          [("tc", 2, 4), "smi", "n16", "pp", "du", "lane"], ["exg", "ex8", "dg8", "du", ("tc", 6, 9), "tri", "mkg"])
+        v([ts(T.dgt[:, 6:7], TC[6], TC[7], A.mult, TC[8], A.add), ts(T.duw[:], T.du[:], float(DUMP - W1 + 1 - 2056), A.add)], [("tc", 6, 9), "du"], ["pick", "duw"])
+
+    def fill3():
+        z = zed(0, 3, 4, 5)
+        v([ms(T.wb[:, DUMP:GB], 0.0), ms(T.wb[:, GB + 769:W2B], 0.0), tc(T.wb[:, GB + 768:GB + 769], RB), ts(DB, PC, 8.0, A.is_lt, -64.0 * 1057, A.mult), ts(TC[9], lm(13), 1024.0, A.mult, WL, A.add)],
+          [("col", 4, 6), "pp", "lmc"], [("wb", DUMP, GB), ("wb", GB + 768, W2B), ("col", 7, 8), ("tc", 9, 10)])
+        z()
+        v(ts(T.dec[:, 0:8], G8, P4, A.is_equal, TC[9], A.mult), ["n16", "pp", ("tc", 9, 10)], [("dec", 0, 8)])
+
+    z12 = zed(1, 2)
     for l in range(3):
-        if l == 0:
-            fill[0][0]()
         own(0, l)
         jump(0, l, 0, "V")
         jump(0, l, 1, "S")
-        after(0, l)
-        for f in fill[l][(1 if l == 0 else 0):]:
-            f()
+        if l == 0:
+            z12()
+        if l == 2:
+            for b in (0, 2, 1):
+                weeks2(b)
+        join(l, 0)
+        if l == 2:
+            after(0, l)
+        join(l, 1)
         if l < 2:
+            after(0, l)
             sums(0, l, 0, "V")
             sums(0, l, 1, "S")
             pointers2(0, l + 1)
-            weeks(2 * l, False)
-            weeks(2 * l + 1, False)
+        (fill0, fill1, fill2)[l]()
+        for f, b in (((weeks, 1), (weeks, 3)), ((weeks, 2), (weeks2, 3)), ())[l]:
+            f(b)
+    weave(datelist())
 
-    def constants1():
-        v([ts(T.kI[:], T.n512[:, 0:256], 15, A.bitwise_and), ts(T.idF[:], N1, PC, A.is_equal), ts(T.nid[:], N1, PC, A.is_equal, -1.0, A.mult),
-           ts(T.gik[:, 0:8], G8, P4, A.is_equal, BIG, A.mult), ts(T.gik[:, 8:16], G8, P4, A.is_equal, BIG / 2, A.mult), ms(T.c8[:], 8 * BIG), ms(T.thr[:, 0:1], 9.0 * BIG)],
-          ["n144", "n512", "pp"], ["kI", "idF", "nid", "gik", "c8", ("thr", 0, 1)])
-        v(ts(T.segm[:], T.kI[:], 0.5, A.is_ge), ["kI"], ["segm"])
-
-    def constants2():
-        v([tc(T.lane[:], T.kI[:]), ts(T.mk[:], T.kI[:], P15, A.is_equal), ts(T.mkg[:, 0:128], K1, 0.0, A.is_ge), ts(T.mkg[:, 128:256], K1, P15, A.is_equal),
-           ts(T.gi16[:], G8, P4, A.is_equal), ts(T.gin[:], G8, P4, A.is_equal, -4096.0, A.mult), tc(T.ex[:], N16), ms(T.rz[:, 0:8], 0.0), ms(T.wg[:, 64:128], 0.0)],
-          ["kI", "pp", "n144"], ["lane", "mk", "mkg", "gi16", "gin", "ex", ("rz", 0, 8), ("wg", 64, 128)])
-        v([ts(T.tc[:, 3:4], P4, 8.0, A.mult, P15, A.add), ts(T.tc[:, 2:3], P15, 8.0, A.is_ge), ts(T.smi[:, 0:16], N16, 7, A.bitwise_and), ts(T.smi[:, 16:17], T.pI[:, 0:1], 7, A.bitwise_and),
-           ts(T.j16[:], N1, PC, A.add, 127.0, A.is_equal), ts(T.jF[:], N1, PC, A.add, 127.0, A.is_equal), ms(T.smk[:], 1.0), ts(T.du[:], T.du[:], P15, A.add)],
-          ["pp", "n144", "pI", "du"], ["tc", "smi", "j16", "jF", "smk", "du"])
-        v([tc(T.dgt[:, 4:5], T.tc[:, 3:4]), tc(T.exg[:], T.smi[:, 0:16]), ts(T.ex8[:], G8, 2.0, A.mult, T.tc[:, 2:3], A.add), ts(T.duw[:], T.du[:], float(DUMP - W1 + 1 - 2056), A.add),
-           ts(T.tc[:, 6:7], T.smi[:, 16:17], 1.0, A.add), ts(T.tc[:, 7:8], T.smi[:, 16:17], 2.0, A.add, 8.0, A.mult), ts(T.tc[:, 8:9], T.tc[:, 2:3], float(EO[8]), A.mult, -1.0, A.add)] +
-          [ts(T.smk[:, EO[b]:EO[b] + 16], N16, P15, A.add, 15.0, A.is_gt) for b in range(8)], ["tc", "smi", "n144", "pp", "du", "smk"], ["dg8", "exg", "ex8", "duw", "tc2", "smk"])
-        v([ts(T.dgt[:, 6:7], T.tc[:, 6:7], T.tc[:, 7:8], A.mult, T.tc[:, 8:9], A.add), zed(0), zed(3), zed(4), zed(5),
-           ts(T.dec[:, 0:8], G8, P4, A.is_equal, col(9), A.mult), ts(T.dec[:, 8:16], G8, P4, A.is_equal, T.cc[:, 10:11], A.mult), ts(DB, PC, 8.0, A.is_lt, -64.0 * 1057, A.mult)],
-          ["tc2", "n144", "col", "col2", "pp", ("cc", 0, 16)], ["pick", "zp", "dec", "dcb"])
-
-    def keys(w, t):
-        p(mm(T.pD[:, 0:16 * w], T.one[0:1, :], T.ck[:, 0:16 * w], False, True), ["one", "ck"], ["pD"])
+    def keys(w):
+        p(mm(T.pD[:, 0:16 * w], T.one[0:1, 0:128], T.ck[:, 0:16 * w], False, True), ["one", "ck"], ["pD"])
         v(lambda: V.tensor_tensor_scan(T.kx[:, 0:16 * w], T.segm[:, 0:16 * w], T.pD[:, 0:16 * w], 0.0, A.mult, A.max), ["segm", "pD"], ["kx"])
 
     def excess(w, t):
@@ -338,19 +370,24 @@ def rank_program(g, core, T, topo):
     def chosen(w):
         v(ts(T.ki[:, 16:16 + w], T.ki[:, 0:w], 4095, A.bitwise_and), [("ki", 0, 16)], [("ki", 16, 32)])
 
-    def eqdays(h):
+    def eqdays(h, q):
         o = EO[8] * h
-        v([ts(T.eq[:, o + EO[b]:o + EO[b + 1]], T.pH[:, 128 * h + 128 - EW[b]:128 * h + 128], T.pA[:, 8 * h + b:8 * h + b + 1], A.is_equal) for b in range(8)], ["pH", "pA"], [("eq", o, o + EO[8])])
+        row = [T.pH[:, 128 * h + 128 - EW[b]:128 * h + 128] for b in range(8)]
+        out = [T.eq[:, o + EO[b]:o + EO[b + 1]] for b in range(8)]
+        if q == "V":
+            v([ts(out[b], row[b], T.pA[:, 8 * h + b:8 * h + b + 1], A.not_equal, FAR, A.mult) for b in range(8)], ["pH", "pA"], [("eq", o, o + EO[8])])
+        else:
+            s([act(out[b], row[b], AF.Abs, T.sm[:, 48 + 8 * h + b:49 + 8 * h + b], -FAR) for b in range(8)], ["pH", ("sm", 48, 64)], [("eq", o, o + EO[8])])
 
     def scan(h):
         a = slice(EO[8] * h, EO[8] * h + EO[8])
-        v(lambda: V.tensor_tensor_scan(T.scn[:, a], T.eq[:, a], T.smk[:], 0.0, A.max, A.mult), [("eq", a.start, a.stop), "smk"], [("scn", a.start, a.stop)])
+        v(lambda: V.tensor_tensor_scan(T.scn[:, a], T.eq[:, a], T.smk[:], 0.0, A.min, A.max), [("eq", a.start, a.stop), "smk"], [("scn", a.start, a.stop)])
 
     def dayoffsets(w):
         return [
-            later("V", tt(T.sm[:, 0:16], T.scn[:].indirect(T.dgt[:, 6:7]), T.du[:], A.mult), ["scn", "pick", "du"], [("sm", 0, 16)]),
-            later("V", tt(T.sm[:, 16:16 + w], T.sm[:, 0:w], T.pA[:, 0:w], A.max), [("sm", 0, 16), "pA"], [("sm", 16, 32)]),
-            later("V", tc(T.u16s[:, 16:16 + w], T.sm[:, 16:16 + w]), [("sm", 16, 32)], [("u16s", 16, 32)])]
+            later("V", tt(T.sm[:, 0:16], T.scn[:].indirect(T.dgt[:, 6:7]), T.du[:], A.subtract), ["scn", "pick", "du"], [("sm", 0, 16)]),
+            later("V", tt(T.sm[:, 16:16 + w], T.sm[:, 0:w], T.pA[:, 0:w], A.min), [("sm", 0, 16), "pA"], [("sm", 16, 32)]),
+            later("V", ts(T.u16s[:, 16:16 + w], T.sm[:, 16:16 + w], -1.0, A.mult), [("sm", 16, 32)], [("u16s", 16, 32)])]
 
     def copies(q, src, sname, so, dst, n, ks):
         f = act if q == "S" else tc
@@ -360,9 +397,9 @@ def rank_program(g, core, T, topo):
         a = slice(16 * c0, 16 * c0 + 16 * n)
         v(tt(T.cmp[:, a], T.sd[:, 0:2049].indirect(T.cg[:, c0:c0 + n]), T.xr[:, a], A.is_lt), [("sd", 0, 2049), "cg", ("xrS", a.start, a.stop), ("xrV", a.start, a.stop)], [("cmp", a.start, a.stop)])
 
-    def count(c0, n, stop=False):
+    def count(c0, n):
         o = 128 * (c0 // 128)
-        p([mm(T.pD[c0 % 128:c0 % 128 + n, o + k:o + 128:16], T.cmp[:, 16 * c0 + k:16 * c0 + 16 * n:16], T.gik[:, 0:8], False, stop and k == 15) for k in range(16)],
+        p([mm(T.pD[c0 % 128:c0 % 128 + n, o + k:o + 128:16], T.cmp[:, 16 * c0 + k:16 * c0 + 16 * n:16], T.gik[:, 0:8], False, False) for k in range(16)],
           [("cmp", 16 * c0, 16 * c0 + 16 * n), "gik"], ["pD"])
 
     def fetch(c0):
@@ -373,15 +410,15 @@ def rank_program(g, core, T, topo):
             p([f for k in range(8) for f in (mm(T[BK[h]][:, 64 * k:64 * k + 64], T.idb[:], src[:, so:so + 64], True, False),
                                               mm(T[BK[h]][:, 64 * k:64 * k + 64], T.nid[:], T.sgb[:, 8 * h + k:1024:16], False, True))], [(sname, so, so + 64), "sgb", "idb", "nid"], [BK[h]])
 
-    def signs(c0, stop=False):
+    def signs(c0):
         o = 128 * (c0 // 128)
         for h in (0, 1):
             s(act(T.sgn[:, 512 * h:512 * h + 512], T[BK[h]][:], AF.Sign, -TINY), [BK[h]], [("sgn", 512 * h, 512 * h + 512)])
-            p([mm(T.pD[64:128, o + k:o + 128:16], T.sgn[:, 64 * k:64 * k + 64], T.gik[:, 8:16], False, stop and k == 15) for k in range(8 * h, 8 * h + 8)],
+            p([mm(T.pD[64:128, o + k:o + 128:16], T.sgn[:, 64 * k:64 * k + 64], T.gik[:, 8:16], False, False) for k in range(8 * h, 8 * h + 8)],
               [("sgn", 512 * h, 512 * h + 512), "gik"], ["pD"])
 
     def open_keys(w, signed):
-        f = [mm(T.pD[:, 0:16 * w], T.one[0:1, :], T.ck[:, 0:16 * w], True, False)]
+        f = [mm(T.pD[:, 0:16 * w], T.one[0:1, 0:128], T.ck[:, 0:16 * w], True, False)]
         if signed:
             f.append(mm(T.pD[64:128, 16 * w - 128:16 * w], T.one[0:1, 0:64], T.c8[:], False, False))
         p(f, ["one", "ck", "c8"], ["pD"])
@@ -389,51 +426,54 @@ def rank_program(g, core, T, topo):
     for t in range(RO):
         last = t == RO - 1
         a1 = (t + 1) % 2
-        gxa, gda, gha = (128 * t, 128 * t + 128), (16 * t, 16 * t + 8), (768 * t, 768 * t + 768)
+        gxa, gla, gda, gha = (128 * t, 128 * t + 128), (16 * t, 16 * t + 8), (16 * t + 8, 16 * t + 16), (768 * t, 768 * t + 768)
         to, fro = (rank + 1 + t % (N - 1)) % N, (rank - 1 - t % (N - 1)) % N
-        v(tc(T.ldI[:], T.pG[:, 0:64]), ["pG"], ["ldI"])
-        v(ts(T.ldI[:], T.ldI[:], 2047, A.bitwise_and), ["ldI"], ["ldI"])
-        v(ts(T.lfd[:], T.ldI[:], 1.0, A.add), ["ldI"], ["lfd"])
+
+        def ghosts(d):
+            a, b = gha[0] + 256 * (d - 1), GH[a1] + 256 * (d - 1)
+            s(act(T.ghs[:, a:a + 256], T.t8[:, 0:1025].indirect(T.sl[:, 16 * d - 16:16 * d])), [("t8", 0, 1025), "sl"], [("ghs", a, a + 256)])
+            send((rank + d) % N, T.wb[:, b:b + 256], T.ghs[:, a:a + 256], [("ghs", a, a + 256)], "gh%d" % t)
+            if d == 1:
+                landed(("wb", GH[a1], GH[a1] + 768), "gh%d" % t, sum(len(topo.engines(cores[(rank - e) % N], core)) for e in range(1, N)))
+
+        def cands(h):
+            s(act(T.cv[:, 1 + 512 * h:513 + 512 * h], T.cw[:, 0:2049].indirect(T.lfd[:, 32 * h:32 * h + 32])), ["cw", "lfd"], [("cv", 1 + 512 * h, 513 + 512 * h)])
+
+        if 0 < t < RO - 1:
+            ghosts(2)
+            ghosts(3)
+        p(mm(T.pH[:, 0:256], T.idb[:], T.xw[:, 769:1025], True, False), ["idb", ("xw", 1, 1025)], ["pH"])
+        s(act(T.sgb[:, 0:256], T.sd[:, 0:2049].indirect(T.lfd[:, 48:64])), [("sd", 0, 2049), "lfd"], ["sgb"])
+        p(mm(T.pH[:, 0:256], T.nid[:], T.sgb[:, 0:256], False, True), ["nid", "sgb"], ["pH"])
         if t == 0:
-            for b in range(4):
-                weeks(b, True)
+            sums(0, 2, 0)
+        elif not last:
+            ghosts(1)
+        s(act(T.sgn[:, 0:256], T.pH[:, 0:256], AF.Sign, TINY), ["pH"], [("sgn", 0, 512)])
+        cands(0)
         for h in (0, 1):
-            if t > 0:
-                s(act(T.cv[:, 1 + 512 * h:513 + 512 * h], T.cw[:, 0:2049].indirect(T.lfd[:, 32 * h:32 * h + 32])), ["cw", "lfd"], [("cv", 1 + 512 * h, 513 + 512 * h)])
-            v(tt(T.cmp[:, 512 * h:512 * h + 512], T.sd[:, 0:2049].indirect(T.lfd[:, 32 * h:32 * h + 32]), T.xw[:, 1 + 512 * h:513 + 512 * h], A.is_le),
-              [("sd", 0, 2049), "lfd", ("xw", 1, 1025)], [("cmp", 512 * h, 512 * h + 512)])
-            p([mm(T.pA[:, 8 * c:8 * c + 8], T.cmp[:, 128 * c:128 * c + 128], T.gib[:]) for c in range(4 * h, 4 * h + 4)], [("cmp", 512 * h, 512 * h + 512), "gib"], ["pA"])
-        if t > 0:
-            sums(t % 2, 2, 0)
+            a = slice(384 * h, 384 * h + 384)
+            v(tt(T.cmp[:, a], T.sd[:, 0:2049].indirect(T.lfd[:, 24 * h:24 * h + 24]), T.xw[:, 1 + a.start:1 + a.stop], A.is_le), [("sd", 0, 2049), "lfd", ("xw", 1, 1025)], [("cmp", a.start, a.stop)])
+            if h == 1:
+                p([f for c in (0, 1) for f in (mm(T.pA[:, 48 + 8 * c:56 + 8 * c], T.one[0:1, 0:128], T.c8b[0:1, 0:8], True, False),
+                                               mm(T.pA[:, 48 + 8 * c:56 + 8 * c], T.sgn[:, 128 * c:128 * c + 128], T.gib[:, 8:16], False, True))], [("sgn", 0, 512), "gib", "one", "c8b"], ["pA"])
+            p([mm(T.pA[:, 8 * c:8 * c + 8], T.cmp[:, 128 * c:128 * c + 128], T.gib[:, 0:8]) for c in range(3 * h, 3 * h + 3)], [("cmp", a.start, a.stop), "gib"], ["pA"])
         v(ts(T.bz[:, 56:120], T.pA[:, 0:64], 4.5, A.is_lt), ["pA"], [("bz", 56, 120)])
-        p([mm(T.pB[:, 0:64], T.upr[:], T.bz[:, 56:120], True, False)] + [mm(T.pB[:, 0:64], T.one[:], T.bz[:, 56 - 8 * q:120 - 8 * q], False, q == 7) for q in range(1, 8)],
+        p([mm(T.pB[:, 0:64], T.upr[:, 0:128], T.bz[:, 56:120], True, False)] + [mm(T.pB[:, 0:64], ONE, T.bz[:, 56 - 8 * q:120 - 8 * q], False, q == 7) for q in range(1, 8)],
           ["upr", "one", "bz"], ["pB"])
         v(tc(T.rkI[:], T.pB[:, 0:64]), ["pB"], ["rkI"])
         s([act(T.th[:, c::17], T.pB[:, 0:64], AF.Sign, 16.0 * c - 4096.5, -1.0) for c in range(17)], ["pB"], ["th"])
         v(ts(T.loI[:], T.rkI[:], 15, A.bitwise_and), ["rkI"], ["loI"])
-        v([ts(T.oa[:, i::16], T.loI[:], float(i), A.is_equal) for i in range(16)], ["loI"], ["oa"])
+        v([ts(T.lo2[:, k::2], T.loI[:], -8.0 * k, A.add) for k in (0, 1)], ["loI"], ["lo2"])
+        v([ts(T.oa[:, i::8], T.lo2[:], float(i), A.is_equal) for i in range(8)], ["lo2"], ["oa"])
         for c in range(8):
             a = slice(128 * c, 128 * c + 128)
             v(ts(T.oa[:, a], T.oa[:, a], T.v1c[:, 8 + c:9 + c], A.mult), [("oa", a.start, a.stop), "v1h"], [("oa", a.start, a.stop)])
             p(mm(T.pC[:, 0:136], T.oa[:, a], T.th[:, 136 * c:136 * c + 136], c == 0, c == 7), [("oa", a.start, a.stop), "th"], ["pC"])
+        cands(1)
         if t == 0:
-            for h in (0, 1):
-                s(act(T.cv[:, 1 + 512 * h:513 + 512 * h], T.cw[:, 0:2049].indirect(T.lfd[:, 32 * h:32 * h + 32])), ["cw", "lfd"], [("cv", 1 + 512 * h, 513 + 512 * h)])
-            sums(0, 2, 0, "V")
-            sums(0, 2, 1, "V")
-            constants1()
-        else:
-            sums(t % 2, 2, 1)
-
-        def ghosts():
-            s(act(T.ghs[:, gha[0]:gha[1]], T.t8[:, 0:1025].indirect(T.sl[:])), [("t8", 0, 1025), "sl"], [("ghs",) + gha])
-            for d in range(1, N):
-                a, b = gha[0] + 256 * (d - 1), GH[a1] + 256 * (d - 1)
-                send((rank + d) % N, T.wb[:, b:b + 256], T.ghs[:, a:a + 256], [("ghs", a, a + 256)], "gh%d" % t)
-            landed(("wb", GH[a1], GH[a1] + 768), "gh%d" % t, sum(len(topo.engines(cores[(rank - d) % N], core)) for d in range(1, N)))
-
-        if 0 < t < RO - 1:
-            ghosts()
+            sums(0, 2, 1)
+            ghosts(2)
         v(tc(T.win[:, 0:136], T.pC[:, 0:136]), ["pC"], ["win"])
         v(tc(T.g16[:], T.win[:, 0:136].indirect(T.dgt[:, 0:1])), ["win", "dgl"], ["g16"])
         v(tt(T.lvf[:], T.win[:, 0:136].indirect(T.dgt[:, 2:3]), T.g16[:], A.subtract), ["win", "dgl", "g16"], ["lvf"])
@@ -446,115 +486,130 @@ def rank_program(g, core, T, topo):
         fetch(192)
         differ(T.xg, "xg", 193)
         copies("S", T.xg, "xg", 129, 2048, 64, range(0, 16))
+        if t == 0:
+            ghosts(3)
+            ghosts(1)
         compare(0, 128)
         count(0, 128)
         signs(192)
         s(act(T.cgf[:], T.cv[:, 0:1025].indirect(T.lv[:])), ["cv", "lv"], ["cgf"])
         p([mm(T.pD[:, 128 * q:128 * q + 128], T.cgf[:, 128 * q:128 * q + 128], T.idF[:], False, False) for q in (0, 1)], ["cgf", "idF"], ["pD"])
+        s(act(T.db[:], T.t8[:, 0:1025].indirect(T.lv[:])), [("t8", 0, 1025), "lv"], ["db"])
+        p([mm(T.pB[:, 32 + 8 * q:40 + 8 * q], T.db[:, 128 * q:128 * q + 128], T.dec[:, 8:16]) for q in (0, 1)], ["db", ("dec", 8, 16)], ["pB"])
         compare(128, 64)
         count(128, 64)
-        s(act(T.db[:, 1:257], T.t8[:, 0:1025].indirect(T.lv[:])), [("t8", 0, 1025), "lv"], [("db", 1, 257)])
         if t == 0:
-            ghosts()
-            constants2()
-        keys(16, t)
-        v([excess(16, t), ts(T.rz[:, 8:24], T.kx[:, 15:256:16], T.thr[:, t % 2:t % 2 + 1], A.is_lt)], ["kx", ("thr", t % 2, t % 2 + 1)], [("ki", 0, 16), ("rz", 8, 24)])
-        p([mm(T.pB[:, 0:16], T.upr[:], T.rz[:, 8:24], True, False), mm(T.pB[:, 0:16], T.one[:], T.rz[:, 0:16], False, True)], ["upr", "one", "rz"], ["pB"])
+            s([act(T.jF[:], T.jb[:])] + [act(T.smk[:, EO[b]:EO[b] + 16], T.tri[:], AF.Copy, 0.0, FAR) for b in range(8)], ["jb", "tri", "smk0"], ["jF", "smk"])
+            fill3()
+        v(tc(T.dI[:, 0:16], T.pB[:, 32:48]), ["pB"], [("dI", 0, 16)])
+        v(ts(T.dI[:, 16:32], T.dI[:, 0:16], 2047, A.bitwise_and), [("dI", 0, 16)], [("dI", 16, 32)])
+        keys(16)
+        v([ts(T.rz[:, 8:24], T.kx[:, 15:256:16], T.thr[:, t % 2:t % 2 + 1], A.is_lt), excess(16, t)], ["kx", ("thr", t % 2, t % 2 + 1)], [("ki", 0, 16), ("rz", 8, 24)])
+        p([mm(T.pB[:, 0:16], T.upr[:, 0:128], T.rz[:, 8:24], True, False), mm(T.pB[:, 0:16], ONE, T.rz[:, 0:16], False, True)], ["upr", "one", "rz"], ["pB"])
+        if not last:
+            p([mm(T.pG[:, 64:65], ONE, T.rz[:, 8 + c:9 + c], c == 0, c == 15) for c in range(16)], ["one", "rz"], ["pG"])
         chosen(16)
         s(act(T.xf[:], T.ki[:, 16:32].indirect(T.ex[:])), [("ki", 16, 32), "ex"], ["xf"])
         v(tc(T.rkI[:, 0:16], T.pB[:, 0:16]), ["pB"], ["rkI"])
-        v(tt(T.xe[:], T.ki[:, 16:32].indirect(T.ex[:]), T.mk[:], A.mult), [("ki", 16, 32), "ex", "mk"], ["xe"])
-        p([mm(T.pA[:, 8 * q:8 * q + 8], T.xe[:, 128 * q:128 * q + 128], T.gi16[:]) for q in (0, 1)] + [mm(T.pA[:, 16:32], T.id16[:], T.duw[:], True, False)] +
-          [mm(T.pA[:, 16 + 8 * q:24 + 8 * q], T.xe[:, 128 * q:128 * q + 128], T.gin[:], False, q == 1) for q in (0, 1)], ["xe", "gi16", "gin", "id16", "duw"], ["pA"])
+        v(tt(T.xe[:], T.ki[:, 16:32].indirect(T.ex[:]), T.mkg[:, 128:384], A.mult), [("ki", 16, 32), "ex", "mkg"], ["xe"])
+        p([mm(T.pA[:, 8 * q + 32 * k:8 * q + 8 + 32 * k], T.xe[:, 128 * q:128 * q + 128], T.gin[:, 8 * k:8 * k + 8]) for k in (0, 1) for q in (0, 1)] +
+          [f for q in (0, 1) for f in (mm(T.pA[:, 16 + 8 * q:24 + 8 * q], T.idb[:], T.duw[:, 8 * q:8 * q + 8], True, False),
+                                       mm(T.pA[:, 16 + 8 * q:24 + 8 * q], T.xe[:, 128 * q:128 * q + 128], T.gin[:, 8:16], False, True))], ["xe", "gin", "idb", "duw"], ["pA"])
+        p([mm(T.pH[:, 128 * q:128 * q + 128], T.xf[:, 128 * q:128 * q + 128], T.jF[:]) for q in (1, 0)], ["xf", "jF"], ["pH"])
         v([ts(T.loI[:, 0:16], T.rkI[:, 0:16], 15, A.bitwise_and), ts(T.hiI[:, 0:16], T.rkI[:, 0:16], 4, A.arith_shift_right)], ["rkI"], ["loI", "hiI"])
-        v(tt(T.oa[:, 0:256], T.loI[:, 0:16].indirect(T.ex[:]), T.lane[:], A.is_equal), ["loI", "ex", "lane"], [("oa", 0, 256)])
-        v([ts(T.u16s[:, 32:48], T.pA[:, 0:16], -1.0, A.add), tt(T.sm[:, 32:48], T.pA[:, 16:32], T.lvf[:], A.max)], ["pA", "lvf"], [("u16s", 32, 48), ("sm", 32, 48)])
-        s(act(T.wv[:], T.tab[:].indirect(T.u16s[:, 32:48]), AF.Identity, RB, MB), ["tab", ("u16s", 32, 48), "col"], ["wv"])
-        p([mm(T.pH[:, 128 * q:128 * q + 128], T.xf[:, 128 * q:128 * q + 128], T.jF[:]) for q in (0, 1)], ["xf", "jF"], ["pH"])
         v(tt(T.ob[:], T.hiI[:, 0:16].indirect(T.ex8[:]), T.ct8[:], A.is_equal), ["hiI", "ex8", "ct8"], ["ob"])
-        v([ts(T.oa[:, 256 + 128 * q:384 + 128 * q], T.oa[:, 128 * q:128 * q + 128], T.v1c[:, q:q + 1], A.mult) for q in (0, 1)], [("oa", 0, 256), "v1c"], [("oa", 256, 512)])
-        p([mm(T.pC[:, 0:64], T.oa[:, 256 + 128 * q:384 + 128 * q], T.ob[:, 64 * q:64 * q + 64], q == 0, q == 1) for q in (0, 1)], [("oa", 256, 512), "ob"], ["pC"])
-        v(tc(T.u16s[:, 0:16], T.sm[:, 32:48]), [("sm", 32, 48)], [("u16s", 0, 16)])
-        v(tc(T.wg[:, 0:64], T.pC[:, 0:64]), ["pC"], [("wg", 0, 64)])
-        v(tc(T.gl[:], T.wg[:].indirect(T.dgt[:, 4:5])), ["wg", "dg8"], ["gl"])
-        s(act(T.dgh[:], T.db[:, 0:257].indirect(T.gl[:, 0:8])), ["db", "gl"], ["dgh"])
-        conv(T.pC[:, 128:136], "pC", T.dgh, "dgh", 0, 8, "zd", 0)
-        s(act(T.gxs[:, gxa[0]:gxa[1]], T.xg[:, 0:257].indirect(T.gl[:, 0:8])), ["xg", "gl"], [("gxs",) + gxa])
+        v([ts(T.u16s[:, 32:48], T.pA[:, 0:16], -1.0, A.mult, -1.0, A.add), tc(T.sm[:, 48:64], T.pA[:, 32:48]), tt(T.sm[:, 32:48], T.pA[:, 16:32], T.lvf[:], A.max)],
+          ["pA", "lvf"], [("u16s", 32, 48), ("sm", 32, 64)])
+        s([act(T.obj[:, 64 * q:64 * q + 64], T.ob[:, 64 * q:64 * q + 64], AF.Copy, 0.0, T.v1c[:, q:q + 1]) for q in (0, 1)], ["ob", "v1c"], ["obj"])
+        s(act(T.wv[:], T.tab[:].indirect(T.u16s[:, 32:48]), AF.Identity, RB, MB), ["tab", ("u16s", 32, 48), ("col", 1, 5)], ["wv"])
+        v([tt(T.oa[:, 256:384], T.dI[:, 16:32].indirect(T.ex8[:]), T.ob[:], A.mult), tt(T.oa[:, 0:256], T.loI[:, 0:16].indirect(T.ex[:]), T.lane[:], A.is_equal)],
+          ["loI", "ex", "lane", ("dI", 16, 32), "ex8", "ob"], [("oa", 0, 384)])
+        rhs = (T.ob[:, 0:64], T.ob[:, 64:128], T.oa[:, 256:320], T.oa[:, 320:384])
+        p([mm(T.pC[:, 0:64], T.oa[:, 128 * q:128 * q + 128], T.obj[:, 64 * q:64 * q + 64], q == 0, q == 1) for q in (0, 1)] +
+          [mm(T.pC[:, 64:128], T.oa[:, 128 * (q % 2):128 * (q % 2) + 128], rhs[q], q == 0, q == 3) for q in range(4)], [("oa", 0, 384), "ob", "obj"], ["pC"])
+        eqdays(1, "S")
+        v([tc(T.u16s[:, 0:16], T.sm[:, 32:48])] + ([] if last else [tc(T.smi[:, 16:17], T.pG[:, 64:65])]), [("sm", 32, 48), "pG"], [("u16s", 0, 16), ("smi", 16, 17)])
+        v(tc(T.wg[:], T.pC[:, 0:128]), ["pC"], ["wg"])
+        v(tc(T.gds[:, gla[0]:gda[1]], T.wg[:].indirect(T.dgt[:, 4:5])), ["wg", "dg8"], [("gds", gla[0], gda[1])])
+        s(act(T.gxs[:, gxa[0]:gxa[1]], T.xg[:, 0:257].indirect(T.gds[:, gla[0]:gla[1]])), ["xg", ("gds",) + gla], [("gxs",) + gxa])
+        send(to, T.gdl[:, gda[0]:gda[1]], T.gds[:, gda[0]:gda[1]], [("gds",) + gda], "gd%d" % t)
         send(to, T.gxl[:, gxa[0]:gxa[1]], T.gxs[:, gxa[0]:gxa[1]], [("gxs",) + gxa], "gx%d" % t)
+        ne = len(topo.engines(cores[fro], core))
+        landed(("gxl",) + gxa, "gx%d" % t, ne)
+        landed(("gdl",) + gda, "gd%d" % t, ne)
+        eqdays(0, "S")
         v(lambda: V.tensor_copy(T.wb[:, W1 - 1:DUMP + 256].indirect(T.u16s[:, 0:16]), T.wv[:]), ["wv", ("u16s", 0, 16)], [("wb", W1 - 1, DUMP + 256)])
         if last:
             for h in (0, 1):
                 p(mm(T[BK[h]][0:16, :], T.dec[:], T.wb[:, W1 + 512 * h:W1 + 512 * h + 512]), ["dec", ("wb", W1, DUMP)], [BK[h]])
-                s(act(T.yb[0:16, 512 * h:512 * h + 512], T[BK[h]][0:16, :], AF.Identity, T.col[0:16, 7:8]), [BK[h], "dcb"], [("yb", 512 * h, 512 * h + 512)])
+                s(act(T.yb[0:16, 512 * h:512 * h + 512], T[BK[h]][0:16, :], AF.Identity, T.col[0:16, 7:8]), [BK[h], ("col", 7, 8)], [("yb", 512 * h, 512 * h + 512)])
             copy("Y", T.yan[:], T.yb[0:8, :], ["yb"], [])
             copy("Y", T.yof[:], T.yb[8:16, :], ["yb"], [])
         else:
             pointers(a1, 0, T.wb, "wb", W1)
             own(a1, 0)
-            p([mm(T.pB[:, 64:65], T.one[:], T.rz[:, 8 + c:9 + c], c == 0, c == 15) for c in range(16)], ["one", "rz"], ["pB"])
-        weave([later("V", tc(T.smi[:, 0:8], T.pC[:, 128:136]), ["pC"], [("smi", 0, 8)]),
-               later("V", ts(T.smi[:, 8:16], T.smi[:, 0:8], 2047, A.bitwise_and), [("smi", 0, 8)], [("smi", 8, 16)]),
-               later("V", ts(T.gds[:, gda[0]:gda[1]], T.smi[:, 8:16], 1.0, A.add), [("smi", 8, 16)], [("gds",) + gda])],
-              [lambda: eqdays(1)] + ([] if last else [lambda: pointers2(a1, 0)]))
-        send(to, T.gdl[:, gda[0]:gda[1]], T.gds[:, gda[0]:gda[1]], [("gds",) + gda], "gd%d" % t)
-        ne = len(topo.engines(cores[fro], core))
-        landed(("gxl",) + gxa, "gx%d" % t, ne)
-        landed(("gdl",) + gda, "gd%d" % t, ne)
-        if not last:
-            jump(a1, 0, 0)
-            jump(a1, 0, 1)
-            after(a1, 0)
-            sums(a1, 0, 0)
-            sums(a1, 0, 1)
-            own(a1, 1)
-        eqdays(0)
         scan(1)
         scan(0)
-        hh = [] if last else [later("V", tc(T.smi[:, 16:17], T.pB[:, 64:65]), ["pB"], [("smi", 16, 17)]),
-                              later("V", ts(T.smi[:, 17:18], T.smi[:, 16:17], 1, A.bitwise_and), [("smi", 16, 17)], [("smi", 17, 18)]),
-                              later("V", ts(T.thr[:, a1:a1 + 1], T.smi[:, 17:18], BIG, A.mult, 9.0 * BIG, A.add), [("smi", 17, 18)], [("thr", a1, a1 + 1)])]
+        hh = [] if last else [lambda: pointers2(a1, 0), later("V", ts(T.smi[:, 17:18], T.smi[:, 16:17], 1, A.bitwise_and), [("smi", 16, 17)], [("smi", 17, 18)])]
         weave(dayoffsets(16), hh)
+        if not last:
+            for h in (0, 1):
+                jump(a1, 0, h)
+                join(0, h)
+            after(a1, 0)
         v(lambda: V.tensor_copy(T.sd[:, 0:2320].indirect(T.u16s[:, 24:32]), T.xg[:, 129:257]), [("xg", 1, 257), ("u16s", 16, 32)], ["sd"])
         if not last:
-            pointers2(a1, 1)
+            v(ts(T.thr[:, a1:a1 + 1], T.smi[:, 17:18], BIG, A.mult, 9.0 * BIG, A.add), [("smi", 17, 18)], [("thr", a1, a1 + 1)])
         v(lambda: V.tensor_copy(T.sd[:, 0:2320].indirect(T.u16s[:, 16:24]), T.xg[:, 1:129]), [("xg", 1, 257), ("u16s", 16, 32)], ["sd"])
         gl = T.gdl[:, gda[0]:gda[1]]
-        open_keys(8, last)
+        open_keys(8, False)
+        v(tc(T.cg[:, 0:128], T.cw[:, 0:2049].indirect(gl)), ["cw", ("gdl",) + gda], ["cg"])
         if last:
-            copies("S", T.gxl, "gxl", gxa[0], 0, 64, range(0, 16))
-            v(tc(T.cg[:, 0:128], T.cw[:, 0:2049].indirect(gl)), ["cw", ("gdl",) + gda], ["cg"])
-            fetch(64)
-            differ(T.gxl, "gxl", gxa[0] + 64)
+            copies("S", T.gxl, "gxl", gxa[0], 0, 64, range(0, 8))
+            copies("V", T.gxl, "gxl", gxa[0], 0, 64, range(8, 16))
+            copies("S", T.gxl, "gxl", gxa[0] + 64, 1024, 64, range(0, 16))
             s(act(T.cgf[:, 0:128], T.cw[:, 0:2049].indirect(gl)), ["cw", ("gdl",) + gda], ["cgf"])
-            compare(0, 64)
-            count(0, 64)
             p(mm(T.pD[:, 0:128], T.cgf[:, 0:128], T.idF[:], False, False), ["cgf", "idF"], ["pD"])
-            signs(64)
+            for c in (0, 64):
+                compare(c, 64)
+                count(c, 64)
         else:
-            jump(a1, 1, 0)
-            jump(a1, 1, 1)
-            after(a1, 1)
             copies("V", T.gxl, "gxl", gxa[0], 0, 128, range(0, 16))
-            v(tc(T.cg[:, 0:128], T.cw[:, 0:2049].indirect(gl)), ["cw", ("gdl",) + gda], ["cg"])
+            sums(a1, 0, 0)
+            sums(a1, 0, 1)
+            pointers2(a1, 1)
+            own(a1, 1)
+            s(act(T.cgf[:, 0:128], T.cw[:, 0:2049].indirect(gl)), ["cw", ("gdl",) + gda], ["cgf"])
+            p(mm(T.pD[:, 0:128], T.cgf[:, 0:128], T.idF[:], False, False), ["cgf", "idF"], ["pD"])
+            compare(0, 64)
+            jump(a1, 1, 0)
+            join(1, 0)
+            jump(a1, 1, 1)
+            count(0, 64)
+            join(1, 1)
+            after(a1, 1)
+            compare(64, 64)
             sums(a1, 1, 0)
             sums(a1, 1, 1)
             pointers2(a1, 2)
+            count(64, 64)
+        keys(8)
+        if not last:
             own(a1, 2)
-            s(act(T.cgf[:, 0:128], T.cw[:, 0:2049].indirect(gl)), ["cw", ("gdl",) + gda], ["cgf"])
-            p(mm(T.pD[:, 0:128], T.cgf[:, 0:128], T.idF[:], False, False), ["cgf", "idF"], ["pD"])
-            compare(0, 128)
             jump(a1, 2, 0)
-            count(0, 128)
+            join(2, 0)
             jump(a1, 2, 1)
-            after(a1, 2)
-        keys(8, t)
+            sums(a1, 2, 0)
         v(excess(8, t), ["kx", ("thr", t % 2, t % 2 + 1)], [("ki", 0, 16)])
         chosen(8)
-        v(tt(T.xe[:], T.ki[:, 16:24].indirect(T.exg[:]), T.mkg[:], A.mult), [("ki", 16, 32), "exg", "mkg"], ["xe"])
-        p([mm(T.pA[:, 0:8], T.xe[:, 128:256], T.gi16[:]), mm(T.pH[:, 0:128], T.xe[:, 0:128], T.j16[:])], ["xe", "gi16", "j16"], ["pA", "pH"])
-        eqdays(0)
-        scan(0)
-        weave(dayoffsets(8))
+        v(tt(T.xe[:], T.ki[:, 16:24].indirect(T.exg[:]), T.mkg[:, 0:256], A.mult), [("ki", 16, 32), "exg", "mkg"], ["xe"])
+        p([mm(T.pA[:, 0:8], T.xe[:, 128:256], T.gin[:, 0:8]), mm(T.pH[:, 0:128], T.xe[:, 0:128], T.jb[:])], ["xe", "gin", "jb"], ["pA", "pH"])
+        if not last:
+            after(a1, 2)
+            join(2, 1)
+            sums(a1, 2, 1)
+        eqdays(0, "V")
+        weave([] if last else datelist(), [lambda: scan(0)] + dayoffsets(8))
         v(lambda a=gxa[0]: V.tensor_copy(T.sd[:, 0:2320].indirect(T.u16s[:, 16:24]), T.gxl[:, a:a + 128]), [("gxl",) + gxa, ("u16s", 16, 32)], ["sd"])
     copy("Y", T.ys[:], T.sd[:, 1:2049], ["sd"], [])
     finish([("ls", sent[0])])

@@ -15,18 +15,20 @@ SB = {
     "anI": (64, I), "ofI": (112, I), "snI": (48, I), "wkb": (2048, B), "xw": (1040, B), "sd": (2320, B),
     "pI": (3, I), "pp": (3, F), "n16": (16, I), "n144": (144, B), "lmc": (16, F), "pw": (16, F), "cc": (32, F), "col": (24, F), "hi16": (16, F), "tc": (16, F),
     "tab": (2048, B), "idb": (128, B), "idF": (128, F), "jF": (128, F), "jb": (128, B), "upr": (256, B), "amb": (128, B), "nid": (128, B),
-    "one": (256, B), "seven": (128, B), "m1k": (128, B), "gin": (16, B), "gib": (16, B), "gik": (16, B), "zp": (864, H), "zd": (144, H), "dec": (16, B),
-    "mkg": (384, B), "lane": (256, B), "segm": (256, B), "ct8": (128, B), "ex": (16, U), "exg": (16, U), "ex8": (8, U), "dgt": (8, U), "v1c": (16, F),
-    "smk": (576, B), "tri": (16, F), "du": (16, F), "duw": (16, H), "anl": (64, U), "ofl": (112, U), "an1": (128, F),
+    "one": (128, B), "seven": (128, B), "m1k": (128, B), "gin": (24, B), "gib": (16, B), "gik": (16, B), "zp": (864, H), "zd": (144, H), "dec": (16, B),
+    "mkg": (384, B), "lane": (256, B), "segm": (128, B), "ct8": (128, B), "ex": (16, U), "exg": (16, U), "ex8": (8, U), "dgt": (8, U), "v1c": (16, F),
+    "smk": (576, B), "tri": (16, F), "du": (16, F), "duw": (48, H), "anl": (64, U), "ofl": (112, U), "an1": (128, F),
     "wb": (WEND, B), "g0": (1024, B), "g1": (1024, B), "t8": (1040, B), "l0": (64, U), "l1": (64, U), "l2": (64, U), "sl": (48, U), "cw": (2056, F), "sg": (2048, B),
-    "ldI": (128, I), "lfd": (64, U), "cv": (1032, F), "cmp": (3072, B), "xr": (3072, B), "sgb": (1024, B), "sgn": (1024, B), "bz": (120, B), "rz": (24, B), "rkI": (64, I), "loI": (64, I), "hiI": (16, I), "lo2": (128, B), "obj": (128, B), "c8b": (16, B),
+    "ldI": (128, I), "lfd": (64, U), "cv": (1032, F), "cmp": (3072, B), "xr": (3072, B), "sgb": (1536, B), "sgn": (1536, B), "bz": (120, B), "rz": (24, B), "rkI": (64, I), "loI": (64, I), "hiI": (16, I), "lo2": (128, B), "obj": (128, B), "c8b": (8, B),
     "oa": (1024, H), "ob": (128, B), "th": (1088, B), "win": (144, F), "wg": (128, F), "g16": (16, F), "lv": (16, U), "lvf": (16, F),
     "xg": (272, B), "cg": (256, U), "cgf": (256, F), "db": (256, B), "dI": (32, I), "kx": (256, F), "ki": (32, I), "sm": (64, F), "smi": (32, I), "u16s": (64, U),
     "thr": (2, F), "xe": (256, H), "xf": (256, F), "wv": (256, B), "eq": (1152, B), "scn": (1152, B), "yb": (1024, F),
     "ghs": (2304, B), "gxs": (512, B), "gxl": (512, B), "gds": (64, U), "gdl": (64, U),
 }
 SCRATCH = {k: ("sbuf", [128, n], d) for k, (n, d) in SB.items()}
-SCRATCH.update({"ck": ("sbuf", [1, 256], B), "c8": ("sbuf", [1, 128], B), "n256": ("sbuf", [1, 512], B)})
+SCRATCH.update({"ck": ("sbuf", [1, 128], B), "c8": ("sbuf", [1, 128], B), "up64": ("sbuf", [1, 128], B), "nil": ("sbuf", [1, 128], B), "n256": ("sbuf", [1, 512], B)})
+LISTS = [k for k, (n, d) in SB.items() if d == U] + ["dgl", "dg8", "pick"]
+GATHER, SCATTER, PE, WAKE, LOAD, FLIGHT, PASSES = 1.56, 3.5, 0.55, 100, 2500, 2500, 4
 PS = ("pA", "pB", "pC", "pD", "pE", "pF", "pG", "pH")
 SCRATCH.update({k: ("psum", [128, 512], F) for k in PS})
 SEMAPHORES = ["qV", "qS", "qP", "qG", "ls"] + ["d%d" % i for i in range(11)] + ["gh%d" % t for t in range(3)] + ["gx%d" % t for t in range(RO)] + ["gd%d" % t for t in range(RO)]
@@ -40,7 +42,7 @@ def layer(g, T):
     dma = [0]
 
     def reg(r):
-        return (r, 0, 1 << 20) if isinstance(r, str) else r
+        return (r.rstrip("+"), 0, 1 << 20) if isinstance(r, str) else r
 
     def prepare(q, reads, writes):
         best = {}
@@ -103,6 +105,58 @@ def layer(g, T):
     return op, copy, landed, prepare, finish
 
 
+def order(steps):
+    n = len(steps)
+    pre = [set() for _ in steps]
+    hist = {}
+    for i, (q, _, reads, writes, _, _) in enumerate(steps):
+        for rs, w in ((reads, False), (writes, True)):
+            for r in rs:
+                name, lo, hi = (r, 0, 1 << 20) if isinstance(r, str) else r
+                adds = name[-1] == "+"
+                h = hist.setdefault(name.rstrip("+"), [])
+                for a, b, w2, q2, j, adds2 in h:
+                    if j != i and not (adds and adds2) and ((lo < b and a < hi and (w or w2)) or (name in PS and q != q2)):
+                        pre[i].add(j)
+                h[:] = [e for e in h if adds or not (w and lo <= e[0] and e[1] <= hi)]
+                h.append((lo, hi, w, q, i, adds))
+    post = [[] for _ in steps]
+    for i in range(n):
+        for j in pre[i]:
+            post[j].append(i)
+
+    def place(seq, before, back):
+        end, taken = [0.0] * n, {}
+        for i in seq:
+            q, busy = steps[i][0], steps[i][4]
+            t = steps[i][5] if back else 0.0
+            for j in before[i]:
+                t = max(t, end[j] + steps[i if back else j][5] + (0 if q == steps[j][0] == "P" else WAKE))
+            row = taken.setdefault(q, [])
+            k = len(row)
+            while k and row[k - 1][1] > t:
+                k -= 1
+            while k < len(row) and t + busy > row[k][0]:
+                t = max(t, row[k][1])
+                k += 1
+            row.insert(k, (t, t + busy))
+            end[i] = t + busy
+        return end
+
+    seq, best = list(range(n)), None
+    for _ in range(PASSES):
+        end = place(seq, pre, False)
+        pos = {i: k for k, i in enumerate(seq)}
+        seq = sorted(seq, key=lambda i: (end[i] - steps[i][4], pos[i]))
+        last = max(end[i] + steps[i][5] for i in seq)
+        if best is None or last < best[0]:
+            best = (last, seq)
+        seq = sorted(seq[::-1], key=lambda i: -end[i])
+        end = place(seq, post, True)
+        seq = sorted(seq[::-1], key=lambda i: -end[i])
+    return best[1]
+
+
 def weave(*chains):
     for i in range(max(len(c) for c in chains)):
         for c in chains:
@@ -116,9 +170,28 @@ def rank_program(g, core, T, topo):
         return
     cores = T.cores
     N = len(cores)
-    op, copy, landed, prepare, finish = layer(g, T)
+    issue, dma, arrive, prepare, finish = layer(g, T)
     V, S, P = g.vector, g.scalar, g.tensor
     sent = [0]
+    steps = []
+
+    def cols(a):
+        return a.shape[1]
+
+    def narrow(*aps):
+        return 0.5 if all("16" in str(a.dtype) for a in aps) else 1.0
+
+    def op(q, fns, reads, writes):
+        fns = fns if isinstance(fns, list) else [fns]
+        gather = any((r if isinstance(r, str) else r[0]) in LISTS for r in reads)
+        busy = sum(f[2] if gather else f[1]() for f in fns)
+        steps.append((q, lambda: issue(q, [f[0] for f in fns], reads, writes), reads, writes, busy, 0))
+
+    def copy(q, out, in_, reads, writes, lag=LOAD):
+        steps.append((q, lambda: dma(q, out, in_, reads, writes), reads, writes, 50, lag))
+
+    def landed(region, sem, count):
+        steps.append(("N", lambda: arrive(region, sem, count), [sem], [region], 0, FLIGHT))
 
     def v(f, r, w):
         op("V", f, r, w)
@@ -130,43 +203,50 @@ def rank_program(g, core, T, topo):
         op("P", f, r, w)
 
     def tc(o, i):
-        return lambda: V.tensor_copy(o, i)
+        return lambda: V.tensor_copy(o, i), lambda: max(64, cols(o) * narrow(o, i)), 50 + GATHER * cols(o)
+
+    def scatter(o, i):
+        return lambda: V.tensor_copy(o, i), None, 50 + SCATTER * cols(i)
 
     def tt(o, a, b, f):
-        return lambda: V.tensor_tensor(o, a, b, f)
+        return lambda: V.tensor_tensor(o, a, b, f), lambda: max(64, 2 * cols(o)), 50 + GATHER * cols(o)
 
     def ts(o, a, s1, f1, s2=None, f2=None):
-        if f2 is None:
-            return lambda: V.tensor_scalar(o, a, s1, None, f1)
-        return lambda: V.tensor_scalar(o, a, s1, s2, f1, f2)
+        return (lambda: V.tensor_scalar(o, a, s1, None, f1) if f2 is None else V.tensor_scalar(o, a, s1, s2, f1, f2)), lambda: max(64, cols(o) * narrow(o, a)), 50 + GATHER * cols(o)
+
+    def sweep(o, a, b, f1, f2):
+        return lambda: V.tensor_tensor_scan(o, a, b, 0.0, f1, f2), lambda: max(64, cols(o) * narrow(o, a, b)), 0
 
     def ms(o, c):
-        return lambda: V.memset(o, c)
+        return lambda: V.memset(o, c), lambda: max(64, cols(o) * narrow(o)), 0
 
     def act(o, i, f=AF.Copy, bias=0.0, scale=1.0):
-        return lambda: S.activation(o, i, f, bias=bias, scale=scale)
+        return lambda: S.activation(o, i, f, bias=bias, scale=scale), lambda: max(64, cols(o)), 65 + GATHER * cols(o)
 
     def mm(o, l, r, st=True, sp=True):
-        return lambda: P.matmul(o, l, r, st, sp)
+        return lambda: P.matmul(o, l, r, st, sp), lambda: max(min(64, cols(l)), cols(r)) * PE * (1 if narrow(l) < 1 else 4), 0
 
     def later(q, f, r, w):
         return lambda: op(q, f, r, w)
 
     def send(dst, out, in_, reads, sem):
-        d = cores[dst]
-        prepare("G", reads, [])
-        rid, pid = topo.addr(d, core)
-        g.remote_dma(out, in_, T.sem[sem], T.sem.ls, pid, rid, topo.mask(core, d))
-        sent[0] += len(topo.engines(core, d))
+        def run():
+            d = cores[dst]
+            prepare("G", reads, [])
+            rid, pid = topo.addr(d, core)
+            g.remote_dma(out, in_, T.sem[sem], T.sem.ls, pid, rid, topo.mask(core, d))
+            sent[0] += len(topo.engines(core, d))
+        steps.append(("G", run, reads, [(sem, dst, dst + 1)], 300 if any(x[3][:1] == [("gh0", (rank + 2) % N, (rank + 2) % N + 1)] for x in steps) else 2500, 0))
 
     def iota(name, view, pat, base, ch, fl=True):
-        if fl:
-            op("G", lambda: g.iota(view, pat, base, ch, allow_small_or_imprecise_dtypes=True), [], [name])
-        else:
-            op("G", lambda: g.iota(view, pat, base, ch), [], [name])
+        f = (lambda: g.iota(view, pat, base, ch, allow_small_or_imprecise_dtypes=True)) if fl else (lambda: g.iota(view, pat, base, ch))
+        op("G", (f, lambda: 130 + 2 * cols(view), 0), [], [name])
 
     def select(name, view, src, sname, pat, cmp, fill, base, ch):
-        op("G", lambda: g.affine_select(view, src, pat, cmp, fill, base, ch), [sname], [name])
+        op("G", (lambda: g.affine_select(view, src, pat, cmp, fill, base, ch), lambda: 170 + 2 * cols(view), 0), [sname], [name])
+
+    def keep(o, i):
+        return lambda: g.affine_select(o, i, [[0, cols(o)]], A.is_ge, 0.0, 0, 0), lambda: 170 + 2 * cols(o), 0
 
     def col(i):
         return T.col[:, i:i + 1]
@@ -185,19 +265,23 @@ def rank_program(g, core, T, topo):
     iota("pI", T.pI[:, 0:1], [[0, 1]], 0, 1, False)
     iota("n16", T.n16[:], [[1, 16]], 0, 0, False)
     select("idb", T.idb[:], ONE, "one", [[-1, 128]], A.is_equal, 0.0, 0, 1)
-    iota("n144", T.n144[:], [[1, 144]], 0, 0)
     iota("n256", T.n256[:], [[0, 2], [1, 256]], 0, 0)
+    iota("n144", T.n144[:], [[1, 144]], 0, 0)
     select("up0", T.upr[:, 128:256], ONE, "one", [[1, 128]], A.is_gt, 0.0, 0, -1)
-    select("upr", T.upr[:, 0:128], T.upr[:, 128:256], "up0", [[-1, 128]], A.not_equal, -4096.0, 0, 1)
     iota("v1c", T.v1c[:, 0:8], [[128, 8]], 1, 1)
+    select("upr", T.upr[:, 0:128], T.upr[:, 128:256], "up0", [[-1, 128]], A.not_equal, -4096.0, 0, 1)
     iota("du", T.du[:], [[16, 16]], 2056, 0)
-    iota("ck", T.ck[:], [[0, 16], [-2048, 16]], 30720, 0)
-    iota("c8", T.c8[:], [[0, 128]], 8 * 65536, 0)
     iota("lane", T.lane[:], [[0, 16], [1, 16]], 0, 0)
-    select("segm", T.segm[:], T.one[:], "one", [[0, 16], [1, 16]], A.is_gt, 0.0, 0, 0)
+    for name, a, b, c in (("c8b", 0, 8, 8), ("bz", 0, 56, 0), ("t8", 0, 1, 0), ("cv", 0, 1, 1), ("cw", 0, 1, 1), ("thr", 0, 1, 9 * 65536), ("rz", 0, 8, 0), ("mkg", 0, 128, 1), ("c8", 0, 128, 8 * 65536), ("nil", 0, 128, 0)):
+        iota((name, a, b), T[name][:, a:b], [[0, b - a]], c, 0)
+    iota("ck", T.ck[:], [[0, 8], [-4096, 16]], 61440, 0)
+    select("up64", T.up64[:], T.one[0:1, 0:128], "one", [[1, 128]], A.is_ge, 0.0, -32, 0)
+    select("segm", T.segm[:], ONE, "one", [[0, 8], [1, 16]], A.is_gt, 0.0, 0, 0)
     iota("ct8", T.ct8[:], [[0, 16], [1, 8]], -256, 0)
     select("jb0", T.jb[:], ONE, "one", [[1, 128]], A.not_equal, -1.0, -127, 1)
+    iota(("wb", GB + 769, W2B), T.wb[:, GB + 769:W2B], [[0, W2B - GB - 769]], 0, 0)
     select("jb", T.jb[:], T.jb[:], "jb0", [[1, 128]], A.is_equal, 0.0, -127, 1)
+    iota(("wb", DUMP, GB), T.wb[:, DUMP:GB], [[0, GB - DUMP]], 0, 0)
     iota("smk0", T.smk[:], [[0, 576]], 0, 0)
 
     P15, P4, PC = T.pp[:, 0:1], T.pp[:, 1:2], T.pp[:, 2:3]
@@ -210,46 +294,51 @@ def rank_program(g, core, T, topo):
     v(ts(T.lmc[:], N16, P15, A.is_equal), ["n16", "pp"], ["lmc"])
     v([ms(T.tab[:, 0:1], 0.0), ms(T.hi16[:, 0:1], 0.0)], [], [("tab", 0, 1), ("hi16", 0, 1)])
     v([ts(T.cc[:, 16:21], T.pw[:, 0:5], lm(11), A.mult), ts(T.cc[:, 21:26], T.pw[:, 0:5], lm(12), A.mult), tc(T.cc[:, 26:27], lm(13))], ["pw", "pwa", "lmc"], [("cc", 16, 32)])
-    v([ts(MB, P15, 11.0, A.is_lt), ts(MP, P15, 11.0, A.is_ge)], ["pp"], [("col", 1, 3)])
+    v([ts(MB, P15, 11.0, A.is_lt), ts(T.gib[:, 0:8], G8, P4, A.is_equal)], ["pp", "n16"], [("col", 1, 2), ("gib", 0, 8)])
     v(tt(T.cc[:, 0:11], T.cc[:, 16:27], T.lmc[:, 0:11], A.add), [("cc", 16, 32), "lmc"], [("cc", 0, 16)])
-    s([act(T.seven[:], T.idb[:], AF.Copy, 0.0, 7.0), act(T.m1k[:], T.idb[:], AF.Copy, 0.0, -1024.0), act(T.nid[:], T.idb[:], AF.Copy, 0.0, -1.0), act(T.idF[:], T.idb[:]),
-       act(T.amb[:], T.idb[:], AF.Copy, 0.0, MB)], ["idb", ("col", 1, 3)], ["seven", "m1k", "nid", "idF", "amb"])
+    s([act(T.seven[:], T.idb[:], AF.Copy, 0.0, 7.0), act(T.m1k[:], T.idb[:], AF.Copy, 0.0, -1024.0), act(T.nid[:], T.idb[:], AF.Copy, 0.0, -1.0), act(T.idF[:], T.idb[:])],
+      ["idb"], ["seven", "m1k", "nid", "idF"])
+    s([act(MP, MB, AF.Copy, 1.0, -1.0), act(BP, MB, AF.Copy, 64.0, -65.0), act(ZC, P4, AF.Copy, 15.0, 16.0), act(WL, lm(12), AF.Identity, lm(11), 32.0), act(WD, lm(12), AF.Identity, lm(13), 24.0),
+       act(T.amb[:], T.idb[:], AF.Copy, 0.0, MB)], ["idb", ("col", 1, 2), "pp", "lmc"], [("col", 0, 1), ("col", 2, 4), ("col", 5, 7), "amb"])
+    s(act(RB, MP, AF.Identity, WD, 64.0), [("col", 2, 3), ("col", 6, 7)], [("col", 4, 5)])
+    s([act(o, T.gib[:, 0:8], AF.Copy, 0.0, c) for o, c in ((T.gib[:, 8:16], 0.5), (T.gik[:, 0:8], BIG), (T.gik[:, 8:16], BIG / 2), (T.gin[:, 0::3], -1.0), (T.gin[:, 1::3], -FAR), (T.gin[:, 2::3], -FAR))],
+      [("gib", 0, 8)], [("gib", 8, 16), "gik", "gin"])
 
     def double(name, first, n):
         return [later("V", ts(T[name][:, 1 << b:2 << b], T[name][:, 0:1 << b], T.cc[:, first + b:first + b + 1], A.add), [(name, 0, 1 << b), ("cc", 0, 16)], [(name, 1 << b, 2 << b)]) for b in range(n)]
 
-    more = [
-        later("V", [ts(WD, lm(12), 24.0, A.mult, lm(13), A.add), ts(BP, MP, 65.0, A.mult, -1.0, A.add)], ["lmc", ("col", 1, 3)], [("col", 3, 4), ("col", 6, 7)]),
-        later("V", [tc(T.anl[:], T.anI[:]), tc(T.ofl[:], T.ofI[:])], ["anI", "ofI"], ["anl", "ofl"]),
-        later("V", ts(RB, MP, 64.0, A.mult, WD, A.add), [("col", 1, 3), ("col", 6, 7)], [("col", 4, 5)])]
-    weave(double("tab", 0, 7), double("hi16", 7, 4) + more)
-    v([ts(T.tab[:, 128 * a:128 * a + 128], T.tab[:, 0:128], T.hi16[:, a:a + 1], A.add) for a in range(1, 16)], [("tab", 0, 128), "hi16"], [("tab", 128, 2048)])
+    weave(double("tab", 0, 7), double("hi16", 7, 4))
+    v([tc(T.anl[:], T.anI[:]), tc(T.ofl[:], T.ofI[:])], ["anI", "ofI"], ["anl", "ofl"])
+    s([act(T.tab[:, 128 * a:128 * a + 128], T.tab[:, 0:128], AF.Identity, T.hi16[:, a:a + 1]) for a in range(11, 16)], [("tab", 0, 128), "hi16"], [("tab", 1408, 2048)])
+    v([ts(T.tab[:, 128 * a:128 * a + 128], T.tab[:, 0:128], T.hi16[:, a:a + 1], A.add) for a in range(1, 11)], [("tab", 0, 128), "hi16"], [("tab", 128, 1408)])
 
-    WKB = ("pH", "pD", "pC", "pB")
-
-    def weeks(b):
-        bank = WKB[b]
+    WKB = ("pB", "pC", "pH", "pD")
+    for b, bank in enumerate(WKB):
         p([mm(T[bank][:], T.seven[:], T.wkb[:, 512 * b:512 * b + 512], True, False), mm(T[bank][:], T.one[0:1, 0:128], T.n256[:], False, True)], ["seven", "wkb", "one", "n256"], [bank])
+
+    def sign(b):
+        bank = WKB[b]
         s([act(T.sg[:, 512 * b + c:512 * b + c + 256], T[bank][:, c:c + 256], AF.Sign, 512 * b + c - 2047.5) for c in (0, 256)], [bank], [("sg", 512 * b, 512 * b + 512)])
 
     def weeks2(b):
         bank = WKB[b]
         p([mm(T[bank][:], T.seven[:], T.wkb[:, 512 * b:512 * b + 512], True, False), mm(T[bank][:], T.one[0:1, 0:128], T.n256[:], False, False),
            mm(T[bank][:], T.m1k[:], T.sg[:, 512 * b:512 * b + 512], False, True)], ["seven", "wkb", "one", "n256", "m1k", ("sg", 512 * b, 512 * b + 512)], [bank])
+
+    def weeks3(b):
+        bank = WKB[b]
         s([act(T.cw[:, 1 + 512 * b + c:257 + 512 * b + c], T[bank][:, c:c + 256], AF.Copy, 512 * b + c - 1023.0) for c in (0, 256)], [bank], [("cw", 1 + 512 * b, 513 + 512 * b)])
 
     for h in (0, 1):
         s(act(T.g1[:, 512 * h:512 * h + 512], T.tab[:].indirect(T.anl[:, 32 * h:32 * h + 32]), AF.Identity, BP, MP), ["tab", "anl", ("col", 1, 4)], [("g1", 512 * h, 512 * h + 512)])
-    v(ts(T.wb[:, GA:GA + 512], T.tab[:].indirect(T.ofl[:, 64:96]), MB, A.mult, RB, A.add), ["tab", "ofl", ("col", 1, 5)], [("wb", GA, GA + 512)])
-    s(act(T.wb[:, GA + 512:GA + 768], T.tab[:].indirect(T.ofl[:, 96:112]), AF.Identity, RB, MB), ["tab", "ofl", ("col", 1, 5)], [("wb", GA + 512, GA + 768)])
+    v(ts(T.wb[:, GA:GA + 256], T.tab[:].indirect(T.ofl[:, 64:80]), MB, A.mult, RB, A.add), ["tab", "ofl", ("col", 1, 5)], [("wb", GA, GA + 256)])
+    s(act(T.wb[:, GA + 256:GA + 768], T.tab[:].indirect(T.ofl[:, 80:112]), AF.Identity, RB, MB), ["tab", "ofl", ("col", 1, 5)], [("wb", GA + 256, GA + 768)])
     v([ts(T.an1[:, 0:64], T.anI[:], 1024.0, A.is_ge, float(GA - W1 - 1024), A.mult), ms(T.wb[:, GA + 769:W1], 0.0), tc(T.wb[:, GA + 768:GA + 769], RB)],
       ["anI", ("col", 4, 5)], [("an1", 0, 64), ("wb", GA + 768, W1)])
+    v(tt(T.an1[:, 64:128], T.an1[:, 0:64], T.anI[:], A.add), [("an1", 0, 64), "anI"], [("an1", 64, 128)])
     v(tt(T.wb[:, W1:W1 + 512], T.tab[:].indirect(T.ofl[:, 0:32]), T.g1[:, 0:512], A.max), ["tab", "ofl", ("g1", 0, 512)], [("wb", W1, W1 + 512)])
-    v([tt(T.an1[:, 64:128], T.an1[:, 0:64], T.anI[:], A.add), ts(ZC, P4, 16.0, A.mult, 15.0, A.add), ts(WL, lm(12), 32.0, A.mult, lm(11), A.add)],
-      [("an1", 0, 64), "anI", "pp", "lmc"], [("an1", 64, 128), ("col", 0, 1), ("col", 5, 6)])
-    v(tt(T.wb[:, W1 + 512:DUMP], T.tab[:].indirect(T.ofl[:, 32:64]), T.g1[:, 512:1024], A.max), ["tab", "ofl", ("g1", 512, 1024)], [("wb", W1 + 512, DUMP)])
     v(ts(T.l0[:], T.an1[:, 64:128], float(W1 - GA), A.add), [("an1", 64, 128)], ["l0"])
-    weeks(0)
+    v(tt(T.wb[:, W1 + 512:DUMP], T.tab[:].indirect(T.ofl[:, 32:64]), T.g1[:, 512:1024], A.max), ["tab", "ofl", ("g1", 512, 1024)], [("wb", W1 + 512, DUMP)])
 
     BK = ("pE", "pF")
 
@@ -291,7 +380,8 @@ def rank_program(g, core, T, topo):
             f = WIN[a][l + 1][2] + c
             op(q, (act if q == "S" else tc)(T.wb[:, f:f + 512], T[BK[h]][:]), [BK[h]], [("wb", f, f + 512)])
         else:
-            s(act(T.t8[:, 1 + c:513 + c], T[BK[h]][:], AF.Identity, RB), [BK[h], ("col", 4, 5)], [("t8", 1 + c, 513 + c)])
+            o = T.t8[:, 1 + c:513 + c]
+            op(q, act(o, T[BK[h]][:], AF.Identity, RB) if q == "S" else ts(o, T[BK[h]][:], RB, A.add), [BK[h], ("col", 4, 5)], [("t8", 1 + c, 513 + c)])
 
     def datelist():
         return [later("V", tc(T.ldI[:, 0:64], T.pG[:, 0:64]), ["pG"], [("ldI", 0, 64)]),
@@ -306,63 +396,59 @@ def rank_program(g, core, T, topo):
     TC = [T.tc[:, i:i + 1] for i in range(16)]
     WB = T.cc[:, 10:11]
 
-    def fill0():
-        v([ts(T.pw[:, 5:10], T.pw[:, 0:5], 32.0, A.mult), ms(T.pw[:, 10:11], 1024.0), ms(T.t8[:, 0:1], 0.0), ms(T.cv[:, 0:1], 1.0), ms(T.cw[:, 0:1], 1.0), ms(T.xg[:, 0:1], LOW),
-           ts(T.gib[:, 0:8], G8, P4, A.is_equal), ts(T.gib[:, 8:16], G8, P4, A.is_equal, 0.5, A.mult), ms(T.c8b[:], 8.0), ms(T.bz[:, 0:56], 0.0)],
-          ["pw", "pwa", "n16", "pp"], ["pw2", ("t8", 0, 1), ("cv", 0, 1), ("cw", 0, 1), ("xg", 0, 1), "gib", "c8b", ("bz", 0, 56)])
-        v([tt(T.cc[:, 16:27], T.pw[:, 0:11], T.lmc[:, 0:11], A.mult), ts(TC[5], P4, 17.0, A.mult, P15, A.add), ts(T.v1c[:, 8:16], T.v1c[:, 0:8], 0.5, A.mult)],
-          ["pw", "pwa", "pw2", "lmc", "pp", "v1c"], [("cc", 16, 32), ("tc", 5, 6), "v1h"])
-        v([lambda: V.tensor_tensor_scan(T.cc[:, 0:11], T.cc[:, 16:27], T.cc[:, 16:27], 0.0, A.max, A.max), tc(T.dgt[:, 0:1], TC[5]), ts(T.dgt[:, 2:3], TC[5], 1.0, A.add)],
-          [("cc", 16, 32), ("tc", 5, 6)], [("cc", 0, 16), "dgl"])
-
-    def fill1():
-        v([ts(T.zd[:], T.n144[:], ZC, A.is_equal, WB, A.mult), ts(T.sl[:], T.snI[:], 1.0, A.add), ts(T.gik[:, 0:8], G8, P4, A.is_equal, BIG, A.mult), ts(T.gik[:, 8:16], G8, P4, A.is_equal, BIG / 2, A.mult),
-           ms(T.thr[:, 0:1], 9.0 * BIG), ts(T.gin[:, 0:8], G8, P4, A.is_equal, -1.0, A.mult), ts(T.gin[:, 8:16], G8, P4, A.is_equal, -FAR, A.mult), tc(T.ex[:], N16), ms(T.rz[:, 0:8], 0.0),
-           ts(T.dec[:, 8:16], G8, P4, A.is_equal, WB, A.mult), ts(TC[2], P15, 8.0, A.is_ge), ts(TC[3], P4, 8.0, A.mult, P15, A.add), ts(T.smi[:, 0:16], N16, 7, A.bitwise_and),
-           ts(T.smi[:, 16:17], T.pI[:, 0:1], 7, A.bitwise_and)], ["n144", "n16", "pp", "pI", "snI", ("col", 0, 1), ("cc", 0, 16)],
-          ["zd", "sl", "gik", ("thr", 0, 1), "gin", "ex", ("rz", 0, 8), ("dec", 8, 16), ("tc", 2, 4), "smi"])
-
-    def fill2():
-        v([tc(T.exg[:], T.smi[:, 0:16]), ts(T.ex8[:], G8, 2.0, A.mult, TC[2], A.add), ts(T.dgt[:, 4:5], TC[2], 56.0, A.mult, TC[3], A.add), ts(T.du[:], T.du[:], P15, A.add),
-           ts(TC[6], T.smi[:, 16:17], 1.0, A.add), ts(TC[7], T.smi[:, 16:17], 2.0, A.add, 8.0, A.mult), ts(TC[8], TC[2], float(EO[8]), A.mult, -1.0, A.add),
-           ts(T.tri[:], N16, P15, A.add, 15.5, A.is_lt), ms(T.mkg[:, 0:128], 1.0), ts(T.mkg[:, 128:384], T.lane[:], P15, A.is_equal)],
-          [("tc", 2, 4), "smi", "n16", "pp", "du", "lane"], ["exg", "ex8", "dg8", "du", ("tc", 6, 9), "tri", "mkg"])
-        v([ts(T.dgt[:, 6:7], TC[6], TC[7], A.mult, TC[8], A.add), ts(T.duw[:], T.du[:], float(DUMP - W1 + 1 - 2056), A.add)], [("tc", 6, 9), "du"], ["pick", "duw"])
+    z12 = zed(1, 2)
+    fills = [
+        [z12, later("V", [ts(T.pw[:, 5:10], T.pw[:, 0:5], 32.0, A.mult), ms(T.pw[:, 10:11], 1024.0), ms(T.xg[:, 0:1], LOW), ts(TC[5], P4, 17.0, A.mult, P15, A.add)],
+                    ["pw", "pwa", "pp"], ["pw2", ("xg", 0, 1), ("tc", 5, 6)])],
+        [later("V", [tt(T.cc[:, 16:27], T.pw[:, 0:11], T.lmc[:, 0:11], A.mult), tc(T.dgt[:, 0:1], TC[5]), ts(T.dgt[:, 2:3], TC[5], 1.0, A.add)],
+               ["pw", "pwa", "pw2", "lmc", ("tc", 5, 6)], [("cc", 16, 32), "dgl"])],
+        [later("V", [sweep(T.cc[:, 0:11], T.cc[:, 16:27], T.cc[:, 16:27], A.max, A.max), ts(T.sl[:], T.snI[:], 1.0, A.add), tc(T.ex[:], N16),
+                     ts(TC[2], P15, 8.0, A.is_ge), ts(TC[3], P4, 8.0, A.mult, P15, A.add), ts(T.smi[:, 0:16], N16, 7, A.bitwise_and), ts(T.smi[:, 16:17], T.pI[:, 0:1], 7, A.bitwise_and)],
+               [("cc", 16, 32), "snI", "n16", "pp", "pI"], [("cc", 0, 16), "sl", "ex", ("tc", 2, 4), "smi"])],
+        [later("V", [ts(T.zd[:], T.n144[:], ZC, A.is_equal, WB, A.mult), tc(T.exg[:], T.smi[:, 0:16]), ts(T.ex8[:], G8, 2.0, A.mult, TC[2], A.add)],
+               ["n144", "n16", ("col", 0, 1), ("cc", 0, 16), "smi", ("tc", 2, 4)], ["zd", "exg", "ex8"])],
+        [later("V", [ts(T.dgt[:, 4:5], TC[2], 56.0, A.mult, TC[3], A.add), ts(TC[6], T.smi[:, 16:17], 1.0, A.add), ts(TC[7], T.smi[:, 16:17], 2.0, A.add, 8.0, A.mult),
+                     ts(TC[8], TC[2], float(EO[8]), A.mult, -1.0, A.add), ts(T.tri[:], N16, P15, A.add, 15.5, A.is_lt), ts(T.mkg[:, 128:384], T.lane[:], P15, A.is_equal), ms(T.duw[:], 0.0),
+                     ts(T.du[:], T.du[:], P15, A.add)], [("tc", 2, 4), "smi", "n16", "pp", "lane", "du"], ["dg8", ("tc", 6, 9), "tri", ("mkg", 128, 384), "duw", "du"]),
+         later("V", [ts(T.dgt[:, 6:7], TC[6], TC[7], A.mult, TC[8], A.add), ts(T.duw[:, 2::3], T.du[:], float(DUMP - W1 + 1 - 2056), A.add), ts(T.dec[:, 8:16], G8, P4, A.is_equal, WB, A.mult),
+                     ts(TC[9], lm(13), 1024.0, A.mult, WL, A.add)], [("tc", 6, 9), "du", "duw", "n16", "pp", ("cc", 0, 16), "lmc", ("col", 5, 6)], ["pick", "duw", ("dec", 8, 16), ("tc", 9, 10)])]]
 
     def fill3():
         z = zed(0, 3, 4, 5)
-        v([ms(T.wb[:, DUMP:GB], 0.0), ms(T.wb[:, GB + 769:W2B], 0.0), tc(T.wb[:, GB + 768:GB + 769], RB), ts(DB, PC, 8.0, A.is_lt, -64.0 * 1057, A.mult), ts(TC[9], lm(13), 1024.0, A.mult, WL, A.add)],
-          [("col", 4, 6), "pp", "lmc"], [("wb", DUMP, GB), ("wb", GB + 768, W2B), ("col", 7, 8), ("tc", 9, 10)])
+        v([tc(T.wb[:, GB + 768:GB + 769], RB), ts(DB, PC, 8.0, A.is_lt, -64.0 * 1057, A.mult), ts(T.dec[:, 0:8], G8, P4, A.is_equal, TC[9], A.mult)],
+          [("col", 4, 6), "pp", "n16", ("tc", 9, 10)], [("wb", GB + 768, GB + 769), ("col", 7, 8), ("dec", 0, 8)])
         z()
-        v(ts(T.dec[:, 0:8], G8, P4, A.is_equal, TC[9], A.mult), ["n16", "pp", ("tc", 9, 10)], [("dec", 0, 8)])
 
-    z12 = zed(1, 2)
     for l in range(3):
         own(0, l)
         jump(0, l, 0, "V")
         jump(0, l, 1, "S")
-        if l == 0:
-            z12()
-        if l == 2:
-            for b in (0, 2, 1):
-                weeks2(b)
+        for f in fills[2 * l]:
+            f()
+        if l > 0:
+            weeks2(l - 1)
         join(l, 0)
         if l == 2:
             after(0, l)
         join(l, 1)
         if l < 2:
+            sign(2 * l)
             after(0, l)
             sums(0, l, 0, "V")
             sums(0, l, 1, "S")
+            for f in fills[2 * l + 1]:
+                f()
             pointers2(0, l + 1)
-        (fill0, fill1, fill2)[l]()
-        for f, b in (((weeks, 1), (weeks, 3)), ((weeks, 2), (weeks2, 3)), ())[l]:
-            f(b)
+            sign(2 * l + 1)
+    weeks3(0)
+    weeks3(1)
     weave(datelist())
 
-    def keys(w):
-        p(mm(T.pD[:, 0:16 * w], T.one[0:1, 0:128], T.ck[:, 0:16 * w], False, True), ["one", "ck"], ["pD"])
-        v(lambda: V.tensor_tensor_scan(T.kx[:, 0:16 * w], T.segm[:, 0:16 * w], T.pD[:, 0:16 * w], 0.0, A.mult, A.max), ["segm", "pD"], ["kx"])
+    KB = ("pD", "pC")
+    XS, XO = 2, 2
+
+    def keys(q):
+        v(sweep(T.kx[:, 128 * q:128 * q + 128], T.segm[:], T[KB[q]][:, 0:128], A.mult, A.max), ["segm", KB[q]], [("kx", 128 * q, 128 * q + 128)])
 
     def excess(w, t):
         return ts(T.ki[:, 0:w], T.kx[:, 15:16 * w:16], T.thr[:, t % 2:t % 2 + 1], A.subtract, 0.0, A.max)
@@ -370,58 +456,48 @@ def rank_program(g, core, T, topo):
     def chosen(w):
         v(ts(T.ki[:, 16:16 + w], T.ki[:, 0:w], 4095, A.bitwise_and), [("ki", 0, 16)], [("ki", 16, 32)])
 
-    def eqdays(h, q):
+    def eqdays(h, q, bank, bs):
         o = EO[8] * h
-        row = [T.pH[:, 128 * h + 128 - EW[b]:128 * h + 128] for b in range(8)]
+        row = [T[bank][:, 128 * h + 128 - EW[b]:128 * h + 128] for b in range(8)]
         out = [T.eq[:, o + EO[b]:o + EO[b + 1]] for b in range(8)]
+        w = [("eq", o + EO[b], o + EO[b + 1]) for b in bs]
         if q == "V":
-            v([ts(out[b], row[b], T.pA[:, 8 * h + b:8 * h + b + 1], A.not_equal, FAR, A.mult) for b in range(8)], ["pH", "pA"], [("eq", o, o + EO[8])])
+            v([ts(out[b], row[b], T.pA[:, 24 * h + 3 * b:24 * h + 3 * b + 1], A.not_equal, FAR, A.mult) for b in bs], [bank, "pA"], w)
         else:
-            s([act(out[b], row[b], AF.Abs, T.sm[:, 48 + 8 * h + b:49 + 8 * h + b], -FAR) for b in range(8)], ["pH", ("sm", 48, 64)], [("eq", o, o + EO[8])])
+            s([act(out[b], row[b], AF.Abs, T.sm[:, 48 + 8 * h + b:49 + 8 * h + b], -FAR) for b in bs], [bank, ("sm", 48, 64)], w)
 
     def scan(h):
         a = slice(EO[8] * h, EO[8] * h + EO[8])
-        v(lambda: V.tensor_tensor_scan(T.scn[:, a], T.eq[:, a], T.smk[:], 0.0, A.min, A.max), [("eq", a.start, a.stop), "smk"], [("scn", a.start, a.stop)])
+        v(sweep(T.scn[:, a], T.eq[:, a], T.smk[:], A.min, A.max), [("eq", a.start, a.stop), "smk"], [("scn", a.start, a.stop)])
 
     def dayoffsets(w):
         return [
             later("V", tt(T.sm[:, 0:16], T.scn[:].indirect(T.dgt[:, 6:7]), T.du[:], A.subtract), ["scn", "pick", "du"], [("sm", 0, 16)]),
-            later("V", tt(T.sm[:, 16:16 + w], T.sm[:, 0:w], T.pA[:, 0:w], A.min), [("sm", 0, 16), "pA"], [("sm", 16, 32)]),
+            later("V", tt(T.sm[:, 16:16 + w], T.sm[:, 0:w], T.pA[:, 0:3 * w:3], A.min), [("sm", 0, 16), "pA"], [("sm", 16, 32)]),
             later("V", ts(T.u16s[:, 16:16 + w], T.sm[:, 16:16 + w], -1.0, A.mult), [("sm", 16, 32)], [("u16s", 16, 32)])]
 
     def copies(q, src, sname, so, dst, n, ks):
-        f = act if q == "S" else tc
+        f = {"S": act, "V": tc, "G": keep}[q]
         op(q, [f(T.xr[:, dst + k:dst + 16 * n:16], src[:, so:so + n]) for k in ks], [(sname, so, so + n)], [("xr" + q, dst, dst + 16 * n)])
 
     def compare(c0, n):
         a = slice(16 * c0, 16 * c0 + 16 * n)
-        v(tt(T.cmp[:, a], T.sd[:, 0:2049].indirect(T.cg[:, c0:c0 + n]), T.xr[:, a], A.is_lt), [("sd", 0, 2049), "cg", ("xrS", a.start, a.stop), ("xrV", a.start, a.stop)], [("cmp", a.start, a.stop)])
+        v(tt(T.cmp[:, a], T.sd[:, 0:2049].indirect(T.cg[:, c0:c0 + n]), T.xr[:, a], A.is_lt), [("sd", 0, 2049), "cg"] + [("xr" + q, a.start, a.stop) for q in "SVG"], [("cmp", a.start, a.stop)])
+        bank = KB[c0 // 128]
+        p([mm(T[bank][c0 % 128:c0 % 128 + n, k:128:16], T.cmp[:, 16 * c0 + k:16 * c0 + 16 * n:16], T.gik[:, 0:8], False, False) for k in range(16)],
+          [("cmp", 16 * c0, 16 * c0 + 16 * n), "gik"], [bank + "+"])
 
-    def count(c0, n):
-        o = 128 * (c0 // 128)
-        p([mm(T.pD[c0 % 128:c0 % 128 + n, o + k:o + 128:16], T.cmp[:, 16 * c0 + k:16 * c0 + 16 * n:16], T.gik[:, 0:8], False, False) for k in range(16)],
-          [("cmp", 16 * c0, 16 * c0 + 16 * n), "gik"], ["pD"])
+    def signed(src, sname, so, c0, o, b):
+        def first():
+            p(mm(T[b][:], T.nil[:], T.n256[:], True, False), ["nil", "n256"], [b])
+            p([mm(T[b][:, k::16], T.idb[:], src[:, so:so + 32], False, False) for k in range(16)], [(sname, so, so + 32), "idb"], [b])
+            s(act(T.sgb[:, o:o + 512], T.sd[:, 0:2049].indirect(T.cg[:, c0:c0 + 32])), [("sd", 0, 2049), "cg"], [("sgb", o, o + 512)])
+            p(mm(T[b][:], T.nid[:], T.sgb[:, o:o + 512], False, True), [("sgb", o, o + 512), "nid"], [b])
 
-    def fetch(c0):
-        s(act(T.sgb[:], T.sd[:, 0:2049].indirect(T.cg[:, c0:c0 + 64])), [("sd", 0, 2049), "cg"], ["sgb"])
-
-    def differ(src, sname, so):
-        for h in (0, 1):
-            p([f for k in range(8) for f in (mm(T[BK[h]][:, 64 * k:64 * k + 64], T.idb[:], src[:, so:so + 64], True, False),
-                                              mm(T[BK[h]][:, 64 * k:64 * k + 64], T.nid[:], T.sgb[:, 8 * h + k:1024:16], False, True))], [(sname, so, so + 64), "sgb", "idb", "nid"], [BK[h]])
-
-    def signs(c0):
-        o = 128 * (c0 // 128)
-        for h in (0, 1):
-            s(act(T.sgn[:, 512 * h:512 * h + 512], T[BK[h]][:], AF.Sign, -TINY), [BK[h]], [("sgn", 512 * h, 512 * h + 512)])
-            p([mm(T.pD[64:128, o + k:o + 128:16], T.sgn[:, 64 * k:64 * k + 64], T.gik[:, 8:16], False, False) for k in range(8 * h, 8 * h + 8)],
-              [("sgn", 512 * h, 512 * h + 512), "gik"], ["pD"])
-
-    def open_keys(w, signed):
-        f = [mm(T.pD[:, 0:16 * w], T.one[0:1, 0:128], T.ck[:, 0:16 * w], True, False)]
-        if signed:
-            f.append(mm(T.pD[64:128, 16 * w - 128:16 * w], T.one[0:1, 0:64], T.c8[:], False, False))
-        p(f, ["one", "ck", "c8"], ["pD"])
+        def second():
+            s(act(T.sgn[:, o:o + 512], T[b][:], AF.Sign, -TINY), [b], [("sgn", o, o + 512)])
+            p([mm(T[KB[c0 // 128]][c0 % 128:c0 % 128 + 32, k:128:16], T.sgn[:, o + k:o + 512:16], T.gik[:, 8:16], False, False) for k in range(16)], [("sgn", o, o + 512), "gik"], [KB[c0 // 128] + "+"])
+        return [first, second]
 
     for t in range(RO):
         last = t == RO - 1
@@ -439,25 +515,35 @@ def rank_program(g, core, T, topo):
         def cands(h):
             s(act(T.cv[:, 1 + 512 * h:513 + 512 * h], T.cw[:, 0:2049].indirect(T.lfd[:, 32 * h:32 * h + 32])), ["cw", "lfd"], [("cv", 1 + 512 * h, 513 + 512 * h)])
 
-        if 0 < t < RO - 1:
-            ghosts(2)
-            ghosts(3)
-        p(mm(T.pH[:, 0:256], T.idb[:], T.xw[:, 769:1025], True, False), ["idb", ("xw", 1, 1025)], ["pH"])
-        s(act(T.sgb[:, 0:256], T.sd[:, 0:2049].indirect(T.lfd[:, 48:64])), [("sd", 0, 2049), "lfd"], ["sgb"])
-        p(mm(T.pH[:, 0:256], T.nid[:], T.sgb[:, 0:256], False, True), ["nid", "sgb"], ["pH"])
+        nv = 3 if t else 4
         if t == 0:
             sums(0, 2, 0)
-        elif not last:
-            ghosts(1)
-        s(act(T.sgn[:, 0:256], T.pH[:, 0:256], AF.Sign, TINY), ["pH"], [("sgn", 0, 512)])
+            sums(0, 2, 1)
+            ghosts(2)
+            for b in (2, 3):
+                weeks2(b)
+                weeks3(b)
+        else:
+            if not last:
+                ghosts(2)
+                ghosts(3)
+            p(mm(T.pH[:, 0:256], T.idb[:], T.xw[:, 769:1025], True, False), ["idb", ("xw", 1, 1025)], ["pH"])
+            s(act(T.sgb[:, 0:256], T.sd[:, 0:2049].indirect(T.lfd[:, 48:64])), [("sd", 0, 2049), "lfd"], ["sgb"])
+            p(mm(T.pH[:, 0:256], T.nid[:], T.sgb[:, 0:256], False, True), ["nid", "sgb"], ["pH"])
+            if not last:
+                ghosts(1)
+            s(act(T.sgn[:, 0:256], T.pH[:, 0:256], AF.Sign, TINY), ["pH"], [("sgn", 0, 512)])
         cands(0)
         for h in (0, 1):
-            a = slice(384 * h, 384 * h + 384)
-            v(tt(T.cmp[:, a], T.sd[:, 0:2049].indirect(T.lfd[:, 24 * h:24 * h + 24]), T.xw[:, 1 + a.start:1 + a.stop], A.is_le), [("sd", 0, 2049), "lfd", ("xw", 1, 1025)], [("cmp", a.start, a.stop)])
-            if h == 1:
+            a = slice(128 * nv * h, 128 * nv * h + 128 * nv)
+            v(tt(T.cmp[:, a], T.sd[:, 0:2049].indirect(T.lfd[:, 8 * nv * h:8 * nv * h + 8 * nv]), T.xw[:, 1 + a.start:1 + a.stop], A.is_le),
+              [("sd", 0, 2049), "lfd", ("xw", 1, 1025)], [("cmp", a.start, a.stop)])
+            if h == 1 and t > 0:
                 p([f for c in (0, 1) for f in (mm(T.pA[:, 48 + 8 * c:56 + 8 * c], T.one[0:1, 0:128], T.c8b[0:1, 0:8], True, False),
                                                mm(T.pA[:, 48 + 8 * c:56 + 8 * c], T.sgn[:, 128 * c:128 * c + 128], T.gib[:, 8:16], False, True))], [("sgn", 0, 512), "gib", "one", "c8b"], ["pA"])
-            p([mm(T.pA[:, 8 * c:8 * c + 8], T.cmp[:, 128 * c:128 * c + 128], T.gib[:, 0:8]) for c in range(3 * h, 3 * h + 3)], [("cmp", a.start, a.stop), "gib"], ["pA"])
+            p([mm(T.pA[:, 8 * c:8 * c + 8], T.cmp[:, 128 * c:128 * c + 128], T.gib[:, 0:8]) for c in range(nv * h, nv * h + nv)], [("cmp", a.start, a.stop), "gib"], ["pA"])
+        if t == 0:
+            v(ts(T.v1c[:, 8:16], T.v1c[:, 0:8], 0.5, A.mult), ["v1c"], ["v1h"])
         v(ts(T.bz[:, 56:120], T.pA[:, 0:64], 4.5, A.is_lt), ["pA"], [("bz", 56, 120)])
         p([mm(T.pB[:, 0:64], T.upr[:, 0:128], T.bz[:, 56:120], True, False)] + [mm(T.pB[:, 0:64], ONE, T.bz[:, 56 - 8 * q:120 - 8 * q], False, q == 7) for q in range(1, 8)],
           ["upr", "one", "bz"], ["pB"])
@@ -471,65 +557,65 @@ def rank_program(g, core, T, topo):
             v(ts(T.oa[:, a], T.oa[:, a], T.v1c[:, 8 + c:9 + c], A.mult), [("oa", a.start, a.stop), "v1h"], [("oa", a.start, a.stop)])
             p(mm(T.pC[:, 0:136], T.oa[:, a], T.th[:, 136 * c:136 * c + 136], c == 0, c == 7), [("oa", a.start, a.stop), "th"], ["pC"])
         cands(1)
-        if t == 0:
-            sums(0, 2, 1)
-            ghosts(2)
         v(tc(T.win[:, 0:136], T.pC[:, 0:136]), ["pC"], ["win"])
         v(tc(T.g16[:], T.win[:, 0:136].indirect(T.dgt[:, 0:1])), ["win", "dgl"], ["g16"])
         v(tt(T.lvf[:], T.win[:, 0:136].indirect(T.dgt[:, 2:3]), T.g16[:], A.subtract), ["win", "dgl", "g16"], ["lvf"])
         v(tc(T.lv[:], T.lvf[:]), ["lvf"], ["lv"])
-        open_keys(16, True)
+        for bank in KB:
+            p(mm(T[bank][:, 0:128], T.one[0:1, 0:128], T.ck[:], True, False), ["one", "ck"], [bank])
         s(act(T.xg[:, 1:257], T.xw[:, 0:1025].indirect(T.lv[:])), ["xw", "lv"], [("xg", 1, 257)])
         v(tc(T.cg[:], T.cv[:, 0:1025].indirect(T.lv[:])), ["cv", "lv"], ["cg"])
-        copies("S", T.xg, "xg", 1, 0, 128, range(11, 16))
-        copies("V", T.xg, "xg", 1, 0, 128, range(0, 11))
-        fetch(192)
-        differ(T.xg, "xg", 193)
-        copies("S", T.xg, "xg", 129, 2048, 64, range(0, 16))
+        copies("S", T.xg, "xg", 1, 0, 128, range(0, XO))
+        copies("V", T.xg, "xg", 1, 0, 128, range(XO, 16))
+        copies("G", T.xg, "xg", 129, 2048, 32, range(0, 16))
+        parts = [signed(T.xg, "xg", 161 + 32 * k, 160 + 32 * k, 512 * k, b) for k, b in enumerate(("pE", "pF", "pH"))]
+        parts[0][0]()
+        s(act(T.cgf[:], T.cv[:, 0:1025].indirect(T.lv[:])), ["cv", "lv"], ["cgf"])
+        parts[1][0]()
+        parts[2][0]()
+        for q in (1, 0):
+            p(mm(T[KB[q]][:, 0:128], T.cgf[:, 128 * q:128 * q + 128], T.idF[:], False, False), ["cgf", "idF"], [KB[q] + "+"])
+        for k, (c, n) in enumerate(((0, 96), (96, 32), (128, 32))):
+            compare(c, n)
+            parts[k][1]()
+        p(mm(T.pD[:, 0:128], T.nil[:], T.c8[:], False, True), ["nil", "c8"], ["pD"])
+        s(act(T.db[:], T.t8[:, 0:1025].indirect(T.lv[:])), [("t8", 0, 1025), "lv"], ["db"])
+        p(mm(T.pC[:, 0:128], T.up64[:], T.c8[:], False, True), ["up64", "c8"], ["pC"])
+        p([mm(T.pB[:, 32 + 8 * q:40 + 8 * q], T.db[:, 128 * q:128 * q + 128], T.dec[:, 8:16]) for q in (0, 1)], ["db", ("dec", 8, 16)], ["pB"])
         if t == 0:
             ghosts(3)
             ghosts(1)
-        compare(0, 128)
-        count(0, 128)
-        signs(192)
-        s(act(T.cgf[:], T.cv[:, 0:1025].indirect(T.lv[:])), ["cv", "lv"], ["cgf"])
-        p([mm(T.pD[:, 128 * q:128 * q + 128], T.cgf[:, 128 * q:128 * q + 128], T.idF[:], False, False) for q in (0, 1)], ["cgf", "idF"], ["pD"])
-        s(act(T.db[:], T.t8[:, 0:1025].indirect(T.lv[:])), [("t8", 0, 1025), "lv"], ["db"])
-        p([mm(T.pB[:, 32 + 8 * q:40 + 8 * q], T.db[:, 128 * q:128 * q + 128], T.dec[:, 8:16]) for q in (0, 1)], ["db", ("dec", 8, 16)], ["pB"])
-        compare(128, 64)
-        count(128, 64)
-        if t == 0:
             s([act(T.jF[:], T.jb[:])] + [act(T.smk[:, EO[b]:EO[b] + 16], T.tri[:], AF.Copy, 0.0, FAR) for b in range(8)], ["jb", "tri", "smk0"], ["jF", "smk"])
             fill3()
         v(tc(T.dI[:, 0:16], T.pB[:, 32:48]), ["pB"], [("dI", 0, 16)])
+        keys(0)
         v(ts(T.dI[:, 16:32], T.dI[:, 0:16], 2047, A.bitwise_and), [("dI", 0, 16)], [("dI", 16, 32)])
-        keys(16)
+        keys(1)
+        v(ts(T.dI[:, 0:16], T.dI[:, 16:32], 1.0, A.add), [("dI", 16, 32)], [("dI", 0, 16)])
         v([ts(T.rz[:, 8:24], T.kx[:, 15:256:16], T.thr[:, t % 2:t % 2 + 1], A.is_lt), excess(16, t)], ["kx", ("thr", t % 2, t % 2 + 1)], [("ki", 0, 16), ("rz", 8, 24)])
         p([mm(T.pB[:, 0:16], T.upr[:, 0:128], T.rz[:, 8:24], True, False), mm(T.pB[:, 0:16], ONE, T.rz[:, 0:16], False, True)], ["upr", "one", "rz"], ["pB"])
-        if not last:
-            p([mm(T.pG[:, 64:65], ONE, T.rz[:, 8 + c:9 + c], c == 0, c == 15) for c in range(16)], ["one", "rz"], ["pG"])
         chosen(16)
         s(act(T.xf[:], T.ki[:, 16:32].indirect(T.ex[:])), [("ki", 16, 32), "ex"], ["xf"])
         v(tc(T.rkI[:, 0:16], T.pB[:, 0:16]), ["pB"], ["rkI"])
         v(tt(T.xe[:], T.ki[:, 16:32].indirect(T.ex[:]), T.mkg[:, 128:384], A.mult), [("ki", 16, 32), "ex", "mkg"], ["xe"])
-        p([mm(T.pA[:, 8 * q + 32 * k:8 * q + 8 + 32 * k], T.xe[:, 128 * q:128 * q + 128], T.gin[:, 8 * k:8 * k + 8]) for k in (0, 1) for q in (0, 1)] +
-          [f for q in (0, 1) for f in (mm(T.pA[:, 16 + 8 * q:24 + 8 * q], T.idb[:], T.duw[:, 8 * q:8 * q + 8], True, False),
-                                       mm(T.pA[:, 16 + 8 * q:24 + 8 * q], T.xe[:, 128 * q:128 * q + 128], T.gin[:, 8:16], False, True))], ["xe", "gin", "idb", "duw"], ["pA"])
+        p([f for q in (0, 1) for f in (mm(T.pA[:, 24 * q:24 * q + 24], T.idb[:], T.duw[:, 24 * q:24 * q + 24], True, False),
+                                       mm(T.pA[:, 24 * q:24 * q + 24], T.xe[:, 128 * q:128 * q + 128], T.gin[:], False, True))], ["xe", "gin", "idb", "duw"], ["pA"])
         p([mm(T.pH[:, 128 * q:128 * q + 128], T.xf[:, 128 * q:128 * q + 128], T.jF[:]) for q in (1, 0)], ["xf", "jF"], ["pH"])
         v([ts(T.loI[:, 0:16], T.rkI[:, 0:16], 15, A.bitwise_and), ts(T.hiI[:, 0:16], T.rkI[:, 0:16], 4, A.arith_shift_right)], ["rkI"], ["loI", "hiI"])
         v(tt(T.ob[:], T.hiI[:, 0:16].indirect(T.ex8[:]), T.ct8[:], A.is_equal), ["hiI", "ex8", "ct8"], ["ob"])
-        v([ts(T.u16s[:, 32:48], T.pA[:, 0:16], -1.0, A.mult, -1.0, A.add), tc(T.sm[:, 48:64], T.pA[:, 32:48]), tt(T.sm[:, 32:48], T.pA[:, 16:32], T.lvf[:], A.max)],
-          ["pA", "lvf"], [("u16s", 32, 48), ("sm", 32, 64)])
         s([act(T.obj[:, 64 * q:64 * q + 64], T.ob[:, 64 * q:64 * q + 64], AF.Copy, 0.0, T.v1c[:, q:q + 1]) for q in (0, 1)], ["ob", "v1c"], ["obj"])
+        v([ts(T.u16s[:, 32:48], T.pA[:, 0:48:3], -1.0, A.mult, -1.0, A.add), tc(T.sm[:, 48:64], T.pA[:, 1:48:3])], ["pA"], [("u16s", 32, 48), ("sm", 48, 64)])
         s(act(T.wv[:], T.tab[:].indirect(T.u16s[:, 32:48]), AF.Identity, RB, MB), ["tab", ("u16s", 32, 48), ("col", 1, 5)], ["wv"])
-        v([tt(T.oa[:, 256:384], T.dI[:, 16:32].indirect(T.ex8[:]), T.ob[:], A.mult), tt(T.oa[:, 0:256], T.loI[:, 0:16].indirect(T.ex[:]), T.lane[:], A.is_equal)],
-          ["loI", "ex", "lane", ("dI", 16, 32), "ex8", "ob"], [("oa", 0, 384)])
-        rhs = (T.ob[:, 0:64], T.ob[:, 64:128], T.oa[:, 256:320], T.oa[:, 320:384])
-        p([mm(T.pC[:, 0:64], T.oa[:, 128 * q:128 * q + 128], T.obj[:, 64 * q:64 * q + 64], q == 0, q == 1) for q in (0, 1)] +
-          [mm(T.pC[:, 64:128], T.oa[:, 128 * (q % 2):128 * (q % 2) + 128], rhs[q], q == 0, q == 3) for q in range(4)], [("oa", 0, 384), "ob", "obj"], ["pC"])
-        eqdays(1, "S")
-        v([tc(T.u16s[:, 0:16], T.sm[:, 32:48])] + ([] if last else [tc(T.smi[:, 16:17], T.pG[:, 64:65])]), [("sm", 32, 48), "pG"], [("u16s", 0, 16), ("smi", 16, 17)])
+        eqdays(1, "S", "pH", range(8))
+        v(tt(T.oa[:, 0:256], T.loI[:, 0:16].indirect(T.ex[:]), T.lane[:], A.is_equal), ["loI", "ex", "lane"], [("oa", 0, 256)])
+        p([mm(T.pC[:, 0:64], T.oa[:, 128 * q:128 * q + 128], T.obj[:, 64 * q:64 * q + 64], q == 0, q == 1) for q in (0, 1)], [("oa", 0, 256), "obj"], ["pC"])
+        v(tt(T.oa[:, 256:384], T.dI[:, 0:16].indirect(T.ex8[:]), T.ob[:], A.mult), [("dI", 0, 16), "ex8", "ob"], [("oa", 256, 384)])
+        p([mm(T.pC[:, 64:128], T.oa[:, 128 * q:128 * q + 128], T.oa[:, 256 + 64 * q:320 + 64 * q], q == 0, q == 1) for q in (0, 1)], [("oa", 0, 384)], ["pC"])
+        if not last:
+            p([mm(T.pG[:, 64:65], ONE, T.rz[:, 8 + c:9 + c], c == 0, c == 15) for c in range(16)], ["one", "rz"], ["pG"])
+        v(tt(T.sm[:, 32:48], T.pA[:, 2:48:3], T.lvf[:], A.max), ["pA", "lvf"], [("sm", 32, 48)])
         v(tc(T.wg[:], T.pC[:, 0:128]), ["pC"], ["wg"])
+        v(tc(T.u16s[:, 0:16], T.sm[:, 32:48]), [("sm", 32, 48)], [("u16s", 0, 16)])
         v(tc(T.gds[:, gla[0]:gda[1]], T.wg[:].indirect(T.dgt[:, 4:5])), ["wg", "dg8"], [("gds", gla[0], gda[1])])
         s(act(T.gxs[:, gxa[0]:gxa[1]], T.xg[:, 0:257].indirect(T.gds[:, gla[0]:gla[1]])), ["xg", ("gds",) + gla], [("gxs",) + gxa])
         send(to, T.gdl[:, gda[0]:gda[1]], T.gds[:, gda[0]:gda[1]], [("gds",) + gda], "gd%d" % t)
@@ -537,8 +623,8 @@ def rank_program(g, core, T, topo):
         ne = len(topo.engines(cores[fro], core))
         landed(("gxl",) + gxa, "gx%d" % t, ne)
         landed(("gdl",) + gda, "gd%d" % t, ne)
-        eqdays(0, "S")
-        v(lambda: V.tensor_copy(T.wb[:, W1 - 1:DUMP + 256].indirect(T.u16s[:, 0:16]), T.wv[:]), ["wv", ("u16s", 0, 16)], [("wb", W1 - 1, DUMP + 256)])
+        eqdays(0, "S", "pH", range(8))
+        v(scatter(T.wb[:, W1 - 1:DUMP + 256].indirect(T.u16s[:, 0:16]), T.wv[:]), ["wv", ("u16s", 0, 16)], [("wb", W1 - 1, DUMP + 256)])
         if last:
             for h in (0, 1):
                 p(mm(T[BK[h]][0:16, :], T.dec[:], T.wb[:, W1 + 512 * h:W1 + 512 * h + 512]), ["dec", ("wb", W1, DUMP)], [BK[h]])
@@ -549,6 +635,8 @@ def rank_program(g, core, T, topo):
             pointers(a1, 0, T.wb, "wb", W1)
             own(a1, 0)
         scan(1)
+        if not last:
+            v(tc(T.smi[:, 16:17], T.pG[:, 64:65]), ["pG"], [("smi", 16, 17)])
         scan(0)
         hh = [] if last else [lambda: pointers2(a1, 0), later("V", ts(T.smi[:, 17:18], T.smi[:, 16:17], 1, A.bitwise_and), [("smi", 16, 17)], [("smi", 17, 18)])]
         weave(dayoffsets(16), hh)
@@ -557,59 +645,66 @@ def rank_program(g, core, T, topo):
                 jump(a1, 0, h)
                 join(0, h)
             after(a1, 0)
-        v(lambda: V.tensor_copy(T.sd[:, 0:2320].indirect(T.u16s[:, 24:32]), T.xg[:, 129:257]), [("xg", 1, 257), ("u16s", 16, 32)], ["sd"])
+        v(scatter(T.sd[:, 0:2320].indirect(T.u16s[:, 24:32]), T.xg[:, 129:257]), [("xg", 1, 257), ("u16s", 16, 32)], ["sd"])
         if not last:
             v(ts(T.thr[:, a1:a1 + 1], T.smi[:, 17:18], BIG, A.mult, 9.0 * BIG, A.add), [("smi", 17, 18)], [("thr", a1, a1 + 1)])
-        v(lambda: V.tensor_copy(T.sd[:, 0:2320].indirect(T.u16s[:, 16:24]), T.xg[:, 1:129]), [("xg", 1, 257), ("u16s", 16, 32)], ["sd"])
+        v(scatter(T.sd[:, 0:2320].indirect(T.u16s[:, 16:24]), T.xg[:, 1:129]), [("xg", 1, 257), ("u16s", 16, 32)], ["sd"])
         gl = T.gdl[:, gda[0]:gda[1]]
-        open_keys(8, False)
         v(tc(T.cg[:, 0:128], T.cw[:, 0:2049].indirect(gl)), ["cw", ("gdl",) + gda], ["cg"])
+
+        def guestdays():
+            s(act(T.cgf[:, 0:128], T.cw[:, 0:2049].indirect(gl)), ["cw", ("gdl",) + gda], ["cgf"])
+            p(mm(T.pD[:, 0:128], T.cgf[:, 0:128], T.idF[:], True, False), ["cgf", "idF"], ["pD"])
+
         if last:
             copies("S", T.gxl, "gxl", gxa[0], 0, 64, range(0, 8))
             copies("V", T.gxl, "gxl", gxa[0], 0, 64, range(8, 16))
             copies("S", T.gxl, "gxl", gxa[0] + 64, 1024, 64, range(0, 16))
-            s(act(T.cgf[:, 0:128], T.cw[:, 0:2049].indirect(gl)), ["cw", ("gdl",) + gda], ["cgf"])
-            p(mm(T.pD[:, 0:128], T.cgf[:, 0:128], T.idF[:], False, False), ["cgf", "idF"], ["pD"])
-            for c in (0, 64):
-                compare(c, 64)
-                count(c, 64)
+            guestdays()
+            for c, n in ((0, 64), (64, 32), (96, 32)):
+                compare(c, n)
         else:
-            copies("V", T.gxl, "gxl", gxa[0], 0, 128, range(0, 16))
+            copies("S", T.gxl, "gxl", gxa[0], 0, 128, range(0, XS))
+            copies("V", T.gxl, "gxl", gxa[0], 0, 128, range(XS, 16))
             sums(a1, 0, 0)
             sums(a1, 0, 1)
             pointers2(a1, 1)
             own(a1, 1)
-            s(act(T.cgf[:, 0:128], T.cw[:, 0:2049].indirect(gl)), ["cw", ("gdl",) + gda], ["cgf"])
-            p(mm(T.pD[:, 0:128], T.cgf[:, 0:128], T.idF[:], False, False), ["cgf", "idF"], ["pD"])
+            guestdays()
             compare(0, 64)
             jump(a1, 1, 0)
             join(1, 0)
             jump(a1, 1, 1)
-            count(0, 64)
             join(1, 1)
             after(a1, 1)
-            compare(64, 64)
+            compare(64, 32)
+            compare(96, 32)
             sums(a1, 1, 0)
             sums(a1, 1, 1)
+        p(mm(T.pD[:, 0:128], T.one[0:1, 0:128], T.ck[:], False, True), ["one", "ck"], ["pD"])
+        if not last:
             pointers2(a1, 2)
-            count(64, 64)
-        keys(8)
+        keys(0)
         if not last:
             own(a1, 2)
             jump(a1, 2, 0)
             join(2, 0)
             jump(a1, 2, 1)
-            sums(a1, 2, 0)
         v(excess(8, t), ["kx", ("thr", t % 2, t % 2 + 1)], [("ki", 0, 16)])
         chosen(8)
         v(tt(T.xe[:], T.ki[:, 16:24].indirect(T.exg[:]), T.mkg[:, 0:256], A.mult), [("ki", 16, 32), "exg", "mkg"], ["xe"])
-        p([mm(T.pA[:, 0:8], T.xe[:, 128:256], T.gin[:, 0:8]), mm(T.pH[:, 0:128], T.xe[:, 0:128], T.jb[:])], ["xe", "gin", "jb"], ["pA", "pH"])
+        p([mm(T.pA[:, 0:24], T.xe[:, 128:256], T.gin[:]), mm(T.pH[:, 0:128], T.xe[:, 0:128], T.jb[:]), mm(T.pB[:, 0:128], T.xe[:, 0:128], T.jb[:])], ["xe", "gin", "jb"], ["pA", "pH", "pB"])
+        v(tc(T.sm[:, 48:56], T.pA[:, 1:24:3]), ["pA"], [("sm", 48, 64)])
+        eqdays(0, "S", "pB", (6, 4, 2))
         if not last:
             after(a1, 2)
             join(2, 1)
+            sums(a1, 2, 0)
             sums(a1, 2, 1)
-        eqdays(0, "V")
+        eqdays(0, "V", "pH", (7, 5, 3, 1, 0))
         weave([] if last else datelist(), [lambda: scan(0)] + dayoffsets(8))
-        v(lambda a=gxa[0]: V.tensor_copy(T.sd[:, 0:2320].indirect(T.u16s[:, 16:24]), T.gxl[:, a:a + 128]), [("gxl",) + gxa, ("u16s", 16, 32)], ["sd"])
+        v(scatter(T.sd[:, 0:2320].indirect(T.u16s[:, 16:24]), T.gxl[:, gxa[0]:gxa[1]]), [("gxl",) + gxa, ("u16s", 16, 32)], ["sd"])
     copy("Y", T.ys[:], T.sd[:, 1:2049], ["sd"], [])
+    for i in order(steps):
+        steps[i][1]()
     finish([("ls", sent[0])])

@@ -4,7 +4,9 @@ BIG = 65536.0
 LOW = -1073741824.0
 TINY = 2.0 ** -110
 FAR = 4096.0
+STEP16 = 1.5 * 2 ** 27
 RO = 4
+D0 = 2048
 F, B, H, I, U = "float32", "bfloat16", "float16", "int32", "uint16"
 W3A, W2A, GA, W1, DUMP, GB, W2B, W3B, WEND = 0, 1024, 2048, 2833, 3857, 4128, 4912, 5936, 6960
 WIN = (((GA, DUMP, W1), (W2A, GA + 769, W2A), (W3A, GA + 769, W3A)), ((W1 - 1, GB + 769, W1), (GB, W3B, W2B), (GB, WEND, W3B)))
@@ -12,23 +14,23 @@ GH = (GA, GB)
 EW = [16 * (b + 1) for b in range(8)]
 EO = [8 * b * (b + 1) for b in range(9)]
 SB = {
-    "anI": (64, I), "ofI": (112, I), "snI": (48, I), "wkb": (2048, B), "xw": (1040, B), "sd": (2320, B),
+    "anI": (64, I), "ofI": (112, I), "snI": (48, I), "wkb": (2048, B), "xw": (1040, B), "sd": (D0 + 2064, B),
     "pI": (3, I), "pp": (3, F), "n16": (16, I), "n144": (144, B), "lmc": (16, F), "pw": (16, F), "cc": (32, F), "col": (24, F), "hi16": (16, F), "tc": (16, F),
     "tab": (2048, B), "idb": (128, B), "idF": (128, F), "jF": (128, F), "jb": (128, B), "upr": (256, B), "amb": (128, B), "nid": (128, B),
     "one": (128, B), "seven": (128, B), "m1k": (128, B), "gin": (24, B), "gib": (16, B), "gik": (16, B), "zp": (864, H), "zd": (144, H), "dec": (16, B),
     "mkg": (384, B), "lane": (256, B), "segm": (128, B), "ct8": (128, B), "ex": (16, U), "exg": (16, U), "ex8": (8, U), "dgt": (8, U), "v1c": (16, F),
     "smk": (576, B), "tri": (16, F), "du": (16, F), "duw": (48, H), "anl": (64, U), "ofl": (112, U), "an1": (128, F),
     "wb": (WEND, B), "g0": (1024, B), "g1": (1024, B), "t8": (1040, B), "l0": (64, U), "l1": (64, U), "l2": (64, U), "sl": (48, U), "cw": (2056, F), "sg": (2048, B),
-    "ldI": (128, I), "lfd": (64, U), "cv": (1032, F), "cmp": (3072, B), "xr": (3072, B), "sgb": (1536, B), "sgn": (1536, B), "bz": (120, B), "rz": (24, B), "rkI": (64, I), "loI": (64, I), "hiI": (16, I), "lo2": (128, B), "obj": (128, B), "c8b": (8, B),
-    "oa": (1024, H), "ob": (128, B), "th": (1088, B), "win": (144, F), "wg": (128, F), "g16": (16, F), "lv": (16, U), "lvf": (16, F),
-    "xg": (272, B), "cg": (256, U), "cgf": (256, F), "db": (256, B), "dI": (32, I), "kx": (256, F), "ki": (32, I), "sm": (64, F), "smi": (32, I), "u16s": (64, U),
-    "thr": (2, F), "xe": (256, H), "xf": (256, F), "wv": (256, B), "eq": (1152, B), "scn": (1152, B), "yb": (1024, F),
-    "ghs": (2304, B), "gxs": (512, B), "gxl": (512, B), "gds": (64, U), "gdl": (64, U),
+    "ldI": (128, I), "lfd": (64, U), "cv": (1032, F), "cmp": (3072, B), "xr": (3072, B), "sgb": (1536, B), "sgn": (1536, B), "bz": (120, B), "rz": (24, B), "rkI": (64, I), "loI": (64, I), "hl": (32, F), "c75": (16, B), "lo2": (128, B), "obj": (128, B), "c8b": (8, B),
+    "oa": (1024, H), "ob": (128, B), "th": (1088, B), "win": (144, F), "wg": (128, F), "dif": (144, F), "lv": (16, U), "lvf": (16, F),
+    "xg": (1088, B), "cg": (256, U), "cgf": (256, F), "db": (256, B), "dI": (32, I), "kx": (256, I), "ki": (32, I), "sm": (96, F), "smi": (32, I), "u16s": (64, U),
+    "xe": (256, H), "xf": (256, F), "wv": (256, B), "eq": (1152, B), "scn": (1152, B), "yb": (1024, F),
+    "ghs": (2304, B), "xal": (1088, B), "gx": (128, B), "xt": (128, B), "rep": (512, B), "gds": (64, U), "gdl": (64, U),
 }
 SCRATCH = {k: ("sbuf", [128, n], d) for k, (n, d) in SB.items()}
-SCRATCH.update({"ck": ("sbuf", [1, 128], B), "c8": ("sbuf", [1, 128], B), "up64": ("sbuf", [1, 128], B), "nil": ("sbuf", [1, 128], B), "n256": ("sbuf", [1, 512], B)})
+SCRATCH.update({"ck": ("sbuf", [1, 128], B), "c8": ("sbuf", [1, 128], B), "up64": ("sbuf", [1, 128], B), "thr": ("sbuf", [1, 256], B), "n256": ("sbuf", [1, 512], B)})
 LISTS = [k for k, (n, d) in SB.items() if d == U] + ["dgl", "dg8", "pick"]
-GATHER, SCATTER, PE, WAKE, LOAD, FLIGHT, PASSES = 1.56, 3.5, 0.55, 100, 2500, 2500, 4
+GATHER, SCATTER, PE, WAKE, LOAD, FLIGHT, PASSES = 1.75, 4.2, 0.55, 100, 2500, 1800, 4
 PS = ("pA", "pB", "pC", "pD", "pE", "pF", "pG", "pH")
 SCRATCH.update({k: ("psum", [128, 512], F) for k in PS})
 SEMAPHORES = ["qV", "qS", "qP", "qG", "ls"] + ["d%d" % i for i in range(11)] + ["gh%d" % t for t in range(3)] + ["gx%d" % t for t in range(RO)] + ["gd%d" % t for t in range(RO)]
@@ -97,15 +99,15 @@ def layer(g, T):
         for q in cnt:
             if cnt[q]:
                 g.wait_ge(T.sem["q" + q], cnt[q])
-        for i in range(dma[0]):
-            g.wait_ge(T.sem["d%d" % i], 16)
         for s, n in extra:
             g.wait_ge(T.sem[s], n)
+        for i in range(dma[0]):
+            g.wait_ge(T.sem["d%d" % i], 16)
 
     return op, copy, landed, prepare, finish
 
 
-def order(steps):
+def order(steps, aside):
     n = len(steps)
     pre = [set() for _ in steps]
     hist = {}
@@ -131,7 +133,7 @@ def order(steps):
             q, busy = steps[i][0], steps[i][4]
             t = steps[i][5] if back else 0.0
             for j in before[i]:
-                t = max(t, end[j] + steps[i if back else j][5] + (0 if q == steps[j][0] == "P" else WAKE))
+                t = max(t, end[j] + (0 if q == steps[j][0] in "PG" else steps[i if back else j][5] + WAKE))
             row = taken.setdefault(q, [])
             k = len(row)
             while k and row[k - 1][1] > t:
@@ -143,7 +145,18 @@ def order(steps):
             end[i] = t + busy
         return end
 
-    seq, best = list(range(n)), None
+    seq, best, done = [], None, set()
+
+    def take(i):
+        done.add(i)
+        for j in sorted(pre[i] - done):
+            if j not in done:
+                take(j)
+        seq.append(i)
+
+    for i in [i for i in range(n) if i not in aside] + sorted(aside):
+        if i not in done:
+            take(i)
     for _ in range(PASSES):
         end = place(seq, pre, False)
         pos = {i: k for k, i in enumerate(seq)}
@@ -173,7 +186,12 @@ def rank_program(g, core, T, topo):
     issue, dma, arrive, prepare, finish = layer(g, T)
     V, S, P = g.vector, g.scalar, g.tensor
     sent = [0]
-    steps = []
+    steps, aside = [], set()
+
+    def beside(f, *args):
+        a = len(steps)
+        f(*args)
+        aside.update(range(a, len(steps)))
 
     def cols(a):
         return a.shape[1]
@@ -185,13 +203,14 @@ def rank_program(g, core, T, topo):
         fns = fns if isinstance(fns, list) else [fns]
         gather = any((r if isinstance(r, str) else r[0]) in LISTS for r in reads)
         busy = sum(f[2] if gather else f[1]() for f in fns)
-        steps.append((q, lambda: issue(q, [f[0] for f in fns], reads, writes), reads, writes, busy, 0))
+        real = [[r for r in rs if r[0] != "~"] for rs in (reads, writes)]
+        steps.append((q, lambda: issue(q, [f[0] for f in fns], *real), reads, writes, busy, 0))
 
     def copy(q, out, in_, reads, writes, lag=LOAD):
         steps.append((q, lambda: dma(q, out, in_, reads, writes), reads, writes, 50, lag))
 
     def landed(region, sem, count):
-        steps.append(("N", lambda: arrive(region, sem, count), [sem], [region], 0, FLIGHT))
+        steps.append(("N", lambda: arrive(region, sem, count), [sem], [region], 0, 0))
 
     def v(f, r, w):
         op("V", f, r, w)
@@ -208,8 +227,8 @@ def rank_program(g, core, T, topo):
     def scatter(o, i):
         return lambda: V.tensor_copy(o, i), None, 50 + SCATTER * cols(i)
 
-    def tt(o, a, b, f):
-        return lambda: V.tensor_tensor(o, a, b, f), lambda: max(64, 2 * cols(o)), 50 + GATHER * cols(o)
+    def tt(o, a, b, f, cycles=2):
+        return lambda: V.tensor_tensor(o, a, b, f), lambda: max(64, cycles * cols(o)), 50 + GATHER * cols(o)
 
     def ts(o, a, s1, f1, s2=None, f2=None):
         return (lambda: V.tensor_scalar(o, a, s1, None, f1) if f2 is None else V.tensor_scalar(o, a, s1, s2, f1, f2)), lambda: max(64, cols(o) * narrow(o, a)), 50 + GATHER * cols(o)
@@ -229,14 +248,21 @@ def rank_program(g, core, T, topo):
     def later(q, f, r, w):
         return lambda: op(q, f, r, w)
 
-    def send(dst, out, in_, reads, sem):
+    def lanes(a, b, spare=False):
+        mine = topo.engines(cores[a], cores[b])
+        shared = min((topo.engines(cores[a], c) for c in cores if c != cores[a]), key=len)
+        return [e for e in mine if e not in shared] if spare and len(mine) > len(shared) else mine
+
+    def send(dst, out, in_, reads, sem, spare=False):
+        es = lanes(rank, dst, spare)
+
         def run():
-            d = cores[dst]
             prepare("G", reads, [])
-            rid, pid = topo.addr(d, core)
-            g.remote_dma(out, in_, T.sem[sem], T.sem.ls, pid, rid, topo.mask(core, d))
-            sent[0] += len(topo.engines(core, d))
-        steps.append(("G", run, reads, [(sem, dst, dst + 1)], 300 if any(x[3][:1] == [("gh0", (rank + 2) % N, (rank + 2) % N + 1)] for x in steps) else 2500, 0))
+            rid, pid = topo.addr(cores[dst], core)
+            g.remote_dma(out, in_, T.sem[sem], T.sem.ls, pid, rid, sum(1 << e for e in es))
+            sent[0] += len(es)
+        steps.append(("G", run, reads, [(sem + "s", dst, dst + 1)], 300 if any(x[0][0] == "D" for x in steps) else 2500, FLIGHT))
+        steps.append(("D%d" % es[0], lambda: None, [(sem + "s", dst, dst + 1)], [(sem, dst, dst + 1)], 600 + 5 * cols(in_), 0))
 
     def iota(name, view, pat, base, ch, fl=True):
         f = (lambda: g.iota(view, pat, base, ch, allow_small_or_imprecise_dtypes=True)) if fl else (lambda: g.iota(view, pat, base, ch))
@@ -254,12 +280,10 @@ def rank_program(g, core, T, topo):
     def lm(i):
         return T.lmc[:, i:i + 1]
 
-    v([ms(T.xw[:, 0:1], LOW), ms(T.sd[:, 0:1], 0.0), ms(T.one[:], 1.0)], [], [("xw", 0, 16), ("sd", 0, 16), "one"])
+    v([ms(T.xw[:, 0:1], LOW), ms(T.sd[:, D0:D0 + 1], 0.0), ms(T.one[:], 1.0)], [], [("xw", 0, 16), ("sd", 0, 16), "one"])
     copy("Y", T.anI[:], T.an0[:], [], ["anI"])
     copy("Y", T.ofI[:], T.of0[:], [], ["ofI"])
-    copy("S", T.wkb[:], T.wk[:], [], ["wkb"])
-    copy("Y", T.sd[:, 1:2049], T.s0[:], [], [("sd", 1, 2049)])
-    copy("Y", T.xw[:, 1:1025], T.x[:], [], [("xw", 1, 1025)])
+    copy("S", T.wkb[:], T.wk[:], ["one"], ["wkb"], 4000)
     copy("Y", T.snI[:], T.snd[:], [], ["snI"])
     ONE = T.one[:, 0:128]
     iota("pI", T.pI[:, 0:1], [[0, 1]], 0, 1, False)
@@ -270,14 +294,16 @@ def rank_program(g, core, T, topo):
     select("up0", T.upr[:, 128:256], ONE, "one", [[1, 128]], A.is_gt, 0.0, 0, -1)
     iota("v1c", T.v1c[:, 0:8], [[128, 8]], 1, 1)
     select("upr", T.upr[:, 0:128], T.upr[:, 128:256], "up0", [[-1, 128]], A.not_equal, -4096.0, 0, 1)
-    iota("du", T.du[:], [[16, 16]], 2056, 0)
+    iota("du", T.du[:], [[16, 16]], 0, 0)
     iota("lane", T.lane[:], [[0, 16], [1, 16]], 0, 0)
-    for name, a, b, c in (("c8b", 0, 8, 8), ("bz", 0, 56, 0), ("t8", 0, 1, 0), ("cv", 0, 1, 1), ("cw", 0, 1, 1), ("thr", 0, 1, 9 * 65536), ("rz", 0, 8, 0), ("mkg", 0, 128, 1), ("c8", 0, 128, 8 * 65536), ("nil", 0, 128, 0)):
+    for name, a, b, c in (("c8b", 0, 8, 8), ("bz", 0, 56, 0), ("t8", 0, 1, 0), ("cv", 0, 1, 1), ("cw", 0, 1, 1), ("thr", 0, 128, -9 * 65536), ("rz", 0, 8, 0), ("mkg", 0, 128, 1), ("c8", 0, 128, 8 * 65536)):
         iota((name, a, b), T[name][:, a:b], [[0, b - a]], c, 0)
+    iota("rep", T.rep[:], [[-1, 32], [0, 16]], 0, 1)
+    iota("th0", T.th[:, 0::17], [[0, 64]], -1, 0)
     iota("ck", T.ck[:], [[0, 8], [-4096, 16]], 61440, 0)
     select("up64", T.up64[:], T.one[0:1, 0:128], "one", [[1, 128]], A.is_ge, 0.0, -32, 0)
     select("segm", T.segm[:], ONE, "one", [[0, 8], [1, 16]], A.is_gt, 0.0, 0, 0)
-    iota("ct8", T.ct8[:], [[0, 16], [1, 8]], -256, 0)
+    iota("ct8", T.ct8[:], [[0, 16], [16, 8]], -4096, 0)
     select("jb0", T.jb[:], ONE, "one", [[1, 128]], A.not_equal, -1.0, -127, 1)
     iota(("wb", GB + 769, W2B), T.wb[:, GB + 769:W2B], [[0, W2B - GB - 769]], 0, 0)
     select("jb", T.jb[:], T.jb[:], "jb0", [[1, 128]], A.is_equal, 0.0, -127, 1)
@@ -290,6 +316,8 @@ def rank_program(g, core, T, topo):
     v([ts(T.pI[:, 1:2], T.pI[:, 0:1], 15, A.bitwise_and), ts(T.pI[:, 2:3], T.pI[:, 0:1], 4, A.arith_shift_right)], ["pI"], ["pI2"])
     v([ms(T.pw[:, 0:1], 1.0), ms(T.pw[:, 1:2], 2.0)], [], ["pwa"])
     v([tc(P15, T.pI[:, 1:2]), tc(P4, T.pI[:, 2:3]), tc(PC, T.pI[:, 0:1])], ["pI", "pI2"], ["pp"])
+    copy("Y", T.sd[:, D0 + 1:D0 + 2049], T.s0[:], ["pp"], [("sd", 1, 2049)], 12000)
+    copy("Y", T.xw[:, 1:1025], T.x[:], ["pp"], [("xw", 1, 1025)], 12000)
     v([ms(T.pw[:, b:b + 1], float(1 << b)) for b in range(2, 5)], [], ["pw"])
     v(ts(T.lmc[:], N16, P15, A.is_equal), ["n16", "pp"], ["lmc"])
     v([ms(T.tab[:, 0:1], 0.0), ms(T.hi16[:, 0:1], 0.0)], [], [("tab", 0, 1), ("hi16", 0, 1)])
@@ -305,7 +333,10 @@ def rank_program(g, core, T, topo):
       [("gib", 0, 8)], [("gib", 8, 16), "gik", "gin"])
 
     def double(name, first, n):
-        return [later("V", ts(T[name][:, 1 << b:2 << b], T[name][:, 0:1 << b], T.cc[:, first + b:first + b + 1], A.add), [(name, 0, 1 << b), ("cc", 0, 16)], [(name, 1 << b, 2 << b)]) for b in range(n)]
+        c = [T.cc[:, first + b:first + b + 1] for b in range(n)]
+        return [later("V", [ts(T[name][:, 1 << b:2 << b], T[name][:, 0:1 << b], c[b], A.add)] +
+                      ([ts(T[name][:, 2 << b:3 << b], T[name][:, 0:1 << b], c[b + 1], A.add), ts(T[name][:, 3 << b:4 << b], T[name][:, 0:1 << b], c[b], A.add, c[b + 1], A.add)] if b + 1 < n else []),
+                      [(name, 0, 1 << b), ("cc", 0, 16)], [(name, 1 << b, min(4 << b, 1 << n))]) for b in range(0, n, 2)]
 
     weave(double("tab", 0, 7), double("hi16", 7, 4))
     v([tc(T.anl[:], T.anI[:]), tc(T.ofl[:], T.ofI[:])], ["anI", "ofI"], ["anl", "ofl"])
@@ -314,7 +345,8 @@ def rank_program(g, core, T, topo):
 
     WKB = ("pB", "pC", "pH", "pD")
     for b, bank in enumerate(WKB):
-        p([mm(T[bank][:], T.seven[:], T.wkb[:, 512 * b:512 * b + 512], True, False), mm(T[bank][:], T.one[0:1, 0:128], T.n256[:], False, True)], ["seven", "wkb", "one", "n256"], [bank])
+        p(mm(T[bank][:], T.seven[:], T.wkb[:, 512 * b:512 * b + 512], True, False), ["seven", "wkb"], [bank])
+        p(mm(T[bank][:], T.one[0:1, 0:128], T.n256[:], False, True), ["one", "n256"], [bank])
 
     def sign(b):
         bank = WKB[b]
@@ -322,8 +354,9 @@ def rank_program(g, core, T, topo):
 
     def weeks2(b):
         bank = WKB[b]
-        p([mm(T[bank][:], T.seven[:], T.wkb[:, 512 * b:512 * b + 512], True, False), mm(T[bank][:], T.one[0:1, 0:128], T.n256[:], False, False),
-           mm(T[bank][:], T.m1k[:], T.sg[:, 512 * b:512 * b + 512], False, True)], ["seven", "wkb", "one", "n256", "m1k", ("sg", 512 * b, 512 * b + 512)], [bank])
+        p(mm(T[bank][:], T.seven[:], T.wkb[:, 512 * b:512 * b + 512], True, False), ["seven", "wkb"], [bank])
+        p(mm(T[bank][:], T.one[0:1, 0:128], T.n256[:], False, False), ["one", "n256"], [bank])
+        p(mm(T[bank][:], T.m1k[:], T.sg[:, 512 * b:512 * b + 512], False, True), ["m1k", ("sg", 512 * b, 512 * b + 512)], [bank])
 
     def weeks3(b):
         bank = WKB[b]
@@ -398,10 +431,10 @@ def rank_program(g, core, T, topo):
 
     z12 = zed(1, 2)
     fills = [
-        [z12, later("V", [ts(T.pw[:, 5:10], T.pw[:, 0:5], 32.0, A.mult), ms(T.pw[:, 10:11], 1024.0), ms(T.xg[:, 0:1], LOW), ts(TC[5], P4, 17.0, A.mult, P15, A.add)],
-                    ["pw", "pwa", "pp"], ["pw2", ("xg", 0, 1), ("tc", 5, 6)])],
-        [later("V", [tt(T.cc[:, 16:27], T.pw[:, 0:11], T.lmc[:, 0:11], A.mult), tc(T.dgt[:, 0:1], TC[5]), ts(T.dgt[:, 2:3], TC[5], 1.0, A.add)],
-               ["pw", "pwa", "pw2", "lmc", ("tc", 5, 6)], [("cc", 16, 32), "dgl"])],
+        [z12, later("V", [ts(T.pw[:, 5:10], T.pw[:, 0:5], 32.0, A.mult), ms(T.pw[:, 10:11], 1024.0), ms(T.xg[:, 0::272], LOW), ts(TC[5], P4, 17.0, A.mult, P15, A.add),
+                          ts(T.smi[:, 20:21], T.pI[:, 0:1], 96, A.bitwise_and)], ["pw", "pwa", "pp", "pI"], ["pw2", "xg", ("tc", 5, 6), ("smi", 20, 21)])],
+        [later("V", [tt(T.cc[:, 16:27], T.pw[:, 0:11], T.lmc[:, 0:11], A.mult), tc(T.dgt[:, 0:1], TC[5]), tc(TC[10], T.smi[:, 20:21])],
+               ["pw", "pwa", "pw2", "lmc", ("tc", 5, 6), ("smi", 20, 21)], [("cc", 16, 32), "dgl", ("tc", 10, 11)])],
         [later("V", [sweep(T.cc[:, 0:11], T.cc[:, 16:27], T.cc[:, 16:27], A.max, A.max), ts(T.sl[:], T.snI[:], 1.0, A.add), tc(T.ex[:], N16),
                      ts(TC[2], P15, 8.0, A.is_ge), ts(TC[3], P4, 8.0, A.mult, P15, A.add), ts(T.smi[:, 0:16], N16, 7, A.bitwise_and), ts(T.smi[:, 16:17], T.pI[:, 0:1], 7, A.bitwise_and)],
                [("cc", 16, 32), "snI", "n16", "pp", "pI"], [("cc", 0, 16), "sl", "ex", ("tc", 2, 4), "smi"])],
@@ -410,10 +443,14 @@ def rank_program(g, core, T, topo):
         [later("V", [ts(T.dgt[:, 4:5], TC[2], 56.0, A.mult, TC[3], A.add), ts(TC[6], T.smi[:, 16:17], 1.0, A.add), ts(TC[7], T.smi[:, 16:17], 2.0, A.add, 8.0, A.mult),
                      ts(TC[8], TC[2], float(EO[8]), A.mult, -1.0, A.add), ts(T.tri[:], N16, P15, A.add, 15.5, A.is_lt), ts(T.mkg[:, 128:384], T.lane[:], P15, A.is_equal), ms(T.duw[:], 0.0),
                      ts(T.du[:], T.du[:], P15, A.add)], [("tc", 2, 4), "smi", "n16", "pp", "lane", "du"], ["dg8", ("tc", 6, 9), "tri", ("mkg", 128, 384), "duw", "du"]),
-         later("V", [ts(T.dgt[:, 6:7], TC[6], TC[7], A.mult, TC[8], A.add), ts(T.duw[:, 2::3], T.du[:], float(DUMP - W1 + 1 - 2056), A.add), ts(T.dec[:, 8:16], G8, P4, A.is_equal, WB, A.mult),
+         later("V", [ts(T.dgt[:, 6:7], TC[6], TC[7], A.mult, TC[8], A.add), ts(T.duw[:, 2::3], T.du[:], float(DUMP - W1 + 1), A.add), ts(T.dec[:, 8:16], G8, P4, A.is_equal, WB, A.mult),
                      ts(TC[9], lm(13), 1024.0, A.mult, WL, A.add)], [("tc", 6, 9), "du", "duw", "n16", "pp", ("cc", 0, 16), "lmc", ("col", 5, 6)], ["pick", "duw", ("dec", 8, 16), ("tc", 9, 10)])]]
 
+    fills[4].append(later("V", ts(T.rep[:], T.rep[:], TC[10], A.is_equal), ["rep", ("tc", 10, 11)], ["rep"]))
+
     def fill3():
+        v(ts(T.lane[:], T.lane[:], -7.5, A.add), ["lane"], ["lane"])
+        v(ms(T.c75[:], -7.5), [], ["c75"])
         z = zed(0, 3, 4, 5)
         v([tc(T.wb[:, GB + 768:GB + 769], RB), ts(DB, PC, 8.0, A.is_lt, -64.0 * 1057, A.mult), ts(T.dec[:, 0:8], G8, P4, A.is_equal, TC[9], A.mult)],
           [("col", 4, 6), "pp", "n16", ("tc", 9, 10)], [("wb", GB + 768, GB + 769), ("col", 7, 8), ("dec", 0, 8)])
@@ -427,9 +464,9 @@ def rank_program(g, core, T, topo):
             f()
         if l > 0:
             weeks2(l - 1)
-        join(l, 0)
         if l == 2:
             after(0, l)
+        join(l, 0)
         join(l, 1)
         if l < 2:
             sign(2 * l)
@@ -445,16 +482,18 @@ def rank_program(g, core, T, topo):
     weave(datelist())
 
     KB = ("pD", "pC")
-    XS, XO = 2, 2
+    DAYS = T.sd[:, D0:D0 + 2049]
+    XS, XO = 2, 1
 
     def keys(q):
         v(sweep(T.kx[:, 128 * q:128 * q + 128], T.segm[:], T[KB[q]][:, 0:128], A.mult, A.max), ["segm", KB[q]], [("kx", 128 * q, 128 * q + 128)])
 
-    def excess(w, t):
-        return ts(T.ki[:, 0:w], T.kx[:, 15:16 * w:16], T.thr[:, t % 2:t % 2 + 1], A.subtract, 0.0, A.max)
+    def bound(bank, t, start=False, stop=False):
+        a = 128 * (t % 2)
+        p(mm(T[bank][:, 0:128], T.one[0:1, 0:128], T.thr[:, a:a + 128], start, stop), ["one", ("thr", a, a + 128)], [bank + ("" if start or stop else "+")])
 
     def chosen(w):
-        v(ts(T.ki[:, 16:16 + w], T.ki[:, 0:w], 4095, A.bitwise_and), [("ki", 0, 16)], [("ki", 16, 32)])
+        return ts(T.ki[:, 16:16 + w], T.kx[:, 15:16 * w:16], 4095, A.bitwise_and)
 
     def eqdays(h, q, bank, bs):
         o = EO[8] * h
@@ -472,26 +511,25 @@ def rank_program(g, core, T, topo):
 
     def dayoffsets(w):
         return [
-            later("V", tt(T.sm[:, 0:16], T.scn[:].indirect(T.dgt[:, 6:7]), T.du[:], A.subtract), ["scn", "pick", "du"], [("sm", 0, 16)]),
-            later("V", tt(T.sm[:, 16:16 + w], T.sm[:, 0:w], T.pA[:, 0:3 * w:3], A.min), [("sm", 0, 16), "pA"], [("sm", 16, 32)]),
-            later("V", ts(T.u16s[:, 16:16 + w], T.sm[:, 16:16 + w], -1.0, A.mult), [("sm", 16, 32)], [("u16s", 16, 32)])]
+            later("V", tt(T.sm[:, 16:32], T.scn[:].indirect(T.dgt[:, 6:7]), T.sm[:, 0:16], A.min), ["scn", "pick", ("sm", 0, 16)], [("sm", 16, 32)]),
+            later("V", tc(T.u16s[:, 16:16 + w], T.sm[:, 16:16 + w]), [("sm", 16, 32)], [("u16s", 16, 32)])]
 
     def copies(q, src, sname, so, dst, n, ks):
         f = {"S": act, "V": tc, "G": keep}[q]
-        op(q, [f(T.xr[:, dst + k:dst + 16 * n:16], src[:, so:so + n]) for k in ks], [(sname, so, so + n)], [("xr" + q, dst, dst + 16 * n)])
+        if len(ks):
+            op(q, [f(T.xr[:, dst + k:dst + 16 * n:16], src[:, so:so + n]) for k in ks], [(sname, so, so + n)], [("xr" + q, dst, dst + 16 * n)])
 
-    def compare(c0, n):
+    def compare(c0, n, *mark):
         a = slice(16 * c0, 16 * c0 + 16 * n)
-        v(tt(T.cmp[:, a], T.sd[:, 0:2049].indirect(T.cg[:, c0:c0 + n]), T.xr[:, a], A.is_lt), [("sd", 0, 2049), "cg"] + [("xr" + q, a.start, a.stop) for q in "SVG"], [("cmp", a.start, a.stop)])
+        v(tt(T.cmp[:, a], DAYS.indirect(T.cg[:, c0:c0 + n]), T.xr[:, a], A.is_lt), ["sd", ("cg", c0, c0 + n)] + [("xr" + q, a.start, a.stop) for q in "SVG"], [("cmp", a.start, a.stop)] + list(mark))
         bank = KB[c0 // 128]
         p([mm(T[bank][c0 % 128:c0 % 128 + n, k:128:16], T.cmp[:, 16 * c0 + k:16 * c0 + 16 * n:16], T.gik[:, 0:8], False, False) for k in range(16)],
           [("cmp", 16 * c0, 16 * c0 + 16 * n), "gik"], [bank + "+"])
 
-    def signed(src, sname, so, c0, o, b):
+    def signed(c0, o, b):
         def first():
-            p(mm(T[b][:], T.nil[:], T.n256[:], True, False), ["nil", "n256"], [b])
-            p([mm(T[b][:, k::16], T.idb[:], src[:, so:so + 32], False, False) for k in range(16)], [(sname, so, so + 32), "idb"], [b])
-            s(act(T.sgb[:, o:o + 512], T.sd[:, 0:2049].indirect(T.cg[:, c0:c0 + 32])), [("sd", 0, 2049), "cg"], [("sgb", o, o + 512)])
+            p(mm(T[b][:], T.xt[c0 % 128:c0 % 128 + 32, :], T.rep[c0 % 128:c0 % 128 + 32, :], True, False), ["xt", "rep"], [b])
+            s(act(T.sgb[:, o:o + 512], DAYS.indirect(T.cg[:, c0:c0 + 32])), ["sd", ("cg", c0, c0 + 32)], [("sgb", o, o + 512)])
             p(mm(T[b][:], T.nid[:], T.sgb[:, o:o + 512], False, True), [("sgb", o, o + 512), "nid"], [b])
 
         def second():
@@ -502,53 +540,58 @@ def rank_program(g, core, T, topo):
     for t in range(RO):
         last = t == RO - 1
         a1 = (t + 1) % 2
-        gxa, gla, gda, gha = (128 * t, 128 * t + 128), (16 * t, 16 * t + 8), (16 * t + 8, 16 * t + 16), (768 * t, 768 * t + 768)
+        x0, gda, gha = 272 * t, (16 * t, 16 * t + 16), (768 * t, 768 * t + 768)
+        GX = "S" if last else "V"
         to, fro = (rank + 1 + t % (N - 1)) % N, (rank - 1 - t % (N - 1)) % N
 
-        def ghosts(d):
+        def ghosts(k, q="S"):
+            d = sorted(range(1, N), key=lambda e: len(lanes(rank, (rank + e) % N)))[k]
             a, b = gha[0] + 256 * (d - 1), GH[a1] + 256 * (d - 1)
-            s(act(T.ghs[:, a:a + 256], T.t8[:, 0:1025].indirect(T.sl[:, 16 * d - 16:16 * d])), [("t8", 0, 1025), "sl"], [("ghs", a, a + 256)])
-            send((rank + d) % N, T.wb[:, b:b + 256], T.ghs[:, a:a + 256], [("ghs", a, a + 256)], "gh%d" % t)
-            if d == 1:
-                landed(("wb", GH[a1], GH[a1] + 768), "gh%d" % t, sum(len(topo.engines(cores[(rank - e) % N], core)) for e in range(1, N)))
+            op(q, (act if q == "S" else tc)(T.ghs[:, a:a + 256], T.t8[:, 0:1025].indirect(T.sl[:, 16 * d - 16:16 * d])), [("t8", 0, 1025), "sl"] + ["~db"] * (k == N - 2), [("ghs", a, a + 256), "~g%d" % k])
+            send((rank + d) % N, T.wb[:, b:b + 256], T.ghs[:, a:a + 256], [("ghs", a, a + 256)], "gh%d" % t, True)
+            if k == N - 2:
+                landed(("wb", GH[a1], GH[a1] + 768), "gh%d" % t, sum(len(lanes((rank - e) % N, rank, True)) for e in range(1, N)))
 
-        def cands(h):
-            s(act(T.cv[:, 1 + 512 * h:513 + 512 * h], T.cw[:, 0:2049].indirect(T.lfd[:, 32 * h:32 * h + 32])), ["cw", "lfd"], [("cv", 1 + 512 * h, 513 + 512 * h)])
+        def cands(h, q="S"):
+            op(q, (act if q == "S" else tc)(T.cv[:, 1 + 512 * h:513 + 512 * h], T.cw[:, 0:2049].indirect(T.lfd[:, 32 * h:32 * h + 32])), ["cw", "lfd", "~g0"], [("cv", 1 + 512 * h, 513 + 512 * h)])
 
-        nv = 3 if t else 4
         if t == 0:
             sums(0, 2, 0)
             sums(0, 2, 1)
-            ghosts(2)
+            ghosts(0)
             for b in (2, 3):
                 weeks2(b)
                 weeks3(b)
-        else:
-            if not last:
-                ghosts(2)
-                ghosts(3)
-            p(mm(T.pH[:, 0:256], T.idb[:], T.xw[:, 769:1025], True, False), ["idb", ("xw", 1, 1025)], ["pH"])
-            s(act(T.sgb[:, 0:256], T.sd[:, 0:2049].indirect(T.lfd[:, 48:64])), [("sd", 0, 2049), "lfd"], ["sgb"])
-            p(mm(T.pH[:, 0:256], T.nid[:], T.sgb[:, 0:256], False, True), ["nid", "sgb"], ["pH"])
-            if not last:
-                ghosts(1)
-            s(act(T.sgn[:, 0:256], T.pH[:, 0:256], AF.Sign, TINY), ["pH"], [("sgn", 0, 512)])
-        cands(0)
+        onS = ((7, 8, "pH"), (6, 7, "pC")) if t else ()
+        onV = ((0, 3), (3, 6)) if t else ((0, 4), (4, 8))
+        for c0, c1, b in onS:
+            a, n = 128 * c0, 128 * (c1 - c0)
+            p(mm(T[b][:, 0:n], T.idb[:], T.xw[:, 1 + a:1 + a + n], True, False), ["idb", ("xw", 1, 1025)], [b])
+            s(act(T.sgb[:, a:a + n], DAYS.indirect(T.lfd[:, 8 * c0:8 * c1])), ["sd", "lfd"], [("sgb", a, a + n)])
+            p(mm(T[b][:, 0:n], T.nid[:], T.sgb[:, a:a + n], False, True), ["nid", ("sgb", a, a + n)], [b])
         for h in (0, 1):
-            a = slice(128 * nv * h, 128 * nv * h + 128 * nv)
-            v(tt(T.cmp[:, a], T.sd[:, 0:2049].indirect(T.lfd[:, 8 * nv * h:8 * nv * h + 8 * nv]), T.xw[:, 1 + a.start:1 + a.stop], A.is_le),
-              [("sd", 0, 2049), "lfd", ("xw", 1, 1025)], [("cmp", a.start, a.stop)])
-            if h == 1 and t > 0:
-                p([f for c in (0, 1) for f in (mm(T.pA[:, 48 + 8 * c:56 + 8 * c], T.one[0:1, 0:128], T.c8b[0:1, 0:8], True, False),
-                                               mm(T.pA[:, 48 + 8 * c:56 + 8 * c], T.sgn[:, 128 * c:128 * c + 128], T.gib[:, 8:16], False, True))], [("sgn", 0, 512), "gib", "one", "c8b"], ["pA"])
-            p([mm(T.pA[:, 8 * c:8 * c + 8], T.cmp[:, 128 * c:128 * c + 128], T.gib[:, 0:8]) for c in range(nv * h, nv * h + nv)], [("cmp", a.start, a.stop), "gib"], ["pA"])
+            c0, c1 = onV[h]
+            a = slice(128 * c0, 128 * c1)
+            v(tt(T.cmp[:, a], DAYS.indirect(T.lfd[:, 8 * c0:8 * c1]), T.xw[:, 1 + a.start:1 + a.stop], A.is_le), ["sd", "lfd", ("xw", 1, 1025)], [("cmp", a.start, a.stop)])
+            for d0, d1, b in onS[h:h + 1]:
+                s(act(T.sgn[:, 128 * d0:128 * d1], T[b][:, 0:128 * (d1 - d0)], AF.Sign, TINY), [b], [("sgn", 128 * d0, 128 * d1)])
+            p([mm(T.pA[:, 8 * c:8 * c + 8], T.cmp[:, 128 * c:128 * c + 128], T.gib[:, 0:8]) for c in range(c0, c1)], [("cmp", a.start, a.stop), "gib"], ["pA"])
+            for d0, d1, b in onS[h:h + 1]:
+                p([f for c in range(d0, d1) for f in (mm(T.pA[:, 8 * c:8 * c + 8], T.one[0:1, 0:128], T.c8b[0:1, 0:8], True, False),
+                                                      mm(T.pA[:, 8 * c:8 * c + 8], T.sgn[:, 128 * c:128 * c + 128], T.gib[:, 8:16], False, True))], [("sgn", 128 * d0, 128 * d1), "gib", "one", "c8b"], ["pA"])
+        if 0 < t < RO - 1:
+            ghosts(0)
+        cands(0)
         if t == 0:
             v(ts(T.v1c[:, 8:16], T.v1c[:, 0:8], 0.5, A.mult), ["v1c"], ["v1h"])
         v(ts(T.bz[:, 56:120], T.pA[:, 0:64], 4.5, A.is_lt), ["pA"], [("bz", 56, 120)])
         p([mm(T.pB[:, 0:64], T.upr[:, 0:128], T.bz[:, 56:120], True, False)] + [mm(T.pB[:, 0:64], ONE, T.bz[:, 56 - 8 * q:120 - 8 * q], False, q == 7) for q in range(1, 8)],
           ["upr", "one", "bz"], ["pB"])
+        if not last:
+            ghosts(1, "V")
         v(tc(T.rkI[:], T.pB[:, 0:64]), ["pB"], ["rkI"])
-        s([act(T.th[:, c::17], T.pB[:, 0:64], AF.Sign, 16.0 * c - 4096.5, -1.0) for c in range(17)], ["pB"], ["th"])
+        s([act(T.th[:, c::17], T.pB[:, 0:64], AF.Sign, 16.0 * c - 4096.5, -1.0) for c in range(1, 17)], ["pB", "th0"], ["th"])
+        cands(1)
         v(ts(T.loI[:], T.rkI[:], 15, A.bitwise_and), ["rkI"], ["loI"])
         v([ts(T.lo2[:, k::2], T.loI[:], -8.0 * k, A.add) for k in (0, 1)], ["loI"], ["lo2"])
         v([ts(T.oa[:, i::8], T.lo2[:], float(i), A.is_equal) for i in range(8)], ["lo2"], ["oa"])
@@ -556,121 +599,152 @@ def rank_program(g, core, T, topo):
             a = slice(128 * c, 128 * c + 128)
             v(ts(T.oa[:, a], T.oa[:, a], T.v1c[:, 8 + c:9 + c], A.mult), [("oa", a.start, a.stop), "v1h"], [("oa", a.start, a.stop)])
             p(mm(T.pC[:, 0:136], T.oa[:, a], T.th[:, 136 * c:136 * c + 136], c == 0, c == 7), [("oa", a.start, a.stop), "th"], ["pC"])
-        cands(1)
         v(tc(T.win[:, 0:136], T.pC[:, 0:136]), ["pC"], ["win"])
-        v(tc(T.g16[:], T.win[:, 0:136].indirect(T.dgt[:, 0:1])), ["win", "dgl"], ["g16"])
-        v(tt(T.lvf[:], T.win[:, 0:136].indirect(T.dgt[:, 2:3]), T.g16[:], A.subtract), ["win", "dgl", "g16"], ["lvf"])
-        v(tc(T.lv[:], T.lvf[:]), ["lvf"], ["lv"])
+        v(tt(T.dif[:, 0:135], T.pC[:, 1:136], T.win[:, 0:135], A.subtract, 1), ["pC", "win"], ["dif"])
+        v(tc(T.lv[:], T.dif[:, 0:135].indirect(T.dgt[:, 0:1])), ["dif", "dgl"], ["lv"])
+        v(tc(T.lvf[:], T.dif[:, 0:135].indirect(T.dgt[:, 0:1])), ["dif", "dgl"], ["lvf"])
         for bank in KB:
             p(mm(T[bank][:, 0:128], T.one[0:1, 0:128], T.ck[:], True, False), ["one", "ck"], [bank])
-        s(act(T.xg[:, 1:257], T.xw[:, 0:1025].indirect(T.lv[:])), ["xw", "lv"], [("xg", 1, 257)])
+        s(act(T.xg[:, x0 + 1:x0 + 257], T.xw[:, 0:1025].indirect(T.lv[:])), ["xw", "lv"], [("xg", x0 + 1, x0 + 257)])
         v(tc(T.cg[:], T.cv[:, 0:1025].indirect(T.lv[:])), ["cv", "lv"], ["cg"])
-        copies("S", T.xg, "xg", 1, 0, 128, range(0, XO))
-        copies("V", T.xg, "xg", 1, 0, 128, range(XO, 16))
-        copies("G", T.xg, "xg", 129, 2048, 32, range(0, 16))
-        parts = [signed(T.xg, "xg", 161 + 32 * k, 160 + 32 * k, 512 * k, b) for k, b in enumerate(("pE", "pF", "pH"))]
+        copies("S", T.xg, "xg", x0 + 1, 0, 128, range(0, XO))
+        copies("V", T.xg, "xg", x0 + 1, 0, 128, range(XO, 16))
+        send(to, T.xal[:, x0:x0 + 257], T.xg[:, x0:x0 + 257], [("xg", x0, x0 + 257)], "gx%d" % t)
+        ne = len(topo.engines(cores[fro], core))
+        landed(("xal", x0, x0 + 272), "gx%d" % t, ne)
+        copies("G", T.xg, "xg", x0 + 129, 2048, 32, range(0, 16))
+        p(mm(T.pG[:, 0:128], T.xg[:, x0 + 129:x0 + 257], T.idb[:]), [("xg", x0 + 1, x0 + 257), "idb"], ["pG"])
+        s(act(T.xt[:], T.pG[:, 0:128]), ["pG"], ["xt"])
+        parts = [signed(160 + 32 * k, 512 * k, b) for k, b in enumerate(("pE", "pF", "pH"))]
         parts[0][0]()
         s(act(T.cgf[:], T.cv[:, 0:1025].indirect(T.lv[:])), ["cv", "lv"], ["cgf"])
-        parts[1][0]()
-        parts[2][0]()
         for q in (1, 0):
             p(mm(T[KB[q]][:, 0:128], T.cgf[:, 128 * q:128 * q + 128], T.idF[:], False, False), ["cgf", "idF"], [KB[q] + "+"])
-        for k, (c, n) in enumerate(((0, 96), (96, 32), (128, 32))):
-            compare(c, n)
-            parts[k][1]()
-        p(mm(T.pD[:, 0:128], T.nil[:], T.c8[:], False, True), ["nil", "c8"], ["pD"])
-        s(act(T.db[:], T.t8[:, 0:1025].indirect(T.lv[:])), [("t8", 0, 1025), "lv"], ["db"])
+        parts[1][0]()
+        parts[0][1]()
+        compare(0, 96)
+        parts[2][0]()
+        parts[1][1]()
+        compare(96, 32)
+        parts[2][1]()
+        compare(128, 32)
+        bound("pD", t, False, True)
+        bound("pC", t)
         p(mm(T.pC[:, 0:128], T.up64[:], T.c8[:], False, True), ["up64", "c8"], ["pC"])
-        p([mm(T.pB[:, 32 + 8 * q:40 + 8 * q], T.db[:, 128 * q:128 * q + 128], T.dec[:, 8:16]) for q in (0, 1)], ["db", ("dec", 8, 16)], ["pB"])
+
+        def dates256():
+            s(act(T.db[:], T.t8[:, 0:1025].indirect(T.lv[:])), [("t8", 0, 1025), "lv"], ["db", "~db"])
+            p([mm(T.pE[:, 8 * q:8 + 8 * q], T.db[:, 128 * q:128 * q + 128], T.dec[:, 8:16]) for q in (0, 1)], ["db", ("dec", 8, 16)], ["pE"])
+            v(tc(T.dI[:, 0:16], T.pE[:, 0:16]), ["pE"], [("dI", 0, 16)])
+            v(ts(T.dI[:, 16:32], T.dI[:, 0:16], 2047, A.bitwise_and), [("dI", 0, 16)], [("dI", 16, 32)])
+            v(ts(T.dI[:, 0:16], T.dI[:, 16:32], 1.0, A.add), [("dI", 16, 32)], [("dI", 0, 16)])
+
+        beside(dates256)
+        if not last:
+            ghosts(2)
         if t == 0:
-            ghosts(3)
-            ghosts(1)
-            s([act(T.jF[:], T.jb[:])] + [act(T.smk[:, EO[b]:EO[b] + 16], T.tri[:], AF.Copy, 0.0, FAR) for b in range(8)], ["jb", "tri", "smk0"], ["jF", "smk"])
-            fill3()
-        v(tc(T.dI[:, 0:16], T.pB[:, 32:48]), ["pB"], [("dI", 0, 16)])
+            beside(s, [act(T.jF[:], T.jb[:])] + [act(T.smk[:, EO[b]:EO[b] + 16], T.tri[:], AF.Copy, 0.0, FAR) for b in range(8)], ["jb", "tri", "smk0"], ["jF", "smk"])
+            beside(v, ts(TC[11], P15, 16.0, A.mult), ["pp"], [("tc", 11, 12)])
+            beside(s, [act(T.smk[:, 15:16], lm(0), AF.Identity, TC[11], FAR)] + [act(T.smk[:, EO[b + 1] - 1:EO[b + 1]], T.du[:, b:b + 1], AF.Copy, 0.0, 16.0) for b in range(1, 8)],
+                   ["lmc", "du", ("tc", 11, 12)], ["smk"])
+            beside(fill3)
         keys(0)
-        v(ts(T.dI[:, 16:32], T.dI[:, 0:16], 2047, A.bitwise_and), [("dI", 0, 16)], [("dI", 16, 32)])
         keys(1)
-        v(ts(T.dI[:, 0:16], T.dI[:, 16:32], 1.0, A.add), [("dI", 16, 32)], [("dI", 0, 16)])
-        v([ts(T.rz[:, 8:24], T.kx[:, 15:256:16], T.thr[:, t % 2:t % 2 + 1], A.is_lt), excess(16, t)], ["kx", ("thr", t % 2, t % 2 + 1)], [("ki", 0, 16), ("rz", 8, 24)])
-        p([mm(T.pB[:, 0:16], T.upr[:, 0:128], T.rz[:, 8:24], True, False), mm(T.pB[:, 0:16], ONE, T.rz[:, 0:16], False, True)], ["upr", "one", "rz"], ["pB"])
-        chosen(16)
+        v(ts(T.rz[:, 8:24], T.kx[:, 15:256:16], 0.5, A.is_lt), ["kx"], [("rz", 8, 24)])
+        v(chosen(16), ["kx"], [("ki", 16, 32)])
+        p(mm(T.pB[:, 0:16], T.one[0:1, 0:128], T.c75[0:1, :], True, False), ["one", "c75"], ["pB"])
+        p([mm(T.pB[:, 0:16], T.upr[:, 0:128], T.rz[:, 8:24], False, False), mm(T.pB[:, 0:16], ONE, T.rz[:, 0:16], False, True)], ["upr", "one", "rz"], ["pB"])
         s(act(T.xf[:], T.ki[:, 16:32].indirect(T.ex[:])), [("ki", 16, 32), "ex"], ["xf"])
-        v(tc(T.rkI[:, 0:16], T.pB[:, 0:16]), ["pB"], ["rkI"])
         v(tt(T.xe[:], T.ki[:, 16:32].indirect(T.ex[:]), T.mkg[:, 128:384], A.mult), [("ki", 16, 32), "ex", "mkg"], ["xe"])
+        v(ts(T.hl[:, 0:16], T.pB[:, 0:16], STEP16, A.add, STEP16, A.subtract), ["pB"], [("hl", 0, 16)])
         p([f for q in (0, 1) for f in (mm(T.pA[:, 24 * q:24 * q + 24], T.idb[:], T.duw[:, 24 * q:24 * q + 24], True, False),
                                        mm(T.pA[:, 24 * q:24 * q + 24], T.xe[:, 128 * q:128 * q + 128], T.gin[:], False, True))], ["xe", "gin", "idb", "duw"], ["pA"])
         p([mm(T.pH[:, 128 * q:128 * q + 128], T.xf[:, 128 * q:128 * q + 128], T.jF[:]) for q in (1, 0)], ["xf", "jF"], ["pH"])
-        v([ts(T.loI[:, 0:16], T.rkI[:, 0:16], 15, A.bitwise_and), ts(T.hiI[:, 0:16], T.rkI[:, 0:16], 4, A.arith_shift_right)], ["rkI"], ["loI", "hiI"])
-        v(tt(T.ob[:], T.hiI[:, 0:16].indirect(T.ex8[:]), T.ct8[:], A.is_equal), ["hiI", "ex8", "ct8"], ["ob"])
+        v(tt(T.hl[:, 16:32], T.pB[:, 0:16], T.hl[:, 0:16], A.subtract), ["pB", ("hl", 0, 16)], [("hl", 16, 32)])
+        v(tt(T.ob[:], T.hl[:, 0:16].indirect(T.ex8[:]), T.ct8[:], A.is_equal), [("hl", 0, 16), "ex8", "ct8"], ["ob"])
         s([act(T.obj[:, 64 * q:64 * q + 64], T.ob[:, 64 * q:64 * q + 64], AF.Copy, 0.0, T.v1c[:, q:q + 1]) for q in (0, 1)], ["ob", "v1c"], ["obj"])
         v([ts(T.u16s[:, 32:48], T.pA[:, 0:48:3], -1.0, A.mult, -1.0, A.add), tc(T.sm[:, 48:64], T.pA[:, 1:48:3])], ["pA"], [("u16s", 32, 48), ("sm", 48, 64)])
         s(act(T.wv[:], T.tab[:].indirect(T.u16s[:, 32:48]), AF.Identity, RB, MB), ["tab", ("u16s", 32, 48), ("col", 1, 5)], ["wv"])
         eqdays(1, "S", "pH", range(8))
-        v(tt(T.oa[:, 0:256], T.loI[:, 0:16].indirect(T.ex[:]), T.lane[:], A.is_equal), ["loI", "ex", "lane"], [("oa", 0, 256)])
+        beside(s, act(T.sm[:, 0:16], T.pA[:, 0:48:3], AF.Copy, float(D0), -1.0), ["pA"], [("sm", 0, 16)])
+        v(tt(T.oa[:, 0:256], T.hl[:, 16:32].indirect(T.ex[:]), T.lane[:], A.is_equal), [("hl", 16, 32), "ex", "lane"], [("oa", 0, 256)])
         p([mm(T.pC[:, 0:64], T.oa[:, 128 * q:128 * q + 128], T.obj[:, 64 * q:64 * q + 64], q == 0, q == 1) for q in (0, 1)], [("oa", 0, 256), "obj"], ["pC"])
         v(tt(T.oa[:, 256:384], T.dI[:, 0:16].indirect(T.ex8[:]), T.ob[:], A.mult), [("dI", 0, 16), "ex8", "ob"], [("oa", 256, 384)])
         p([mm(T.pC[:, 64:128], T.oa[:, 128 * q:128 * q + 128], T.oa[:, 256 + 64 * q:320 + 64 * q], q == 0, q == 1) for q in (0, 1)], [("oa", 0, 384)], ["pC"])
+
+        def parity():
+            p(mm(T.pG[:, 0:16], ONE, T.rz[:, 8:24]), ["one", "rz"], ["pG"])
+            s((lambda: S.activation(T.sm[:, 64:80], T.pG[:, 0:16], AF.Copy, accum_out=T.sm[:, 80:81]), lambda: 84, 0), ["pG"], [("sm", 64, 81)])
+            v(tc(T.smi[:, 16:17], T.sm[:, 80:81]), [("sm", 64, 81)], [("smi", 16, 17)])
+            v(ts(T.smi[:, 17:18], T.smi[:, 16:17], 1, A.bitwise_and), [("smi", 16, 17)], [("smi", 17, 18)])
+            v(ts(T.sm[:, 81:82], T.smi[:, 17:18], -BIG, A.mult, -9.0 * BIG, A.add), [("smi", 17, 18)], [("sm", 81, 82)])
+            s(act(T.thr[:, 128 * a1:128 * a1 + 128], T.one[0:1, 0:128], AF.Copy, 0.0, T.sm[0:1, 81:82]), ["one", ("sm", 81, 82)], [("thr", 128 * a1, 128 * a1 + 128)])
+
         if not last:
-            p([mm(T.pG[:, 64:65], ONE, T.rz[:, 8 + c:9 + c], c == 0, c == 15) for c in range(16)], ["one", "rz"], ["pG"])
+            beside(parity)
         v(tt(T.sm[:, 32:48], T.pA[:, 2:48:3], T.lvf[:], A.max), ["pA", "lvf"], [("sm", 32, 48)])
         v(tc(T.wg[:], T.pC[:, 0:128]), ["pC"], ["wg"])
         v(tc(T.u16s[:, 0:16], T.sm[:, 32:48]), [("sm", 32, 48)], [("u16s", 0, 16)])
-        v(tc(T.gds[:, gla[0]:gda[1]], T.wg[:].indirect(T.dgt[:, 4:5])), ["wg", "dg8"], [("gds", gla[0], gda[1])])
-        s(act(T.gxs[:, gxa[0]:gxa[1]], T.xg[:, 0:257].indirect(T.gds[:, gla[0]:gla[1]])), ["xg", ("gds",) + gla], [("gxs",) + gxa])
+        v(tc(T.gds[:, gda[0]:gda[1]], T.wg[:].indirect(T.dgt[:, 4:5])), ["wg", "dg8"], [("gds",) + gda])
         send(to, T.gdl[:, gda[0]:gda[1]], T.gds[:, gda[0]:gda[1]], [("gds",) + gda], "gd%d" % t)
-        send(to, T.gxl[:, gxa[0]:gxa[1]], T.gxs[:, gxa[0]:gxa[1]], [("gxs",) + gxa], "gx%d" % t)
-        ne = len(topo.engines(cores[fro], core))
-        landed(("gxl",) + gxa, "gx%d" % t, ne)
         landed(("gdl",) + gda, "gd%d" % t, ne)
         eqdays(0, "S", "pH", range(8))
-        v(scatter(T.wb[:, W1 - 1:DUMP + 256].indirect(T.u16s[:, 0:16]), T.wv[:]), ["wv", ("u16s", 0, 16)], [("wb", W1 - 1, DUMP + 256)])
-        if last:
-            for h in (0, 1):
-                p(mm(T[BK[h]][0:16, :], T.dec[:], T.wb[:, W1 + 512 * h:W1 + 512 * h + 512]), ["dec", ("wb", W1, DUMP)], [BK[h]])
-                s(act(T.yb[0:16, 512 * h:512 * h + 512], T[BK[h]][0:16, :], AF.Identity, T.col[0:16, 7:8]), [BK[h], ("col", 7, 8)], [("yb", 512 * h, 512 * h + 512)])
-            copy("Y", T.yan[:], T.yb[0:8, :], ["yb"], [])
-            copy("Y", T.yof[:], T.yb[8:16, :], ["yb"], [])
-        else:
+
+        def moves():
+            v(scatter(T.wb[:, W1 - 1:DUMP + 256].indirect(T.u16s[:, 0:16]), T.wv[:]), ["wv", ("u16s", 0, 16), "~cmp"], [("wb", W1 - 1, DUMP + 256)])
+            if last:
+                for h in (0, 1):
+                    p(mm(T[BK[h]][0:16, :], T.dec[:], T.wb[:, W1 + 512 * h:W1 + 512 * h + 512]), ["dec", ("wb", W1, DUMP)], [BK[h]])
+                    s(act(T.yb[0:16, 512 * h:512 * h + 512], T[BK[h]][0:16, :], AF.Identity, T.col[0:16, 7:8]), [BK[h], ("col", 7, 8)], [("yb", 512 * h, 512 * h + 512)])
+                copy("S", T.yan[:], T.yb[0:8, :], ["yb"], [], 0)
+                copy("S", T.yof[:], T.yb[8:16, :], ["yb"], [], 0)
+
+        if not last:
+            moves()
             pointers(a1, 0, T.wb, "wb", W1)
             own(a1, 0)
         scan(1)
-        if not last:
-            v(tc(T.smi[:, 16:17], T.pG[:, 64:65]), ["pG"], [("smi", 16, 17)])
         scan(0)
-        hh = [] if last else [lambda: pointers2(a1, 0), later("V", ts(T.smi[:, 17:18], T.smi[:, 16:17], 1, A.bitwise_and), [("smi", 16, 17)], [("smi", 17, 18)])]
-        weave(dayoffsets(16), hh)
+        weave(dayoffsets(16), [] if last else [lambda: pointers2(a1, 0)])
         if not last:
             for h in (0, 1):
                 jump(a1, 0, h)
                 join(0, h)
             after(a1, 0)
-        v(scatter(T.sd[:, 0:2320].indirect(T.u16s[:, 24:32]), T.xg[:, 129:257]), [("xg", 1, 257), ("u16s", 16, 32)], ["sd"])
-        if not last:
-            v(ts(T.thr[:, a1:a1 + 1], T.smi[:, 17:18], BIG, A.mult, 9.0 * BIG, A.add), [("smi", 17, 18)], [("thr", a1, a1 + 1)])
-        v(scatter(T.sd[:, 0:2320].indirect(T.u16s[:, 16:24]), T.xg[:, 1:129]), [("xg", 1, 257), ("u16s", 16, 32)], ["sd"])
-        gl = T.gdl[:, gda[0]:gda[1]]
+        v(scatter(T.sd[:, 0:D0 + 2049].indirect(T.u16s[:, 24:32]), T.xg[:, x0 + 129:x0 + 257]), [("xg", x0, x0 + 257), ("u16s", 16, 32)], ["sd"])
+        v(scatter(T.sd[:, 0:D0 + 2049].indirect(T.u16s[:, 16:24]), T.xg[:, x0 + 1:x0 + 129]), [("xg", x0, x0 + 257), ("u16s", 16, 32)], ["sd"])
+        gl = T.gdl[:, gda[0] + 8:gda[1]]
+        op(GX, (act if GX == "S" else tc)(T.gx[:], T.xal[:, x0:x0 + 257].indirect(T.gdl[:, gda[0]:gda[0] + 8])), [("xal", x0, x0 + 272), ("gdl",) + gda], ["gx"])
         v(tc(T.cg[:, 0:128], T.cw[:, 0:2049].indirect(gl)), ["cw", ("gdl",) + gda], ["cg"])
 
         def guestdays():
             s(act(T.cgf[:, 0:128], T.cw[:, 0:2049].indirect(gl)), ["cw", ("gdl",) + gda], ["cgf"])
-            p(mm(T.pD[:, 0:128], T.cgf[:, 0:128], T.idF[:], True, False), ["cgf", "idF"], ["pD"])
+            bound("pD", t, True)
+            p(mm(T.pD[:, 0:128], T.cgf[:, 0:128], T.idF[:], False, False), ["cgf", "idF"], ["pD+"])
 
         if last:
-            copies("S", T.gxl, "gxl", gxa[0], 0, 64, range(0, 8))
-            copies("V", T.gxl, "gxl", gxa[0], 0, 64, range(8, 16))
-            copies("S", T.gxl, "gxl", gxa[0] + 64, 1024, 64, range(0, 16))
+            copies("G", T.gx, "gx", 0, 0, 64, range(0, 3))
+            copies("V", T.gx, "gx", 0, 0, 64, range(3, 16))
             guestdays()
-            for c, n in ((0, 64), (64, 32), (96, 32)):
-                compare(c, n)
+            p(mm(T.pB[:, 0:128], T.gx[:], T.idb[:]), ["gx", "idb"], ["pB"])
+            s(act(T.xt[:], T.pB[:, 0:128]), ["pB"], ["xt"])
+            p(mm(T.pD[64:128, 0:128], T.one[0:1, 0:64], T.c8[:], False, False), ["one", "c8"], ["pD+"])
+            parts = [signed(64, 0, "pH"), signed(96, 512, "pE")]
+            parts[0][0]()
+            parts[1][0]()
+            compare(0, 64, "~cmp")
+            parts[0][1]()
+            parts[1][1]()
+            moves()
         else:
-            copies("S", T.gxl, "gxl", gxa[0], 0, 128, range(0, XS))
-            copies("V", T.gxl, "gxl", gxa[0], 0, 128, range(XS, 16))
+            copies("G", T.gx, "gx", 0, 0, 128, range(0, 2))
+            copies("S", T.gx, "gx", 0, 0, 128, range(2, 2 + XS))
+            copies("V", T.gx, "gx", 0, 0, 128, range(2 + XS, 16))
             sums(a1, 0, 0)
             sums(a1, 0, 1)
+            guestdays()
             pointers2(a1, 1)
             own(a1, 1)
-            guestdays()
             compare(0, 64)
             jump(a1, 1, 0)
             join(1, 0)
@@ -690,21 +764,24 @@ def rank_program(g, core, T, topo):
             jump(a1, 2, 0)
             join(2, 0)
             jump(a1, 2, 1)
-        v(excess(8, t), ["kx", ("thr", t % 2, t % 2 + 1)], [("ki", 0, 16)])
-        chosen(8)
+        v(chosen(8), ["kx"], [("ki", 16, 32)])
         v(tt(T.xe[:], T.ki[:, 16:24].indirect(T.exg[:]), T.mkg[:, 0:256], A.mult), [("ki", 16, 32), "exg", "mkg"], ["xe"])
-        p([mm(T.pA[:, 0:24], T.xe[:, 128:256], T.gin[:]), mm(T.pH[:, 0:128], T.xe[:, 0:128], T.jb[:]), mm(T.pB[:, 0:128], T.xe[:, 0:128], T.jb[:])], ["xe", "gin", "jb"], ["pA", "pH", "pB"])
-        v(tc(T.sm[:, 48:56], T.pA[:, 1:24:3]), ["pA"], [("sm", 48, 64)])
-        eqdays(0, "S", "pB", (6, 4, 2))
+        p(mm(T.pA[:, 0:24], T.xe[:, 128:256], T.gin[:]), ["xe", "gin"], ["pA"])
+        for b in ("pH", "pB")[:1 + last]:
+            p(mm(T[b][:, 0:128], T.xe[:, 0:128], T.jb[:]), ["xe", "jb"], [b])
+        if last:
+            v(tc(T.sm[:, 48:56], T.pA[:, 1:24:3]), ["pA"], [("sm", 48, 64)])
+            eqdays(0, "S", "pB", (6, 4, 2))
+        v(ts(T.sm[:, 0:8], T.pA[:, 0:24:3], -1.0, A.mult, float(D0), A.add), ["pA"], [("sm", 0, 16)])
         if not last:
             after(a1, 2)
             join(2, 1)
             sums(a1, 2, 0)
             sums(a1, 2, 1)
-        eqdays(0, "V", "pH", (7, 5, 3, 1, 0))
+        eqdays(0, "V", "pH", (7, 5, 3, 1, 0) if last else range(8))
         weave([] if last else datelist(), [lambda: scan(0)] + dayoffsets(8))
-        v(scatter(T.sd[:, 0:2320].indirect(T.u16s[:, 16:24]), T.gxl[:, gxa[0]:gxa[1]]), [("gxl",) + gxa, ("u16s", 16, 32)], ["sd"])
-    copy("Y", T.ys[:], T.sd[:, 1:2049], ["sd"], [])
-    for i in order(steps):
+        v(scatter(T.sd[:, 0:D0 + 2049].indirect(T.u16s[:, 16:24]), T.gx[:]), ["gx", ("u16s", 16, 32)], ["sd"])
+    copy("Y", T.ys[:], T.sd[:, D0 + 1:D0 + 2049], ["sd"], [])
+    for i in order(steps, aside):
         steps[i][1]()
     finish([("ls", sent[0])])

from concourse.mybir import AluOpType as A, ActivationFunctionType as AF

BIG = 65536.0
LOW = -1073741824.0
TINY = 2.0 ** -110
FAR = 4096.0
STEP16 = 1.5 * 2 ** 27
RO = 4
D0 = 2048
F, B, H, I, U = "float32", "bfloat16", "float16", "int32", "uint16"
W3A, W2A, GA, W1, DUMP, GB, W2B, W3B, WEND = 0, 1024, 2048, 2833, 3857, 4128, 4912, 5936, 6960
WIN = (((GA, DUMP, W1), (W2A, GA + 769, W2A), (W3A, GA + 769, W3A)), ((W1 - 1, GB + 769, W1), (GB, W3B, W2B), (GB, WEND, W3B)))
GH = (GA, GB)
EW = [16 * (b + 1) for b in range(8)]
EO = [8 * b * (b + 1) for b in range(9)]
SB = {
    "anI": (64, I), "ofI": (112, I), "snI": (48, I), "wkb": (2048, B), "xw": (1040, B), "sd": (D0 + 2064, B),
    "pI": (3, I), "pp": (3, F), "n16": (16, I), "n144": (144, B), "lmc": (16, F), "pw": (16, F), "cc": (32, F), "col": (24, F), "hi16": (16, F), "tc": (16, F),
    "tab": (2048, B), "idb": (128, B), "idF": (128, F), "jF": (128, F), "jb": (128, B), "upr": (256, B), "amb": (128, B), "nid": (128, B),
    "one": (128, B), "seven": (128, B), "m1k": (128, B), "gin": (24, B), "gib": (16, B), "gik": (16, B), "zp": (864, H), "zd": (144, H), "dec": (16, B),
    "mkg": (384, B), "lane": (256, B), "segm": (128, B), "ct8": (128, B), "ex": (16, U), "exg": (16, U), "ex8": (8, U), "dgt": (8, U), "v1c": (16, F),
    "smk": (576, B), "tri": (16, F), "du": (16, F), "duw": (48, H), "anl": (64, U), "ofl": (112, U), "an1": (128, F),
    "wb": (WEND, B), "g0": (1024, B), "g1": (1024, B), "t8": (1040, B), "l0": (64, U), "l1": (64, U), "l2": (64, U), "sl": (48, U), "cw": (2056, F), "sg": (2048, B),
    "ldI": (128, I), "lfd": (64, U), "cv": (1032, F), "cmp": (3072, B), "xr": (3072, B), "sgb": (1536, B), "sgn": (1536, B), "bz": (120, B), "rz": (24, B), "rkI": (64, I), "loI": (64, I), "hl": (32, F), "c75": (16, B), "lo2": (128, B), "obj": (128, B), "c8b": (8, B),
    "oa": (1024, H), "ob": (128, B), "th": (1088, B), "win": (144, F), "wg": (128, F), "dif": (144, F), "lv": (16, U), "lvf": (16, F),
    "xg": (1088, B), "cg": (256, U), "cgf": (256, F), "db": (256, B), "dI": (32, I), "kx": (256, I), "ki": (32, I), "sm": (96, F), "smi": (32, I), "u16s": (64, U),
    "xe": (256, H), "xf": (256, F), "wv": (256, B), "eq": (1152, B), "scn": (1152, B), "yb": (1024, F),
    "ghs": (2304, B), "xal": (1088, B), "gx": (128, B), "xt": (128, B), "rep": (512, B), "gds": (64, U), "gdl": (64, U),
}
SCRATCH = {k: ("sbuf", [128, n], d) for k, (n, d) in SB.items()}
SCRATCH.update({"ck": ("sbuf", [1, 128], B), "c8": ("sbuf", [1, 128], B), "up64": ("sbuf", [1, 128], B), "thr": ("sbuf", [1, 256], B), "n256": ("sbuf", [1, 512], B)})
LISTS = [k for k, (n, d) in SB.items() if d == U] + ["dgl", "dg8", "pick"]
GATHER, SCATTER, PE, WAKE, LOAD, FLIGHT, PASSES = 1.75, 4.2, 0.55, 100, 2500, 1800, 4
PS = ("pA", "pB", "pC", "pD", "pE", "pF", "pG", "pH")
SCRATCH.update({k: ("psum", [128, 512], F) for k in PS})
SEMAPHORES = ["qV", "qS", "qP", "qG", "ls"] + ["d%d" % i for i in range(11)] + ["gh%d" % t for t in range(3)] + ["gx%d" % t for t in range(RO)] + ["gd%d" % t for t in range(RO)]


def layer(g, T):
    eng = {"V": g.vector, "S": g.scalar, "P": g.tensor, "G": g, "Y": g.sync}
    cnt = {"V": 0, "S": 0, "P": 0, "G": 0}
    seen = {q: {} for q in eng}
    hist = {}
    dma = [0]

    def reg(r):
        return (r.rstrip("+"), 0, 1 << 20) if isinstance(r, str) else r

    def prepare(q, reads, writes):
        best = {}
        for rs, w in ((reads, False), (writes, True)):
            for r in rs:
                name, lo, hi = reg(r)
                for e in hist.get(name, ()):
                    other = e[3] != q
                    bank = name in PS and other
                    if not (lo < e[1] and e[0] < hi) and not bank:
                        continue
                    if not (w or e[2] or bank) or (q == "P" and not other and name in PS):
                        continue
                    if seen[q].get(e[4], 0) < e[5] and (e[4] not in best or best[e[4]][5] < e[5]):
                        best[e[4]] = e
        for s in best:
            e = best[s]
            if not any(o != s and best[o][6].get(s, 0) >= e[5] for o in best):
                eng[q].wait_ge(T.sem[s], e[5])
        for e in best.values():
            for s, n in list(e[6].items()) + [(e[4], e[5])]:
                if seen[q].get(s, 0) < n:
                    seen[q][s] = n

    def record(q, sem, count, reads, writes):
        clock = dict(seen[q[0]])
        for rs, w in ((reads, False), (writes, True)):
            for r in rs:
                name, lo, hi = reg(r)
                h = hist.setdefault(name, [])
                h[:] = [e for e in h if not (lo <= e[0] and e[1] <= hi and (w or (e[3] == q and not e[2])))]
                h.append((lo, hi, w, q, sem, count, clock))

    def op(q, fns, reads, writes):
        prepare(q, reads, writes)
        for f in fns if isinstance(fns, list) else [fns]:
            f().then_inc(T.sem["q" + q], 1)
            cnt[q] += 1
        record(q, "q" + q, cnt[q], reads, writes)

    def copy(q, out, in_, reads, writes):
        prepare(q, reads, writes)
        sem = "d%d" % dma[0]
        dma[0] += 1
        eng[q].dma_start(out, in_).then_inc(T.sem[sem], 16)
        record(q + "*", sem, 16, reads, writes)

    def landed(region, sem, count):
        hist.setdefault(region[0], []).append((region[1], region[2], True, "net", sem, count, {}))

    def finish(extra):
        for q in cnt:
            if cnt[q]:
                g.wait_ge(T.sem["q" + q], cnt[q])
        for s, n in extra:
            g.wait_ge(T.sem[s], n)
        for i in range(dma[0]):
            g.wait_ge(T.sem["d%d" % i], 16)

    return op, copy, landed, prepare, finish


def order(steps, aside):
    n = len(steps)
    pre = [set() for _ in steps]
    hist = {}
    for i, (q, _, reads, writes, _, _) in enumerate(steps):
        for rs, w in ((reads, False), (writes, True)):
            for r in rs:
                name, lo, hi = (r, 0, 1 << 20) if isinstance(r, str) else r
                adds = name[-1] == "+"
                h = hist.setdefault(name.rstrip("+"), [])
                for a, b, w2, q2, j, adds2 in h:
                    if j != i and not (adds and adds2) and ((lo < b and a < hi and (w or w2)) or (name in PS and q != q2)):
                        pre[i].add(j)
                h[:] = [e for e in h if adds or not (w and lo <= e[0] and e[1] <= hi)]
                h.append((lo, hi, w, q, i, adds))
    post = [[] for _ in steps]
    for i in range(n):
        for j in pre[i]:
            post[j].append(i)

    def place(seq, before, back):
        end, taken = [0.0] * n, {}
        for i in seq:
            q, busy = steps[i][0], steps[i][4]
            t = steps[i][5] if back else 0.0
            for j in before[i]:
                t = max(t, end[j] + (0 if q == steps[j][0] in "PG" else steps[i if back else j][5] + WAKE))
            row = taken.setdefault(q, [])
            k = len(row)
            while k and row[k - 1][1] > t:
                k -= 1
            while k < len(row) and t + busy > row[k][0]:
                t = max(t, row[k][1])
                k += 1
            row.insert(k, (t, t + busy))
            end[i] = t + busy
        return end

    seq, best, done = [], None, set()

    def take(i):
        done.add(i)
        for j in sorted(pre[i] - done):
            if j not in done:
                take(j)
        seq.append(i)

    for i in [i for i in range(n) if i not in aside] + sorted(aside):
        if i not in done:
            take(i)
    for _ in range(PASSES):
        end = place(seq, pre, False)
        pos = {i: k for k, i in enumerate(seq)}
        seq = sorted(seq, key=lambda i: (end[i] - steps[i][4], pos[i]))
        last = max(end[i] + steps[i][5] for i in seq)
        if best is None or last < best[0]:
            best = (last, seq)
        seq = sorted(seq[::-1], key=lambda i: -end[i])
        end = place(seq, post, True)
        seq = sorted(seq[::-1], key=lambda i: -end[i])
    return best[1]


def weave(*chains):
    for i in range(max(len(c) for c in chains)):
        for c in chains:
            if i < len(c):
                c[i]()


def rank_program(g, core, T, topo):
    rank = T.rank_of(core)
    if rank is None:
        return
    cores = T.cores
    N = len(cores)
    issue, dma, arrive, prepare, finish = layer(g, T)
    V, S, P = g.vector, g.scalar, g.tensor
    sent = [0]
    steps, aside = [], set()

    def beside(f, *args):
        a = len(steps)
        f(*args)
        aside.update(range(a, len(steps)))

    def cols(a):
        return a.shape[1]

    def narrow(*aps):
        return 0.5 if all("16" in str(a.dtype) for a in aps) else 1.0

    def op(q, fns, reads, writes):
        fns = fns if isinstance(fns, list) else [fns]
        gather = any((r if isinstance(r, str) else r[0]) in LISTS for r in reads)
        busy = sum(f[2] if gather else f[1]() for f in fns)
        real = [[r for r in rs if r[0] != "~"] for rs in (reads, writes)]
        steps.append((q, lambda: issue(q, [f[0] for f in fns], *real), reads, writes, busy, 0))

    def copy(q, out, in_, reads, writes, lag=LOAD):
        steps.append((q, lambda: dma(q, out, in_, reads, writes), reads, writes, 50, lag))

    def landed(region, sem, count):
        steps.append(("N", lambda: arrive(region, sem, count), [sem], [region], 0, 0))

    def v(f, r, w):
        op("V", f, r, w)

    def s(f, r, w):
        op("S", f, r, w)

    def p(f, r, w):
        op("P", f, r, w)

    def tc(o, i):
        return lambda: V.tensor_copy(o, i), lambda: max(64, cols(o) * narrow(o, i)), 50 + GATHER * cols(o)

    def scatter(o, i):
        return lambda: V.tensor_copy(o, i), None, 50 + SCATTER * cols(i)

    def tt(o, a, b, f, cycles=2):
        return lambda: V.tensor_tensor(o, a, b, f), lambda: max(64, cycles * cols(o)), 50 + GATHER * cols(o)

    def ts(o, a, s1, f1, s2=None, f2=None):
        return (lambda: V.tensor_scalar(o, a, s1, None, f1) if f2 is None else V.tensor_scalar(o, a, s1, s2, f1, f2)), lambda: max(64, cols(o) * narrow(o, a)), 50 + GATHER * cols(o)

    def sweep(o, a, b, f1, f2):
        return lambda: V.tensor_tensor_scan(o, a, b, 0.0, f1, f2), lambda: max(64, cols(o) * narrow(o, a, b)), 0

    def ms(o, c):
        return lambda: V.memset(o, c), lambda: max(64, cols(o) * narrow(o)), 0

    def act(o, i, f=AF.Copy, bias=0.0, scale=1.0):
        return lambda: S.activation(o, i, f, bias=bias, scale=scale), lambda: max(64, cols(o)), 65 + GATHER * cols(o)

    def mm(o, l, r, st=True, sp=True):
        return lambda: P.matmul(o, l, r, st, sp), lambda: max(min(64, cols(l)), cols(r)) * PE * (1 if narrow(l) < 1 else 4), 0

    def later(q, f, r, w):
        return lambda: op(q, f, r, w)

    def lanes(a, b, spare=False):
        mine = topo.engines(cores[a], cores[b])
        shared = min((topo.engines(cores[a], c) for c in cores if c != cores[a]), key=len)
        return [e for e in mine if e not in shared] if spare and len(mine) > len(shared) else mine

    def send(dst, out, in_, reads, sem, spare=False):
        es = lanes(rank, dst, spare)

        def run():
            prepare("G", reads, [])
            rid, pid = topo.addr(cores[dst], core)
            g.remote_dma(out, in_, T.sem[sem], T.sem.ls, pid, rid, sum(1 << e for e in es))
            sent[0] += len(es)
        steps.append(("G", run, reads, [(sem + "s", dst, dst + 1)], 300 if any(x[0][0] == "D" for x in steps) else 2500, FLIGHT))
        steps.append(("D%d" % es[0], lambda: None, [(sem + "s", dst, dst + 1)], [(sem, dst, dst + 1)], 600 + 5 * cols(in_), 0))

    def iota(name, view, pat, base, ch, fl=True):
        f = (lambda: g.iota(view, pat, base, ch, allow_small_or_imprecise_dtypes=True)) if fl else (lambda: g.iota(view, pat, base, ch))
        op("G", (f, lambda: 130 + 2 * cols(view), 0), [], [name])

    def select(name, view, src, sname, pat, cmp, fill, base, ch):
        op("G", (lambda: g.affine_select(view, src, pat, cmp, fill, base, ch), lambda: 170 + 2 * cols(view), 0), [sname], [name])

    def keep(o, i):
        return lambda: g.affine_select(o, i, [[0, cols(o)]], A.is_ge, 0.0, 0, 0), lambda: 170 + 2 * cols(o), 0

    def col(i):
        return T.col[:, i:i + 1]

    def lm(i):
        return T.lmc[:, i:i + 1]

    v([ms(T.xw[:, 0:1], LOW), ms(T.sd[:, D0:D0 + 1], 0.0), ms(T.one[:], 1.0)], [], [("xw", 0, 16), ("sd", 0, 16), "one"])
    copy("Y", T.anI[:], T.an0[:], [], ["anI"])
    copy("Y", T.ofI[:], T.of0[:], [], ["ofI"])
    copy("S", T.wkb[:], T.wk[:], ["one"], ["wkb"], 4000)
    copy("Y", T.snI[:], T.snd[:], [], ["snI"])
    ONE = T.one[:, 0:128]
    iota("pI", T.pI[:, 0:1], [[0, 1]], 0, 1, False)
    iota("n16", T.n16[:], [[1, 16]], 0, 0, False)
    select("idb", T.idb[:], ONE, "one", [[-1, 128]], A.is_equal, 0.0, 0, 1)
    iota("n256", T.n256[:], [[0, 2], [1, 256]], 0, 0)
    iota("n144", T.n144[:], [[1, 144]], 0, 0)
    select("up0", T.upr[:, 128:256], ONE, "one", [[1, 128]], A.is_gt, 0.0, 0, -1)
    iota("v1c", T.v1c[:, 0:8], [[128, 8]], 1, 1)
    select("upr", T.upr[:, 0:128], T.upr[:, 128:256], "up0", [[-1, 128]], A.not_equal, -4096.0, 0, 1)
    iota("du", T.du[:], [[16, 16]], 0, 0)
    iota("lane", T.lane[:], [[0, 16], [1, 16]], 0, 0)
    for name, a, b, c in (("c8b", 0, 8, 8), ("bz", 0, 56, 0), ("t8", 0, 1, 0), ("cv", 0, 1, 1), ("cw", 0, 1, 1), ("thr", 0, 128, -9 * 65536), ("rz", 0, 8, 0), ("mkg", 0, 128, 1), ("c8", 0, 128, 8 * 65536)):
        iota((name, a, b), T[name][:, a:b], [[0, b - a]], c, 0)
    iota("rep", T.rep[:], [[-1, 32], [0, 16]], 0, 1)
    iota("th0", T.th[:, 0::17], [[0, 64]], -1, 0)
    iota("ck", T.ck[:], [[0, 8], [-4096, 16]], 61440, 0)
    select("up64", T.up64[:], T.one[0:1, 0:128], "one", [[1, 128]], A.is_ge, 0.0, -32, 0)
    select("segm", T.segm[:], ONE, "one", [[0, 8], [1, 16]], A.is_gt, 0.0, 0, 0)
    iota("ct8", T.ct8[:], [[0, 16], [16, 8]], -4096, 0)
    select("jb0", T.jb[:], ONE, "one", [[1, 128]], A.not_equal, -1.0, -127, 1)
    iota(("wb", GB + 769, W2B), T.wb[:, GB + 769:W2B], [[0, W2B - GB - 769]], 0, 0)
    select("jb", T.jb[:], T.jb[:], "jb0", [[1, 128]], A.is_equal, 0.0, -127, 1)
    iota(("wb", DUMP, GB), T.wb[:, DUMP:GB], [[0, GB - DUMP]], 0, 0)
    iota("smk0", T.smk[:], [[0, 576]], 0, 0)

    P15, P4, PC = T.pp[:, 0:1], T.pp[:, 1:2], T.pp[:, 2:3]
    G8, N16 = T.n16[:, 0:8], T.n16[:]
    ZC, MB, MP, BP, RB, WL, WD, DB = (col(i) for i in range(8))
    v([ts(T.pI[:, 1:2], T.pI[:, 0:1], 15, A.bitwise_and), ts(T.pI[:, 2:3], T.pI[:, 0:1], 4, A.arith_shift_right)], ["pI"], ["pI2"])
    v([ms(T.pw[:, 0:1], 1.0), ms(T.pw[:, 1:2], 2.0)], [], ["pwa"])
    v([tc(P15, T.pI[:, 1:2]), tc(P4, T.pI[:, 2:3]), tc(PC, T.pI[:, 0:1])], ["pI", "pI2"], ["pp"])
    copy("Y", T.sd[:, D0 + 1:D0 + 2049], T.s0[:], ["pp"], [("sd", 1, 2049)], 12000)
    copy("Y", T.xw[:, 1:1025], T.x[:], ["pp"], [("xw", 1, 1025)], 12000)
    v([ms(T.pw[:, b:b + 1], float(1 << b)) for b in range(2, 5)], [], ["pw"])
    v(ts(T.lmc[:], N16, P15, A.is_equal), ["n16", "pp"], ["lmc"])
    v([ms(T.tab[:, 0:1], 0.0), ms(T.hi16[:, 0:1], 0.0)], [], [("tab", 0, 1), ("hi16", 0, 1)])
    v([ts(T.cc[:, 16:21], T.pw[:, 0:5], lm(11), A.mult), ts(T.cc[:, 21:26], T.pw[:, 0:5], lm(12), A.mult), tc(T.cc[:, 26:27], lm(13))], ["pw", "pwa", "lmc"], [("cc", 16, 32)])
    v([ts(MB, P15, 11.0, A.is_lt), ts(T.gib[:, 0:8], G8, P4, A.is_equal)], ["pp", "n16"], [("col", 1, 2), ("gib", 0, 8)])
    v(tt(T.cc[:, 0:11], T.cc[:, 16:27], T.lmc[:, 0:11], A.add), [("cc", 16, 32), "lmc"], [("cc", 0, 16)])
    s([act(T.seven[:], T.idb[:], AF.Copy, 0.0, 7.0), act(T.m1k[:], T.idb[:], AF.Copy, 0.0, -1024.0), act(T.nid[:], T.idb[:], AF.Copy, 0.0, -1.0), act(T.idF[:], T.idb[:])],
      ["idb"], ["seven", "m1k", "nid", "idF"])
    s([act(MP, MB, AF.Copy, 1.0, -1.0), act(BP, MB, AF.Copy, 64.0, -65.0), act(ZC, P4, AF.Copy, 15.0, 16.0), act(WL, lm(12), AF.Identity, lm(11), 32.0), act(WD, lm(12), AF.Identity, lm(13), 24.0),
       act(T.amb[:], T.idb[:], AF.Copy, 0.0, MB)], ["idb", ("col", 1, 2), "pp", "lmc"], [("col", 0, 1), ("col", 2, 4), ("col", 5, 7), "amb"])
    s(act(RB, MP, AF.Identity, WD, 64.0), [("col", 2, 3), ("col", 6, 7)], [("col", 4, 5)])
    s([act(o, T.gib[:, 0:8], AF.Copy, 0.0, c) for o, c in ((T.gib[:, 8:16], 0.5), (T.gik[:, 0:8], BIG), (T.gik[:, 8:16], BIG / 2), (T.gin[:, 0::3], -1.0), (T.gin[:, 1::3], -FAR), (T.gin[:, 2::3], -FAR))],
      [("gib", 0, 8)], [("gib", 8, 16), "gik", "gin"])

    def double(name, first, n):
        c = [T.cc[:, first + b:first + b + 1] for b in range(n)]
        return [later("V", [ts(T[name][:, 1 << b:2 << b], T[name][:, 0:1 << b], c[b], A.add)] +
                      ([ts(T[name][:, 2 << b:3 << b], T[name][:, 0:1 << b], c[b + 1], A.add), ts(T[name][:, 3 << b:4 << b], T[name][:, 0:1 << b], c[b], A.add, c[b + 1], A.add)] if b + 1 < n else []),
                      [(name, 0, 1 << b), ("cc", 0, 16)], [(name, 1 << b, min(4 << b, 1 << n))]) for b in range(0, n, 2)]

    weave(double("tab", 0, 7), double("hi16", 7, 4))
    v([tc(T.anl[:], T.anI[:]), tc(T.ofl[:], T.ofI[:])], ["anI", "ofI"], ["anl", "ofl"])
    s([act(T.tab[:, 128 * a:128 * a + 128], T.tab[:, 0:128], AF.Identity, T.hi16[:, a:a + 1]) for a in range(11, 16)], [("tab", 0, 128), "hi16"], [("tab", 1408, 2048)])
    v([ts(T.tab[:, 128 * a:128 * a + 128], T.tab[:, 0:128], T.hi16[:, a:a + 1], A.add) for a in range(1, 11)], [("tab", 0, 128), "hi16"], [("tab", 128, 1408)])

    WKB = ("pB", "pC", "pH", "pD")
    for b, bank in enumerate(WKB):
        p(mm(T[bank][:], T.seven[:], T.wkb[:, 512 * b:512 * b + 512], True, False), ["seven", "wkb"], [bank])
        p(mm(T[bank][:], T.one[0:1, 0:128], T.n256[:], False, True), ["one", "n256"], [bank])

    def sign(b):
        bank = WKB[b]
        s([act(T.sg[:, 512 * b + c:512 * b + c + 256], T[bank][:, c:c + 256], AF.Sign, 512 * b + c - 2047.5) for c in (0, 256)], [bank], [("sg", 512 * b, 512 * b + 512)])

    def weeks2(b):
        bank = WKB[b]
        p(mm(T[bank][:], T.seven[:], T.wkb[:, 512 * b:512 * b + 512], True, False), ["seven", "wkb"], [bank])
        p(mm(T[bank][:], T.one[0:1, 0:128], T.n256[:], False, False), ["one", "n256"], [bank])
        p(mm(T[bank][:], T.m1k[:], T.sg[:, 512 * b:512 * b + 512], False, True), ["m1k", ("sg", 512 * b, 512 * b + 512)], [bank])

    def weeks3(b):
        bank = WKB[b]
        s([act(T.cw[:, 1 + 512 * b + c:257 + 512 * b + c], T[bank][:, c:c + 256], AF.Copy, 512 * b + c - 1023.0) for c in (0, 256)], [bank], [("cw", 1 + 512 * b, 513 + 512 * b)])

    for h in (0, 1):
        s(act(T.g1[:, 512 * h:512 * h + 512], T.tab[:].indirect(T.anl[:, 32 * h:32 * h + 32]), AF.Identity, BP, MP), ["tab", "anl", ("col", 1, 4)], [("g1", 512 * h, 512 * h + 512)])
    v(ts(T.wb[:, GA:GA + 256], T.tab[:].indirect(T.ofl[:, 64:80]), MB, A.mult, RB, A.add), ["tab", "ofl", ("col", 1, 5)], [("wb", GA, GA + 256)])
    s(act(T.wb[:, GA + 256:GA + 768], T.tab[:].indirect(T.ofl[:, 80:112]), AF.Identity, RB, MB), ["tab", "ofl", ("col", 1, 5)], [("wb", GA + 256, GA + 768)])
    v([ts(T.an1[:, 0:64], T.anI[:], 1024.0, A.is_ge, float(GA - W1 - 1024), A.mult), ms(T.wb[:, GA + 769:W1], 0.0), tc(T.wb[:, GA + 768:GA + 769], RB)],
      ["anI", ("col", 4, 5)], [("an1", 0, 64), ("wb", GA + 768, W1)])
    v(tt(T.an1[:, 64:128], T.an1[:, 0:64], T.anI[:], A.add), [("an1", 0, 64), "anI"], [("an1", 64, 128)])
    v(tt(T.wb[:, W1:W1 + 512], T.tab[:].indirect(T.ofl[:, 0:32]), T.g1[:, 0:512], A.max), ["tab", "ofl", ("g1", 0, 512)], [("wb", W1, W1 + 512)])
    v(ts(T.l0[:], T.an1[:, 64:128], float(W1 - GA), A.add), [("an1", 64, 128)], ["l0"])
    v(tt(T.wb[:, W1 + 512:DUMP], T.tab[:].indirect(T.ofl[:, 32:64]), T.g1[:, 512:1024], A.max), ["tab", "ofl", ("g1", 512, 1024)], [("wb", W1 + 512, DUMP)])

    BK = ("pE", "pF")

    def conv(o, bank, src, name, c0, cols, z, z0, st=True, sp=True):
        p([mm(o, T[z][:, z0 + 15 - k:z0 + 143 - k], src[:, c0 + k:c0 + 16 * cols:16], st and k == 0, sp and k == 15) for k in range(16)], [(name, c0, c0 + 16 * cols), (z, z0, z0 + 144)], [bank])

    def pointers(a, l, src, name, c0):
        conv(T.pG[:, 0:64], "pG", src, name, c0, 64, "zp", 144 * (3 * a + l))

    def pointers2(a, l):
        lo, hi, f = WIN[a][l]
        v(ts(T["l%d" % l][:], T.pG[:, 0:64], float(f - lo - 64 * (33 + GH[a] - f)), A.add), ["pG"], ["l%d" % l])

    def own(a, l):
        f = WIN[a][l][2]
        for h in (0, 1):
            p(mm(T[BK[h]][:], T.amb[:], T.wb[:, f + 512 * h:f + 512 * h + 512], True, False), ["amb", ("wb", f + 512 * h, f + 512 * h + 512)], [BK[h]])
        if l == 2:
            conv(T.pG[:, 0:64], "pG", T.wb, "wb", f, 64, "zd", 0, True, False)

    def jump(a, l, h, q="S"):
        lo, hi, f = WIN[a][l]
        gn, c = "g%d" % (l % 2), 512 * h
        op(q, (act if q == "S" else tc)(T[gn][:, c:c + 512], T.wb[:, lo:hi].indirect(T["l%d" % l][:, 32 * h:32 * h + 32])), [("wb", lo, hi), "l%d" % l], [(gn, c, c + 512)])

    def join(l, h):
        gn, c = "g%d" % (l % 2), 512 * h
        p(mm(T[BK[h]][:], T["amb" if l == 2 else "idb"][:], T[gn][:, c:c + 512], False, True), ["amb", "idb", (gn, c, c + 512)], [BK[h]])

    def after(a, l):
        if l < 2:
            pointers(a, l + 1, T["g%d" % (l % 2)], "g%d" % (l % 2), 0)
        else:
            conv(T.pG[:, 0:64], "pG", T.g0, "g0", 0, 64, "zd", 0, False, True)

    def sums(a, l, h, q="S"):
        c = 512 * h
        if l < 2:
            f = WIN[a][l + 1][2] + c
            op(q, (act if q == "S" else tc)(T.wb[:, f:f + 512], T[BK[h]][:]), [BK[h]], [("wb", f, f + 512)])
        else:
            o = T.t8[:, 1 + c:513 + c]
            op(q, act(o, T[BK[h]][:], AF.Identity, RB) if q == "S" else ts(o, T[BK[h]][:], RB, A.add), [BK[h], ("col", 4, 5)], [("t8", 1 + c, 513 + c)])

    def datelist():
        return [later("V", tc(T.ldI[:, 0:64], T.pG[:, 0:64]), ["pG"], [("ldI", 0, 64)]),
                later("V", ts(T.ldI[:, 64:128], T.ldI[:, 0:64], 2047, A.bitwise_and), [("ldI", 0, 64)], [("ldI", 64, 128)]),
                later("V", ts(T.lfd[:], T.ldI[:, 64:128], 1.0, A.add), [("ldI", 64, 128)], ["lfd"])]

    def zed(*ids):
        v([ts(col(8 + i), lm(13), float(GH[i // 3] - WIN[i // 3][i % 3][2]), A.mult, WL, A.add) for i in ids], ["lmc", ("col", 5, 6)], [("col", 8 + i, 9 + i) for i in ids])
        return later("V", [ts(T.zp[:, 144 * i:144 * i + 144], T.n144[:], ZC, A.is_equal, col(8 + i), A.mult) for i in ids],
                     ["n144", ("col", 0, 1)] + [("col", 8 + i, 9 + i) for i in ids], [("zp", 144 * i, 144 * i + 144) for i in ids])

    TC = [T.tc[:, i:i + 1] for i in range(16)]
    WB = T.cc[:, 10:11]

    z12 = zed(1, 2)
    fills = [
        [z12, later("V", [ts(T.pw[:, 5:10], T.pw[:, 0:5], 32.0, A.mult), ms(T.pw[:, 10:11], 1024.0), ms(T.xg[:, 0::272], LOW), ts(TC[5], P4, 17.0, A.mult, P15, A.add),
                          ts(T.smi[:, 20:21], T.pI[:, 0:1], 96, A.bitwise_and)], ["pw", "pwa", "pp", "pI"], ["pw2", "xg", ("tc", 5, 6), ("smi", 20, 21)])],
        [later("V", [tt(T.cc[:, 16:27], T.pw[:, 0:11], T.lmc[:, 0:11], A.mult), tc(T.dgt[:, 0:1], TC[5]), tc(TC[10], T.smi[:, 20:21])],
               ["pw", "pwa", "pw2", "lmc", ("tc", 5, 6), ("smi", 20, 21)], [("cc", 16, 32), "dgl", ("tc", 10, 11)])],
        [later("V", [sweep(T.cc[:, 0:11], T.cc[:, 16:27], T.cc[:, 16:27], A.max, A.max), ts(T.sl[:], T.snI[:], 1.0, A.add), tc(T.ex[:], N16),
                     ts(TC[2], P15, 8.0, A.is_ge), ts(TC[3], P4, 8.0, A.mult, P15, A.add), ts(T.smi[:, 0:16], N16, 7, A.bitwise_and), ts(T.smi[:, 16:17], T.pI[:, 0:1], 7, A.bitwise_and)],
               [("cc", 16, 32), "snI", "n16", "pp", "pI"], [("cc", 0, 16), "sl", "ex", ("tc", 2, 4), "smi"])],
        [later("V", [ts(T.zd[:], T.n144[:], ZC, A.is_equal, WB, A.mult), tc(T.exg[:], T.smi[:, 0:16]), ts(T.ex8[:], G8, 2.0, A.mult, TC[2], A.add)],
               ["n144", "n16", ("col", 0, 1), ("cc", 0, 16), "smi", ("tc", 2, 4)], ["zd", "exg", "ex8"])],
        [later("V", [ts(T.dgt[:, 4:5], TC[2], 56.0, A.mult, TC[3], A.add), ts(TC[6], T.smi[:, 16:17], 1.0, A.add), ts(TC[7], T.smi[:, 16:17], 2.0, A.add, 8.0, A.mult),
                     ts(TC[8], TC[2], float(EO[8]), A.mult, -1.0, A.add), ts(T.tri[:], N16, P15, A.add, 15.5, A.is_lt), ts(T.mkg[:, 128:384], T.lane[:], P15, A.is_equal), ms(T.duw[:], 0.0),
                     ts(T.du[:], T.du[:], P15, A.add)], [("tc", 2, 4), "smi", "n16", "pp", "lane", "du"], ["dg8", ("tc", 6, 9), "tri", ("mkg", 128, 384), "duw", "du"]),
         later("V", [ts(T.dgt[:, 6:7], TC[6], TC[7], A.mult, TC[8], A.add), ts(T.duw[:, 2::3], T.du[:], float(DUMP - W1 + 1), A.add), ts(T.dec[:, 8:16], G8, P4, A.is_equal, WB, A.mult),
                     ts(TC[9], lm(13), 1024.0, A.mult, WL, A.add)], [("tc", 6, 9), "du", "duw", "n16", "pp", ("cc", 0, 16), "lmc", ("col", 5, 6)], ["pick", "duw", ("dec", 8, 16), ("tc", 9, 10)])]]

    fills[4].append(later("V", ts(T.rep[:], T.rep[:], TC[10], A.is_equal), ["rep", ("tc", 10, 11)], ["rep"]))

    def fill3():
        v(ts(T.lane[:], T.lane[:], -7.5, A.add), ["lane"], ["lane"])
        v(ms(T.c75[:], -7.5), [], ["c75"])
        z = zed(0, 3, 4, 5)
        v([tc(T.wb[:, GB + 768:GB + 769], RB), ts(DB, PC, 8.0, A.is_lt, -64.0 * 1057, A.mult), ts(T.dec[:, 0:8], G8, P4, A.is_equal, TC[9], A.mult)],
          [("col", 4, 6), "pp", "n16", ("tc", 9, 10)], [("wb", GB + 768, GB + 769), ("col", 7, 8), ("dec", 0, 8)])
        z()

    for l in range(3):
        own(0, l)
        jump(0, l, 0, "V")
        jump(0, l, 1, "S")
        for f in fills[2 * l]:
            f()
        if l > 0:
            weeks2(l - 1)
        if l == 2:
            after(0, l)
        join(l, 0)
        join(l, 1)
        if l < 2:
            sign(2 * l)
            after(0, l)
            sums(0, l, 0, "V")
            sums(0, l, 1, "S")
            for f in fills[2 * l + 1]:
                f()
            pointers2(0, l + 1)
            sign(2 * l + 1)
    weeks3(0)
    weeks3(1)
    weave(datelist())

    KB = ("pD", "pC")
    DAYS = T.sd[:, D0:D0 + 2049]
    XS, XO = 2, 1

    def keys(q):
        v(sweep(T.kx[:, 128 * q:128 * q + 128], T.segm[:], T[KB[q]][:, 0:128], A.mult, A.max), ["segm", KB[q]], [("kx", 128 * q, 128 * q + 128)])

    def bound(bank, t, start=False, stop=False):
        a = 128 * (t % 2)
        p(mm(T[bank][:, 0:128], T.one[0:1, 0:128], T.thr[:, a:a + 128], start, stop), ["one", ("thr", a, a + 128)], [bank + ("" if start or stop else "+")])

    def chosen(w):
        return ts(T.ki[:, 16:16 + w], T.kx[:, 15:16 * w:16], 4095, A.bitwise_and)

    def eqdays(h, q, bank, bs):
        o = EO[8] * h
        row = [T[bank][:, 128 * h + 128 - EW[b]:128 * h + 128] for b in range(8)]
        out = [T.eq[:, o + EO[b]:o + EO[b + 1]] for b in range(8)]
        w = [("eq", o + EO[b], o + EO[b + 1]) for b in bs]
        if q == "V":
            v([ts(out[b], row[b], T.pA[:, 24 * h + 3 * b:24 * h + 3 * b + 1], A.not_equal, FAR, A.mult) for b in bs], [bank, "pA"], w)
        else:
            s([act(out[b], row[b], AF.Abs, T.sm[:, 48 + 8 * h + b:49 + 8 * h + b], -FAR) for b in bs], [bank, ("sm", 48, 64)], w)

    def scan(h):
        a = slice(EO[8] * h, EO[8] * h + EO[8])
        v(sweep(T.scn[:, a], T.eq[:, a], T.smk[:], A.min, A.max), [("eq", a.start, a.stop), "smk"], [("scn", a.start, a.stop)])

    def dayoffsets(w):
        return [
            later("V", tt(T.sm[:, 16:32], T.scn[:].indirect(T.dgt[:, 6:7]), T.sm[:, 0:16], A.min), ["scn", "pick", ("sm", 0, 16)], [("sm", 16, 32)]),
            later("V", tc(T.u16s[:, 16:16 + w], T.sm[:, 16:16 + w]), [("sm", 16, 32)], [("u16s", 16, 32)])]

    def copies(q, src, sname, so, dst, n, ks):
        f = {"S": act, "V": tc, "G": keep}[q]
        if len(ks):
            op(q, [f(T.xr[:, dst + k:dst + 16 * n:16], src[:, so:so + n]) for k in ks], [(sname, so, so + n)], [("xr" + q, dst, dst + 16 * n)])

    def compare(c0, n, *mark):
        a = slice(16 * c0, 16 * c0 + 16 * n)
        v(tt(T.cmp[:, a], DAYS.indirect(T.cg[:, c0:c0 + n]), T.xr[:, a], A.is_lt), ["sd", ("cg", c0, c0 + n)] + [("xr" + q, a.start, a.stop) for q in "SVG"], [("cmp", a.start, a.stop)] + list(mark))
        bank = KB[c0 // 128]
        p([mm(T[bank][c0 % 128:c0 % 128 + n, k:128:16], T.cmp[:, 16 * c0 + k:16 * c0 + 16 * n:16], T.gik[:, 0:8], False, False) for k in range(16)],
          [("cmp", 16 * c0, 16 * c0 + 16 * n), "gik"], [bank + "+"])

    def signed(c0, o, b):
        def first():
            p(mm(T[b][:], T.xt[c0 % 128:c0 % 128 + 32, :], T.rep[c0 % 128:c0 % 128 + 32, :], True, False), ["xt", "rep"], [b])
            s(act(T.sgb[:, o:o + 512], DAYS.indirect(T.cg[:, c0:c0 + 32])), ["sd", ("cg", c0, c0 + 32)], [("sgb", o, o + 512)])
            p(mm(T[b][:], T.nid[:], T.sgb[:, o:o + 512], False, True), [("sgb", o, o + 512), "nid"], [b])

        def second():
            s(act(T.sgn[:, o:o + 512], T[b][:], AF.Sign, -TINY), [b], [("sgn", o, o + 512)])
            p([mm(T[KB[c0 // 128]][c0 % 128:c0 % 128 + 32, k:128:16], T.sgn[:, o + k:o + 512:16], T.gik[:, 8:16], False, False) for k in range(16)], [("sgn", o, o + 512), "gik"], [KB[c0 // 128] + "+"])
        return [first, second]

    for t in range(RO):
        last = t == RO - 1
        a1 = (t + 1) % 2
        x0, gda, gha = 272 * t, (16 * t, 16 * t + 16), (768 * t, 768 * t + 768)
        GX = "S" if last else "V"
        to, fro = (rank + 1 + t % (N - 1)) % N, (rank - 1 - t % (N - 1)) % N

        def ghosts(k, q="S"):
            d = sorted(range(1, N), key=lambda e: len(lanes(rank, (rank + e) % N)))[k]
            a, b = gha[0] + 256 * (d - 1), GH[a1] + 256 * (d - 1)
            op(q, (act if q == "S" else tc)(T.ghs[:, a:a + 256], T.t8[:, 0:1025].indirect(T.sl[:, 16 * d - 16:16 * d])), [("t8", 0, 1025), "sl"] + ["~db"] * (k == N - 2), [("ghs", a, a + 256), "~g%d" % k])
            send((rank + d) % N, T.wb[:, b:b + 256], T.ghs[:, a:a + 256], [("ghs", a, a + 256)], "gh%d" % t, True)
            if k == N - 2:
                landed(("wb", GH[a1], GH[a1] + 768), "gh%d" % t, sum(len(lanes((rank - e) % N, rank, True)) for e in range(1, N)))

        def cands(h, q="S"):
            op(q, (act if q == "S" else tc)(T.cv[:, 1 + 512 * h:513 + 512 * h], T.cw[:, 0:2049].indirect(T.lfd[:, 32 * h:32 * h + 32])), ["cw", "lfd", "~g0"], [("cv", 1 + 512 * h, 513 + 512 * h)])

        if t == 0:
            sums(0, 2, 0)
            sums(0, 2, 1)
            ghosts(0)
            for b in (2, 3):
                weeks2(b)
                weeks3(b)
        onS = ((7, 8, "pH"), (6, 7, "pC")) if t else ()
        onV = ((0, 3), (3, 6)) if t else ((0, 4), (4, 8))
        for c0, c1, b in onS:
            a, n = 128 * c0, 128 * (c1 - c0)
            p(mm(T[b][:, 0:n], T.idb[:], T.xw[:, 1 + a:1 + a + n], True, False), ["idb", ("xw", 1, 1025)], [b])
            s(act(T.sgb[:, a:a + n], DAYS.indirect(T.lfd[:, 8 * c0:8 * c1])), ["sd", "lfd"], [("sgb", a, a + n)])
            p(mm(T[b][:, 0:n], T.nid[:], T.sgb[:, a:a + n], False, True), ["nid", ("sgb", a, a + n)], [b])
        for h in (0, 1):
            c0, c1 = onV[h]
            a = slice(128 * c0, 128 * c1)
            v(tt(T.cmp[:, a], DAYS.indirect(T.lfd[:, 8 * c0:8 * c1]), T.xw[:, 1 + a.start:1 + a.stop], A.is_le), ["sd", "lfd", ("xw", 1, 1025)], [("cmp", a.start, a.stop)])
            for d0, d1, b in onS[h:h + 1]:
                s(act(T.sgn[:, 128 * d0:128 * d1], T[b][:, 0:128 * (d1 - d0)], AF.Sign, TINY), [b], [("sgn", 128 * d0, 128 * d1)])
            p([mm(T.pA[:, 8 * c:8 * c + 8], T.cmp[:, 128 * c:128 * c + 128], T.gib[:, 0:8]) for c in range(c0, c1)], [("cmp", a.start, a.stop), "gib"], ["pA"])
            for d0, d1, b in onS[h:h + 1]:
                p([f for c in range(d0, d1) for f in (mm(T.pA[:, 8 * c:8 * c + 8], T.one[0:1, 0:128], T.c8b[0:1, 0:8], True, False),
                                                      mm(T.pA[:, 8 * c:8 * c + 8], T.sgn[:, 128 * c:128 * c + 128], T.gib[:, 8:16], False, True))], [("sgn", 128 * d0, 128 * d1), "gib", "one", "c8b"], ["pA"])
        if 0 < t < RO - 1:
            ghosts(0)
        cands(0)
        if t == 0:
            v(ts(T.v1c[:, 8:16], T.v1c[:, 0:8], 0.5, A.mult), ["v1c"], ["v1h"])
        v(ts(T.bz[:, 56:120], T.pA[:, 0:64], 4.5, A.is_lt), ["pA"], [("bz", 56, 120)])
        p([mm(T.pB[:, 0:64], T.upr[:, 0:128], T.bz[:, 56:120], True, False)] + [mm(T.pB[:, 0:64], ONE, T.bz[:, 56 - 8 * q:120 - 8 * q], False, q == 7) for q in range(1, 8)],
          ["upr", "one", "bz"], ["pB"])
        if not last:
            ghosts(1, "V")
        v(tc(T.rkI[:], T.pB[:, 0:64]), ["pB"], ["rkI"])
        s([act(T.th[:, c::17], T.pB[:, 0:64], AF.Sign, 16.0 * c - 4096.5, -1.0) for c in range(1, 17)], ["pB", "th0"], ["th"])
        cands(1)
        v(ts(T.loI[:], T.rkI[:], 15, A.bitwise_and), ["rkI"], ["loI"])
        v([ts(T.lo2[:, k::2], T.loI[:], -8.0 * k, A.add) for k in (0, 1)], ["loI"], ["lo2"])
        v([ts(T.oa[:, i::8], T.lo2[:], float(i), A.is_equal) for i in range(8)], ["lo2"], ["oa"])
        for c in range(8):
            a = slice(128 * c, 128 * c + 128)
            v(ts(T.oa[:, a], T.oa[:, a], T.v1c[:, 8 + c:9 + c], A.mult), [("oa", a.start, a.stop), "v1h"], [("oa", a.start, a.stop)])
            p(mm(T.pC[:, 0:136], T.oa[:, a], T.th[:, 136 * c:136 * c + 136], c == 0, c == 7), [("oa", a.start, a.stop), "th"], ["pC"])
        v(tc(T.win[:, 0:136], T.pC[:, 0:136]), ["pC"], ["win"])
        v(tt(T.dif[:, 0:135], T.pC[:, 1:136], T.win[:, 0:135], A.subtract, 1), ["pC", "win"], ["dif"])
        v(tc(T.lv[:], T.dif[:, 0:135].indirect(T.dgt[:, 0:1])), ["dif", "dgl"], ["lv"])
        v(tc(T.lvf[:], T.dif[:, 0:135].indirect(T.dgt[:, 0:1])), ["dif", "dgl"], ["lvf"])
        for bank in KB:
            p(mm(T[bank][:, 0:128], T.one[0:1, 0:128], T.ck[:], True, False), ["one", "ck"], [bank])
        s(act(T.xg[:, x0 + 1:x0 + 257], T.xw[:, 0:1025].indirect(T.lv[:])), ["xw", "lv"], [("xg", x0 + 1, x0 + 257)])
        v(tc(T.cg[:], T.cv[:, 0:1025].indirect(T.lv[:])), ["cv", "lv"], ["cg"])
        copies("S", T.xg, "xg", x0 + 1, 0, 128, range(0, XO))
        copies("V", T.xg, "xg", x0 + 1, 0, 128, range(XO, 16))
        send(to, T.xal[:, x0:x0 + 257], T.xg[:, x0:x0 + 257], [("xg", x0, x0 + 257)], "gx%d" % t)
        ne = len(topo.engines(cores[fro], core))
        landed(("xal", x0, x0 + 272), "gx%d" % t, ne)
        copies("G", T.xg, "xg", x0 + 129, 2048, 32, range(0, 16))
        p(mm(T.pG[:, 0:128], T.xg[:, x0 + 129:x0 + 257], T.idb[:]), [("xg", x0 + 1, x0 + 257), "idb"], ["pG"])
        s(act(T.xt[:], T.pG[:, 0:128]), ["pG"], ["xt"])
        parts = [signed(160 + 32 * k, 512 * k, b) for k, b in enumerate(("pE", "pF", "pH"))]
        parts[0][0]()
        s(act(T.cgf[:], T.cv[:, 0:1025].indirect(T.lv[:])), ["cv", "lv"], ["cgf"])
        for q in (1, 0):
            p(mm(T[KB[q]][:, 0:128], T.cgf[:, 128 * q:128 * q + 128], T.idF[:], False, False), ["cgf", "idF"], [KB[q] + "+"])
        parts[1][0]()
        parts[0][1]()
        compare(0, 96)
        parts[2][0]()
        parts[1][1]()
        compare(96, 32)
        parts[2][1]()
        compare(128, 32)
        bound("pD", t, False, True)
        bound("pC", t)
        p(mm(T.pC[:, 0:128], T.up64[:], T.c8[:], False, True), ["up64", "c8"], ["pC"])

        def dates256():
            s(act(T.db[:], T.t8[:, 0:1025].indirect(T.lv[:])), [("t8", 0, 1025), "lv"], ["db", "~db"])
            p([mm(T.pE[:, 8 * q:8 + 8 * q], T.db[:, 128 * q:128 * q + 128], T.dec[:, 8:16]) for q in (0, 1)], ["db", ("dec", 8, 16)], ["pE"])
            v(tc(T.dI[:, 0:16], T.pE[:, 0:16]), ["pE"], [("dI", 0, 16)])
            v(ts(T.dI[:, 16:32], T.dI[:, 0:16], 2047, A.bitwise_and), [("dI", 0, 16)], [("dI", 16, 32)])
            v(ts(T.dI[:, 0:16], T.dI[:, 16:32], 1.0, A.add), [("dI", 16, 32)], [("dI", 0, 16)])

        beside(dates256)
        if not last:
            ghosts(2)
        if t == 0:
            beside(s, [act(T.jF[:], T.jb[:])] + [act(T.smk[:, EO[b]:EO[b] + 16], T.tri[:], AF.Copy, 0.0, FAR) for b in range(8)], ["jb", "tri", "smk0"], ["jF", "smk"])
            beside(v, ts(TC[11], P15, 16.0, A.mult), ["pp"], [("tc", 11, 12)])
            beside(s, [act(T.smk[:, 15:16], lm(0), AF.Identity, TC[11], FAR)] + [act(T.smk[:, EO[b + 1] - 1:EO[b + 1]], T.du[:, b:b + 1], AF.Copy, 0.0, 16.0) for b in range(1, 8)],
                   ["lmc", "du", ("tc", 11, 12)], ["smk"])
            beside(fill3)
        keys(0)
        keys(1)
        v(ts(T.rz[:, 8:24], T.kx[:, 15:256:16], 0.5, A.is_lt), ["kx"], [("rz", 8, 24)])
        v(chosen(16), ["kx"], [("ki", 16, 32)])
        p(mm(T.pB[:, 0:16], T.one[0:1, 0:128], T.c75[0:1, :], True, False), ["one", "c75"], ["pB"])
        p([mm(T.pB[:, 0:16], T.upr[:, 0:128], T.rz[:, 8:24], False, False), mm(T.pB[:, 0:16], ONE, T.rz[:, 0:16], False, True)], ["upr", "one", "rz"], ["pB"])
        s(act(T.xf[:], T.ki[:, 16:32].indirect(T.ex[:])), [("ki", 16, 32), "ex"], ["xf"])
        v(tt(T.xe[:], T.ki[:, 16:32].indirect(T.ex[:]), T.mkg[:, 128:384], A.mult), [("ki", 16, 32), "ex", "mkg"], ["xe"])
        v(ts(T.hl[:, 0:16], T.pB[:, 0:16], STEP16, A.add, STEP16, A.subtract), ["pB"], [("hl", 0, 16)])
        p([f for q in (0, 1) for f in (mm(T.pA[:, 24 * q:24 * q + 24], T.idb[:], T.duw[:, 24 * q:24 * q + 24], True, False),
                                       mm(T.pA[:, 24 * q:24 * q + 24], T.xe[:, 128 * q:128 * q + 128], T.gin[:], False, True))], ["xe", "gin", "idb", "duw"], ["pA"])
        p([mm(T.pH[:, 128 * q:128 * q + 128], T.xf[:, 128 * q:128 * q + 128], T.jF[:]) for q in (1, 0)], ["xf", "jF"], ["pH"])
        v(tt(T.hl[:, 16:32], T.pB[:, 0:16], T.hl[:, 0:16], A.subtract), ["pB", ("hl", 0, 16)], [("hl", 16, 32)])
        v(tt(T.ob[:], T.hl[:, 0:16].indirect(T.ex8[:]), T.ct8[:], A.is_equal), [("hl", 0, 16), "ex8", "ct8"], ["ob"])
        s([act(T.obj[:, 64 * q:64 * q + 64], T.ob[:, 64 * q:64 * q + 64], AF.Copy, 0.0, T.v1c[:, q:q + 1]) for q in (0, 1)], ["ob", "v1c"], ["obj"])
        v([ts(T.u16s[:, 32:48], T.pA[:, 0:48:3], -1.0, A.mult, -1.0, A.add), tc(T.sm[:, 48:64], T.pA[:, 1:48:3])], ["pA"], [("u16s", 32, 48), ("sm", 48, 64)])
        s(act(T.wv[:], T.tab[:].indirect(T.u16s[:, 32:48]), AF.Identity, RB, MB), ["tab", ("u16s", 32, 48), ("col", 1, 5)], ["wv"])
        eqdays(1, "S", "pH", range(8))
        beside(s, act(T.sm[:, 0:16], T.pA[:, 0:48:3], AF.Copy, float(D0), -1.0), ["pA"], [("sm", 0, 16)])
        v(tt(T.oa[:, 0:256], T.hl[:, 16:32].indirect(T.ex[:]), T.lane[:], A.is_equal), [("hl", 16, 32), "ex", "lane"], [("oa", 0, 256)])
        p([mm(T.pC[:, 0:64], T.oa[:, 128 * q:128 * q + 128], T.obj[:, 64 * q:64 * q + 64], q == 0, q == 1) for q in (0, 1)], [("oa", 0, 256), "obj"], ["pC"])
        v(tt(T.oa[:, 256:384], T.dI[:, 0:16].indirect(T.ex8[:]), T.ob[:], A.mult), [("dI", 0, 16), "ex8", "ob"], [("oa", 256, 384)])
        p([mm(T.pC[:, 64:128], T.oa[:, 128 * q:128 * q + 128], T.oa[:, 256 + 64 * q:320 + 64 * q], q == 0, q == 1) for q in (0, 1)], [("oa", 0, 384)], ["pC"])

        def parity():
            p(mm(T.pG[:, 0:16], ONE, T.rz[:, 8:24]), ["one", "rz"], ["pG"])
            s((lambda: S.activation(T.sm[:, 64:80], T.pG[:, 0:16], AF.Copy, accum_out=T.sm[:, 80:81]), lambda: 84, 0), ["pG"], [("sm", 64, 81)])
            v(tc(T.smi[:, 16:17], T.sm[:, 80:81]), [("sm", 64, 81)], [("smi", 16, 17)])
            v(ts(T.smi[:, 17:18], T.smi[:, 16:17], 1, A.bitwise_and), [("smi", 16, 17)], [("smi", 17, 18)])
            v(ts(T.sm[:, 81:82], T.smi[:, 17:18], -BIG, A.mult, -9.0 * BIG, A.add), [("smi", 17, 18)], [("sm", 81, 82)])
            s(act(T.thr[:, 128 * a1:128 * a1 + 128], T.one[0:1, 0:128], AF.Copy, 0.0, T.sm[0:1, 81:82]), ["one", ("sm", 81, 82)], [("thr", 128 * a1, 128 * a1 + 128)])

        if not last:
            beside(parity)
        v(tt(T.sm[:, 32:48], T.pA[:, 2:48:3], T.lvf[:], A.max), ["pA", "lvf"], [("sm", 32, 48)])
        v(tc(T.wg[:], T.pC[:, 0:128]), ["pC"], ["wg"])
        v(tc(T.u16s[:, 0:16], T.sm[:, 32:48]), [("sm", 32, 48)], [("u16s", 0, 16)])
        v(tc(T.gds[:, gda[0]:gda[1]], T.wg[:].indirect(T.dgt[:, 4:5])), ["wg", "dg8"], [("gds",) + gda])
        send(to, T.gdl[:, gda[0]:gda[1]], T.gds[:, gda[0]:gda[1]], [("gds",) + gda], "gd%d" % t)
        landed(("gdl",) + gda, "gd%d" % t, ne)
        eqdays(0, "S", "pH", range(8))

        def moves():
            v(scatter(T.wb[:, W1 - 1:DUMP + 256].indirect(T.u16s[:, 0:16]), T.wv[:]), ["wv", ("u16s", 0, 16), "~cmp"], [("wb", W1 - 1, DUMP + 256)])
            if last:
                for h in (0, 1):
                    p(mm(T[BK[h]][0:16, :], T.dec[:], T.wb[:, W1 + 512 * h:W1 + 512 * h + 512]), ["dec", ("wb", W1, DUMP)], [BK[h]])
                    s(act(T.yb[0:16, 512 * h:512 * h + 512], T[BK[h]][0:16, :], AF.Identity, T.col[0:16, 7:8]), [BK[h], ("col", 7, 8)], [("yb", 512 * h, 512 * h + 512)])
                copy("S", T.yan[:], T.yb[0:8, :], ["yb"], [], 0)
                copy("S", T.yof[:], T.yb[8:16, :], ["yb"], [], 0)

        if not last:
            moves()
            pointers(a1, 0, T.wb, "wb", W1)
            own(a1, 0)
        scan(1)
        scan(0)
        weave(dayoffsets(16), [] if last else [lambda: pointers2(a1, 0)])
        if not last:
            for h in (0, 1):
                jump(a1, 0, h)
                join(0, h)
            after(a1, 0)
        v(scatter(T.sd[:, 0:D0 + 2049].indirect(T.u16s[:, 24:32]), T.xg[:, x0 + 129:x0 + 257]), [("xg", x0, x0 + 257), ("u16s", 16, 32)], ["sd"])
        v(scatter(T.sd[:, 0:D0 + 2049].indirect(T.u16s[:, 16:24]), T.xg[:, x0 + 1:x0 + 129]), [("xg", x0, x0 + 257), ("u16s", 16, 32)], ["sd"])
        gl = T.gdl[:, gda[0] + 8:gda[1]]
        op(GX, (act if GX == "S" else tc)(T.gx[:], T.xal[:, x0:x0 + 257].indirect(T.gdl[:, gda[0]:gda[0] + 8])), [("xal", x0, x0 + 272), ("gdl",) + gda], ["gx"])
        v(tc(T.cg[:, 0:128], T.cw[:, 0:2049].indirect(gl)), ["cw", ("gdl",) + gda], ["cg"])

        def guestdays():
            s(act(T.cgf[:, 0:128], T.cw[:, 0:2049].indirect(gl)), ["cw", ("gdl",) + gda], ["cgf"])
            bound("pD", t, True)
            p(mm(T.pD[:, 0:128], T.cgf[:, 0:128], T.idF[:], False, False), ["cgf", "idF"], ["pD+"])

        if last:
            copies("G", T.gx, "gx", 0, 0, 64, range(0, 3))
            copies("V", T.gx, "gx", 0, 0, 64, range(3, 16))
            guestdays()
            p(mm(T.pB[:, 0:128], T.gx[:], T.idb[:]), ["gx", "idb"], ["pB"])
            s(act(T.xt[:], T.pB[:, 0:128]), ["pB"], ["xt"])
            p(mm(T.pD[64:128, 0:128], T.one[0:1, 0:64], T.c8[:], False, False), ["one", "c8"], ["pD+"])
            parts = [signed(64, 0, "pH"), signed(96, 512, "pE")]
            parts[0][0]()
            parts[1][0]()
            compare(0, 64, "~cmp")
            parts[0][1]()
            parts[1][1]()
            moves()
        else:
            copies("G", T.gx, "gx", 0, 0, 128, range(0, 2))
            copies("S", T.gx, "gx", 0, 0, 128, range(2, 2 + XS))
            copies("V", T.gx, "gx", 0, 0, 128, range(2 + XS, 16))
            sums(a1, 0, 0)
            sums(a1, 0, 1)
            guestdays()
            pointers2(a1, 1)
            own(a1, 1)
            compare(0, 64)
            jump(a1, 1, 0)
            join(1, 0)
            jump(a1, 1, 1)
            join(1, 1)
            after(a1, 1)
            compare(64, 32)
            compare(96, 32)
            sums(a1, 1, 0)
            sums(a1, 1, 1)
        p(mm(T.pD[:, 0:128], T.one[0:1, 0:128], T.ck[:], False, True), ["one", "ck"], ["pD"])
        if not last:
            pointers2(a1, 2)
        keys(0)
        if not last:
            own(a1, 2)
            jump(a1, 2, 0)
            join(2, 0)
            jump(a1, 2, 1)
        v(chosen(8), ["kx"], [("ki", 16, 32)])
        v(tt(T.xe[:], T.ki[:, 16:24].indirect(T.exg[:]), T.mkg[:, 0:256], A.mult), [("ki", 16, 32), "exg", "mkg"], ["xe"])
        p(mm(T.pA[:, 0:24], T.xe[:, 128:256], T.gin[:]), ["xe", "gin"], ["pA"])
        for b in ("pH", "pB")[:1 + last]:
            p(mm(T[b][:, 0:128], T.xe[:, 0:128], T.jb[:]), ["xe", "jb"], [b])
        if last:
            v(tc(T.sm[:, 48:56], T.pA[:, 1:24:3]), ["pA"], [("sm", 48, 64)])
            eqdays(0, "S", "pB", (6, 4, 2))
        v(ts(T.sm[:, 0:8], T.pA[:, 0:24:3], -1.0, A.mult, float(D0), A.add), ["pA"], [("sm", 0, 16)])
        if not last:
            after(a1, 2)
            join(2, 1)
            sums(a1, 2, 0)
            sums(a1, 2, 1)
        eqdays(0, "V", "pH", (7, 5, 3, 1, 0) if last else range(8))
        weave([] if last else datelist(), [lambda: scan(0)] + dayoffsets(8))
        v(scatter(T.sd[:, 0:D0 + 2049].indirect(T.u16s[:, 16:24]), T.gx[:]), ["gx", ("u16s", 16, 32)], ["sd"])
    copy("Y", T.ys[:], T.sd[:, D0 + 1:D0 + 2049], ["sd"], [])
    for i in order(steps, aside):
        steps[i][1]()
    finish([("ls", sent[0])])
